import numpy as np
import ml_dtypes


def mxq(x, axis, fmt="e4m3"):
    dtype, down = {"e4m3": (ml_dtypes.float8_e4m3fn, 7), "e5m2": (ml_dtypes.float8_e5m2, 14)}[fmt]
    v = np.moveaxis(np.asarray(x, np.float32).astype(ml_dtypes.bfloat16).astype(np.float64), axis, -1)
    blocks = v.reshape(v.shape[:-1] + (-1, 32))
    amax = np.abs(blocks).max(-1, keepdims=True)
    byte = np.maximum(np.where(amax > 0, np.frexp(amax)[1] - 1 + 127, 0) - down, 1)
    scale = np.exp2(byte - 127.0)
    codes = (blocks / scale).astype(np.float32).astype(dtype).astype(np.float64)
    return np.moveaxis((codes * scale).reshape(v.shape), -1, axis)


WIDE = False


def mx_kscale(k):
    if not WIDE:
        return np.ones(k)
    levels = np.array([10, -10, 5, -5, 0])
    if k % 512:
        return np.exp2(np.random.permutation(np.resize(levels, k // 32))).repeat(32)
    a = np.empty((k // 512, 16))
    for p in range(k // 512):
        a[p, :8] = np.random.permutation(np.resize(levels, 8))
        for g in range(8):
            far = levels[np.abs(levels - a[p, g]) >= 10]
            a[p, g + 8] = far[np.random.randint(len(far))]
    return np.exp2(a.ravel()).repeat(32)


def f64(x):
    return np.asarray(x).astype(np.float64)


def striped8(idx):
    return np.concatenate([x.reshape(-1, 16).T for x in idx]).astype(np.uint16)


def runs(offs, k):
    lists = np.stack([offs[16 * r : 16 * r + 16].T.reshape(-1) for r in range(8)]).astype(np.int64)
    return lists[np.arange(k) % 512 // 64]


def pack_weight(w):
    k, n = w.shape
    w = f64(np.asarray(w, np.float32).astype(ml_dtypes.bfloat16)).reshape(k // 32, 32, n)
    amax = np.abs(w).max(1)
    byte = np.clip(np.where(amax > 0, np.frexp(amax)[1] - 1 + 127 - 7, 1), 1, 254)
    scaled = (w * np.exp2(127.0 - byte)[:, None, :]).reshape(k, n).astype(np.float32)
    words = np.ascontiguousarray(scaled.reshape(k // 512, 128, 4, n).transpose(0, 1, 3, 2)).astype(ml_dtypes.float8_e4m3fn).view(np.uint8)
    return words, np.ascontiguousarray(byte.astype(np.uint8).reshape(k // 512, 16, n))


def unpack_weight(words, scales):
    g, p, n, _ = words.shape
    vals = np.ascontiguousarray(words).view(ml_dtypes.float8_e4m3fn).astype(np.float64) * np.repeat(np.exp2(scales.astype(np.float64) - 127.0), 8, axis=1)[..., None]
    return vals.transpose(0, 1, 3, 2).reshape(g * 512, n)


E2M1 = np.array([0.0, 0.5, 1.0, 1.5, 2.0, 3.0, 4.0, 6.0, -0.0, -0.5, -1.0, -1.5, -2.0, -3.0, -4.0, -6.0])


def pack_fp4(w):
    k, n = w.shape
    w = f64(np.asarray(w, np.float32).astype(ml_dtypes.bfloat16)).reshape(k // 32, 32, n)
    amax = np.abs(w).max(1)
    mant, ex = np.frexp(amax / 6.0)
    byte = np.clip(np.where(amax > 0, np.where(mant > 0.5, ex, ex - 1) + 127, 1), 1, 254)
    scaled = (w * np.exp2(127.0 - byte)[:, None, :]).reshape(k, n).astype(np.float32)
    c = np.ascontiguousarray(scaled.reshape(k // 512, 128, 4, n).transpose(0, 1, 3, 2)).astype(ml_dtypes.float4_e2m1fn).view(np.uint8) & 0xF
    words = (c[..., 0::2] | (c[..., 1::2] << 4)).reshape(k // 512, 128, 2 * n)
    return np.ascontiguousarray(words), np.ascontiguousarray(byte.astype(np.uint8).reshape(k // 512, 16, n))


def unpack_fp4(words, scales):
    g, _, n = scales.shape
    words = np.ascontiguousarray(words).reshape(g, 128, n, 2)
    nib = np.empty((g, 128, n, 4), np.uint8)
    nib[..., 0::2] = words & 0xF
    nib[..., 1::2] = words >> 4
    vals = E2M1[nib] * np.repeat(np.exp2(scales.astype(np.float64) - 127.0), 8, axis=1)[..., None]
    return vals.transpose(0, 1, 3, 2).reshape(g * 512, n)


def planes(y):
    n, m = y.shape
    v = y.astype(np.float32).astype(ml_dtypes.bfloat16).astype(np.float64).reshape(n // 32, 32, m)
    top = np.abs(v).max(1)
    byte = np.clip(np.where(top > 0, np.frexp(top)[1] - 1 + 127 - 7, 1), 1, 254)
    codes = (v * np.exp2(127.0 - byte)[:, None, :]).reshape(n, m).astype(np.float32).astype(ml_dtypes.float8_e4m3fn).view(np.uint8)
    words = codes.reshape(n // 512, 128, 4, m).transpose(0, 1, 3, 2)
    return np.ascontiguousarray(words), np.ascontiguousarray(byte.astype(np.uint8).reshape(n // 512, 16, m))


K, T, S, N, H = 512, 2048, 512, 512, 512


def setup_inputs():
    n = np.random.standard_normal
    s = mx_kscale(K)[:, None]
    u = mx_kscale(H)
    packed_xT = pack_weight(n((K, T)) * s)
    packed_w1 = pack_fp4(n((K, H)) / np.sqrt(K) / s)
    packed_w2 = pack_fp4(n((K, H)) / np.sqrt(K) / s)
    packed_w4 = pack_fp4(n((H, N)) / np.sqrt(H) / u[:, None])
    return {
        "x_words": packed_xT[0],
        "x_scales": packed_xT[1],
        "w1_words": packed_w1[0],
        "w1_scales": packed_w1[1],
        "w2_words": packed_w2[0],
        "w2_scales": packed_w2[1],
        "w3": (n((K, H)) / np.sqrt(K) / s * u).astype(np.float32),
        "w4_words": packed_w4[0],
        "w4_scales": packed_w4[1],
        "offs": striped8(np.stack([np.random.permutation(T)[:S] for _ in range(8)])),
        "t1": striped8(np.stack([np.random.permutation(S) for _ in range(8)])),
        "t2": striped8(np.stack([np.random.permutation(S) for _ in range(8)])),
    }


def reference(x_words, x_scales, w1_words, w1_scales, w2_words, w2_scales, w3, w4_words, w4_scales, offs, t1, t2):
    xq = unpack_weight(x_words, x_scales)[np.arange(K)[:, None], runs(offs, K)]
    y = unpack_fp4(w1_words, w1_scales).T @ xq
    e = unpack_fp4(w2_words, w2_scales).T @ xq
    val = mxq(f64(w3), 0, "e4m3").T @ xq
    h = e * (val + val[np.arange(H)[:, None], runs(t1, H)])
    z = y * (h + h[np.arange(H)[:, None], runs(t2, H)])
    out_0 = unpack_fp4(w4_words, w4_scales).T @ mxq(z, 0, "e4m3")
    return (out_0,) + planes(out_0)

@@ -1,0 +1,229 @@
+from contextlib import ExitStack
+
+import concourse.mybir as mybir
+
+K, T, S, H, N = 512, 2048, 512, 512, 512
+FLOPS = 4 * 2 * K * H * S
+
+F32 = mybir.dt.float32
+BF16 = mybir.dt.bfloat16
+I32 = mybir.dt.int32
+U32 = mybir.dt.uint32
+U16 = mybir.dt.uint16
+U8 = mybir.dt.uint8
+FP8X4 = mybir.dt.float8_e4m3fn_x4
+FP4X4 = mybir.dt.float4_e2m1fn_x4
+ADD = mybir.AluOpType.add
+MULT = mybir.AluOpType.mult
+
+P = 128
+PACK = 4
+HALF = S // 2
+CHUNK = 128
+CHUNKS = S // CHUNK
+
+
+def entries(lst, first, count):
+    return lst[:, first // 16 : (first + count) // 16]
+
+
+def tile_picked_hyena2_none_po_kernel(
+    tc, x_words, x_scales, w1_words, w1_scales, w2_words, w2_scales, w3, w4_words, w4_scales,
+    offs, t1, t2, out_0, out_1, out_2,
+):
+    nc = tc.nc
+    with ExitStack() as ctx:
+        keep = ctx.enter_context(tc.tile_pool(name="keep", bufs=1))
+        ring = ctx.enter_context(tc.tile_pool(name="ring", bufs=2))
+        psum = ctx.enter_context(tc.psum_pool(name="psum", bufs=2))
+
+        def held(shape, dtype, name):
+            return keep.tile(shape, dtype, name=name, align_bytes=64)
+
+        offs_sb = held([P, S // 16], U16, "offs_sb")
+        t1_sb = held([P, S // 16], U16, "t1_sb")
+        t2_sb = held([P, S // 16], U16, "t2_sb")
+
+        nc.sync.dma_start(offs_sb[:], offs)
+        x_scale_table = held([P, T], U8, "x_scale_table")
+        nc.vector.memset(x_scale_table[:].bitcast(I32), 0)
+        for j in range(2):
+            nc.scalar.dma_start(x_scale_table[j:P:16, :].bitcast(I32), x_scales[0, j:16:2, :].bitcast(I32))
+        w_scale_rows = held([P, 3 * H], U8, "w_scale_rows")
+        nc.gpsimd.memset(w_scale_rows[:].bitcast(I32), 0)
+        for i, scales in enumerate((w2_scales, w1_scales, w4_scales)):
+            nc.scalar.dma_start(w_scale_rows[0:16, i * H : (i + 1) * H].bitcast(I32), scales[0].bitcast(I32))
+        w3_rows = w3.rearrange("(p j) c -> p j c", j=PACK)
+        w3_raw = []
+        for u in range(2):
+            raw = held([P, PACK, H // 2], F32, "w3_raw%d" % u)
+            nc.sync.dma_start(raw[:], w3_rows[:, :, u * (H // 2) : (u + 1) * (H // 2)])
+            w3_raw.append(raw)
+        x_word_table = held([P, T], U32, "x_word_table")
+        nc.sync.dma_start(x_word_table[:].bitcast(I32), x_words[0].rearrange("p c r -> p (c r)").bitcast(I32))
+
+        def load_words(words, name):
+            raw_words = held([P, 2 * H], U8, name + "_raw_words")
+            nc.sync.dma_start(raw_words[:].bitcast(I32), words[0].bitcast(I32))
+            return raw_words
+
+        def deal_words(raw_words, name):
+            words = held([P, 2 * H], U8, name + "_words")
+            nc.vector.tensor_copy(
+                words[:].rearrange("p (t m b) -> p t m b", t=PACK, b=2),
+                raw_words[:].rearrange("p (m t b) -> p t m b", t=PACK, b=2),
+            )
+            return words
+
+        w2_raw = load_words(w2_words, "w2")
+        nc.sync.dma_start(t1_sb[:], t1)
+        w1_raw = load_words(w1_words, "w1")
+        w4_raw = load_words(w4_words, "w4")
+        nc.sync.dma_start(t2_sb[:], t2)
+
+        x_scale_picked = held([P, S], U8, "x_scale_picked")
+        nc.vector.tensor_copy(x_scale_picked[:], x_scale_table[:].indirect(offs_sb[:]))
+        xq_scales = held([P, S], U8, "xq_scales")
+        nc.vector.tensor_copy(xq_scales[:].bitcast(I32), x_scale_picked[:].bitcast(I32))
+        for j in range(2):
+            nc.scalar.dma_start(xq_scales[2 + j : P : 32, :].bitcast(I32), x_scale_picked[16 + j : P : 32, :].bitcast(I32))
+
+        w_scales = held([P, 3 * H], U8, "w_scales")
+        nc.vector.tensor_copy(
+            w_scales[:].rearrange("p (i t m) -> p i t m", i=3, t=PACK),
+            w_scale_rows[:].rearrange("p (i m t) -> p i t m", i=3, t=PACK),
+        )
+        for q in range(1, 4):
+            nc.sync.dma_start(w_scales[32 * q : 32 * q + 4, :].bitcast(I32), w_scales[4 * q : 4 * q + 4, :].bitcast(I32))
+
+        w3_bf = held([P, PACK * P * PACK], BF16, "w3_bf")
+        w3_dealt = w3_bf[:].rearrange("p (t m j) -> p m t j", t=PACK, j=PACK)
+        for u in range(2):
+            nc.scalar.copy(w3_dealt[:, u * (P // 2) : (u + 1) * (P // 2), :, :], w3_raw[u][:].rearrange("p j (m t) -> p m t j", t=PACK))
+        w3_codes = held([P, H], U32, "w3_codes")
+        w3_scales = held([P, H], U8, "w3_scales")
+        nc.vector.quantize_mx(w3_codes[:].bitcast(FP8X4), w3_scales[:], w3_bf[:])
+
+        xq_words = held([P, S], U32, "xq_words")
+        for u in range(2):
+            nc.vector.tensor_copy(
+                xq_words[:, u * HALF : (u + 1) * HALF], x_word_table[:].indirect(entries(offs_sb, u * HALF, HALF))
+            )
+
+        def fp4_product(bank, weights, t, codes, scales):
+            words, word_scales = weights
+            nc.tensor.matmul_mx(
+                bank, lhsT=words[:, 2 * P * t : 2 * P * (t + 1)].bitcast(FP4X4), lhsT_scale=word_scales[:, P * t : P * (t + 1)],
+                rhs=codes.bitcast(FP8X4), rhs_scale=scales, start=True, stop=True,
+            )
+
+        w2_q = deal_words(w2_raw, "w2"), w_scales[:, 0:H]
+
+        val_window = [held([P, S], F32, "val_window%d" % t) for t in range(PACK)]
+        val_plain = [held([P, S], F32, "val_plain%d" % t) for t in range(PACK)]
+        val_sum = [held([P, S], F32, "val_sum%d" % t) for t in range(PACK)]
+        h_window = [held([P, S], F32, "h_window%d" % t) for t in range(PACK)]
+        h_plain = [held([P, S], F32, "h_plain%d" % t) for t in range(PACK)]
+        e_banks = {}
+
+        def project(t):
+            for u in range(2):
+                cols = slice(u * HALF, (u + 1) * HALF)
+                val_bank = psum.tile([P, HALF], F32, name="val_bank")
+                nc.tensor.matmul_mx(
+                    val_bank[:], lhsT=w3_codes[:, P * t : P * (t + 1)].bitcast(FP8X4), lhsT_scale=w3_scales[:, P * t : P * (t + 1)],
+                    rhs=xq_words[:, cols].bitcast(FP8X4), rhs_scale=xq_scales[:, cols], start=True, stop=True,
+                )
+                nc.scalar.copy(val_window[t][:, cols], val_bank[:])
+                nc.scalar.copy(val_plain[t][:, cols], val_bank[:])
+            e_banks[t] = psum.tile([P, S], F32, name="e_bank")
+            fp4_product(e_banks[t][:], w2_q, t, xq_words[:], xq_scales[:])
+
+        def first_tap(t, u):
+            cols = slice(u * HALF, (u + 1) * HALF)
+            nc.vector.tensor_tensor(
+                val_sum[t][:, cols], val_window[t][:].indirect(entries(t1_sb, u * HALF, HALF)), val_plain[t][:, cols], ADD
+            )
+
+        def first_gate(t, u):
+            cols = slice(u * HALF, (u + 1) * HALF)
+            nc.vector.tensor_tensor(h_window[t][:, cols], e_banks[t][:, cols], val_sum[t][:, cols], MULT)
+            nc.scalar.copy(h_plain[t][:, cols], h_window[t][:, cols])
+
+        steps = [(t, u) for t in range(PACK) for u in range(2)]
+        project(0)
+        w1_q = deal_words(w1_raw, "w1"), w_scales[:, H : 2 * H]
+        w4_q = deal_words(w4_raw, "w4"), w_scales[:, 2 * H : 3 * H]
+        for i, (t, u) in enumerate(steps):
+            if u == 0 and t + 1 < PACK:
+                project(t + 1)
+            first_tap(t, u)
+            if i > 0:
+                first_gate(*steps[i - 1])
+        first_gate(*steps[-1])
+
+        out_codes = held([P, S], U32, "out_codes")
+        out_scales = held([P, S], U8, "out_scales")
+        out_rows = out_0.rearrange("(p t) n -> p t n", t=PACK)
+        out_words = out_1[0].rearrange("p c r -> p (c r)").bitcast(I32)
+        h_sum, z_bf, out_bf = {}, {}, {}
+
+        def second_tap(c, t):
+            if t == 0:
+                h_sum[c] = ring.tile([P, PACK, CHUNK], F32, name="h_sum", align_bytes=64)
+            nc.vector.tensor_tensor(
+                h_sum[c][:, t, :], h_window[t][:].indirect(entries(t2_sb, c * CHUNK, CHUNK)),
+                h_plain[t][:, c * CHUNK : (c + 1) * CHUNK], ADD,
+            )
+
+        def second_gate(c):
+            cols = slice(c * CHUNK, (c + 1) * CHUNK)
+            y_bank = psum.tile([P, PACK, CHUNK], F32, name="y_bank")
+            for t in range(PACK):
+                fp4_product(y_bank[:, t, :], w1_q, t, xq_words[:, cols], xq_scales[:, cols])
+            z_bf[c] = ring.tile([P, CHUNK * PACK], BF16, name="z_bf", align_bytes=64)
+            nc.vector.tensor_tensor(
+                z_bf[c][:].rearrange("p (n i t) -> p n t i", i=2, t=PACK),
+                y_bank[:].rearrange("p t (n i) -> p n t i", i=2),
+                h_sum[c][:].rearrange("p t (n i) -> p n t i", i=2),
+                MULT,
+            )
+
+        def last_layer(c):
+            cols = slice(c * CHUNK, (c + 1) * CHUNK)
+            z_codes = ring.tile([P, CHUNK], U32, name="z_codes", align_bytes=64)
+            z_scales = ring.tile([P, CHUNK], U8, name="z_scales", align_bytes=64)
+            nc.vector.quantize_mx(z_codes[:].bitcast(FP8X4), z_scales[:], z_bf[c][:])
+            out_bank = psum.tile([P, PACK, CHUNK], F32, name="out_bank")
+            for t in range(PACK):
+                fp4_product(out_bank[:, t, :], w4_q, t, z_codes[:], z_scales[:])
+            out_f32 = ring.tile([P, PACK, CHUNK], F32, name="out_f32", align_bytes=64)
+            nc.scalar.copy(out_f32[:], out_bank[:])
+            nc.sync.dma_start(out_rows[:, :, cols], out_f32[:])
+            out_bf[c] = ring.tile([P, CHUNK * PACK], BF16, name="out_bf", align_bytes=64)
+            if c + 1 < CHUNKS:
+                nc.scalar.copy(out_bf[c][:].rearrange("p (n t) -> p n t", t=PACK), out_bank[:].rearrange("p t n -> p n t"))
+            else:
+                nc.vector.tensor_copy(
+                    out_bf[c][:].rearrange("p (n i t) -> p n t i", i=4, t=PACK),
+                    out_f32[:].rearrange("p t (n i) -> p n t i", i=4),
+                )
+
+        def hand_on(c):
+            cols = slice(c * CHUNK, (c + 1) * CHUNK)
+            nc.vector.quantize_mx(out_codes[:, cols].bitcast(FP8X4), out_scales[:, cols], out_bf[c][:])
+            nc.sync.dma_start(out_words[:, cols], out_codes[:, cols].bitcast(I32))
+
+        for c in range(CHUNKS + 2):
+            for t in range(PACK):
+                if c < CHUNKS:
+                    second_tap(c, t)
+                if t == 0 and 1 <= c <= CHUNKS:
+                    second_gate(c - 1)
+                if t == 1 and 1 <= c <= CHUNKS:
+                    last_layer(c - 1)
+                if t == 2 and c >= 2:
+                    hand_on(c - 2)
+        for q in range(4):
+            queue = nc.sync if q % 2 == 0 else nc.scalar
+            queue.dma_start(out_2[0, 4 * q : 4 * q + 4, :].bitcast(I32), out_scales[32 * q : 32 * q + 4, :].bitcast(I32))

@@ -44,41 +44,50 @@ def tile_picked_hyena2_none_po_kernel(
         t1_sb = held([P, S // 16], U16, "t1_sb")
         t2_sb = held([P, S // 16], U16, "t2_sb")
 
-        nc.sync.dma_start(offs_sb[:], offs)
-        x_scale_table = held([P, T], U8, "x_scale_table")
-        nc.vector.memset(x_scale_table[:].bitcast(I32), 0)
-        for j in range(2):
-            nc.scalar.dma_start(x_scale_table[j:P:16, :].bitcast(I32), x_scales[0, j:16:2, :].bitcast(I32))
-        w_scale_rows = held([P, 3 * H], U8, "w_scale_rows")
-        nc.gpsimd.memset(w_scale_rows[:].bitcast(I32), 0)
-        for i, scales in enumerate((w2_scales, w1_scales, w4_scales)):
-            nc.scalar.dma_start(w_scale_rows[0:16, i * H : (i + 1) * H].bitcast(I32), scales[0].bitcast(I32))
-        w3_rows = w3.rearrange("(p j) c -> p j c", j=PACK)
-        w3_raw = []
-        for u in range(2):
-            raw = held([P, PACK, H // 2], F32, "w3_raw%d" % u)
-            nc.sync.dma_start(raw[:], w3_rows[:, :, u * (H // 2) : (u + 1) * (H // 2)])
-            w3_raw.append(raw)
-        x_word_table = held([P, T], U32, "x_word_table")
-        nc.sync.dma_start(x_word_table[:].bitcast(I32), x_words[0].rearrange("p c r -> p (c r)").bitcast(I32))
-
         def load_words(words, name):
             raw_words = held([P, 2 * H], U8, name + "_raw_words")
             nc.sync.dma_start(raw_words[:].bitcast(I32), words[0].bitcast(I32))
             return raw_words
 
-        def deal_words(raw_words, name):
+        w3_rows = w3.rearrange("(p j) c -> p j c", j=PACK)
+
+        def load_w3(u):
+            raw = held([P, PACK, H // 2], F32, "w3_raw%d" % u)
+            nc.sync.dma_start(raw[:], w3_rows[:, :, u * (H // 2) : (u + 1) * (H // 2)])
+            return raw
+
+        warm_in = held([P, 1], F32, "warm_in")
+        warm_out = held([P, 1], F32, "warm_out")
+        nc.gpsimd.memset(warm_in[:], 0.0)
+        nc.scalar.copy(warm_out[:], warm_in[:])
+
+        nc.sync.dma_start(offs_sb[:], offs)
+        w4_raw = load_words(w4_words, "w4")
+        w3_raw = [load_w3(0)]
+        x_scale_table = held([P, T], U8, "x_scale_table")
+        nc.vector.memset(x_scale_table[:].bitcast(I32), 0)
+        for j in range(2):
+            nc.sync.dma_start(x_scale_table[j:P:16, :].bitcast(I32), x_scales[0, j:16:2, :].bitcast(I32))
+        w_scale_rows = held([P, 3 * H], U8, "w_scale_rows")
+        nc.vector.memset(w_scale_rows[:].bitcast(I32), 0)
+        for i, scales in enumerate((w2_scales, w1_scales, w4_scales)):
+            nc.sync.dma_start(w_scale_rows[0:16, i * H : (i + 1) * H].bitcast(I32), scales[0].bitcast(I32))
+        w3_raw.append(load_w3(1))
+        x_word_table = held([P, T], U32, "x_word_table")
+        nc.sync.dma_start(x_word_table[:].bitcast(I32), x_words[0].rearrange("p c r -> p (c r)").bitcast(I32))
+
+        def deal_words(engine, raw_words, name):
             words = held([P, 2 * H], U8, name + "_words")
-            nc.vector.tensor_copy(
-                words[:].rearrange("p (t m b) -> p t m b", t=PACK, b=2),
-                raw_words[:].rearrange("p (m t b) -> p t m b", t=PACK, b=2),
+            order = "p t b m" if name == "w2" else "p t m b"
+            engine.tensor_copy(
+                words[:].rearrange("p (t m b) -> " + order, t=PACK, b=2),
+                raw_words[:].rearrange("p (m t b) -> " + order, t=PACK, b=2),
             )
             return words
 
-        w2_raw = load_words(w2_words, "w2")
         nc.sync.dma_start(t1_sb[:], t1)
+        w2_raw = load_words(w2_words, "w2")
         w1_raw = load_words(w1_words, "w1")
-        w4_raw = load_words(w4_words, "w4")
         nc.sync.dma_start(t2_sb[:], t2)
 
         x_scale_picked = held([P, S], U8, "x_scale_picked")
@@ -89,7 +98,7 @@ def tile_picked_hyena2_none_po_kernel(
             nc.scalar.dma_start(xq_scales[2 + j : P : 32, :].bitcast(I32), x_scale_picked[16 + j : P : 32, :].bitcast(I32))
 
         w_scales = held([P, 3 * H], U8, "w_scales")
-        nc.vector.tensor_copy(
+        nc.gpsimd.tensor_copy(
             w_scales[:].rearrange("p (i t m) -> p i t m", i=3, t=PACK),
             w_scale_rows[:].rearrange("p (i m t) -> p i t m", i=3, t=PACK),
         )
@@ -98,8 +107,8 @@ def tile_picked_hyena2_none_po_kernel(
 
         w3_bf = held([P, PACK * P * PACK], BF16, "w3_bf")
         w3_dealt = w3_bf[:].rearrange("p (t m j) -> p m t j", t=PACK, j=PACK)
-        for u in range(2):
-            nc.scalar.copy(w3_dealt[:, u * (P // 2) : (u + 1) * (P // 2), :, :], w3_raw[u][:].rearrange("p j (m t) -> p m t j", t=PACK))
+        for u, copy in enumerate((nc.scalar.copy, nc.vector.tensor_copy)):
+            copy(w3_dealt[:, u * (P // 2) : (u + 1) * (P // 2), :, :], w3_raw[u][:].rearrange("p j (m t) -> p m t j", t=PACK))
         w3_codes = held([P, H], U32, "w3_codes")
         w3_scales = held([P, H], U8, "w3_scales")
         nc.vector.quantize_mx(w3_codes[:].bitcast(FP8X4), w3_scales[:], w3_bf[:])
@@ -110,6 +119,9 @@ def tile_picked_hyena2_none_po_kernel(
                 xq_words[:, u * HALF : (u + 1) * HALF], x_word_table[:].indirect(entries(offs_sb, u * HALF, HALF))
             )
 
+        w4_q = deal_words(nc.vector, w4_raw, "w4"), w_scales[:, 2 * H : 3 * H]
+        w2_q = deal_words(nc.gpsimd, w2_raw, "w2"), w_scales[:, 0:H]
+
         def fp4_product(bank, weights, t, codes, scales):
             words, word_scales = weights
             nc.tensor.matmul_mx(
@@ -117,7 +129,6 @@ def tile_picked_hyena2_none_po_kernel(
                 rhs=codes.bitcast(FP8X4), rhs_scale=scales, start=True, stop=True,
             )
 
-        w2_q = deal_words(w2_raw, "w2"), w_scales[:, 0:H]
 
         val_window = [held([P, S], F32, "val_window%d" % t) for t in range(PACK)]
         val_plain = [held([P, S], F32, "val_plain%d" % t) for t in range(PACK)]
@@ -152,8 +163,7 @@ def tile_picked_hyena2_none_po_kernel(
 
         steps = [(t, u) for t in range(PACK) for u in range(2)]
         project(0)
-        w1_q = deal_words(w1_raw, "w1"), w_scales[:, H : 2 * H]
-        w4_q = deal_words(w4_raw, "w4"), w_scales[:, 2 * H : 3 * H]
+        w1_q = deal_words(nc.vector, w1_raw, "w1"), w_scales[:, H : 2 * H]
         for i, (t, u) in enumerate(steps):
             if u == 0 and t + 1 < PACK:
                 project(t + 1)

@@ -21,6 +21,7 @@ PACK = 4
 HALF = S // 2
 CHUNK = 128
 CHUNKS = S // CHUNK
+W3_PIECES = ((0, 256), (256, 384), (384, 512))
 
 
 def entries(lst, first, count):
@@ -35,7 +36,7 @@ def tile_picked_hyena2_none_po_kernel(
     with ExitStack() as ctx:
         keep = ctx.enter_context(tc.tile_pool(name="keep", bufs=1))
         ring = ctx.enter_context(tc.tile_pool(name="ring", bufs=2))
-        psum = ctx.enter_context(tc.psum_pool(name="psum", bufs=2))
+        psum = ctx.enter_context(tc.psum_pool(name="psum", bufs=1))
 
         def held(shape, dtype, name):
             return keep.tile(shape, dtype, name=name, align_bytes=64)
@@ -51,9 +52,9 @@ def tile_picked_hyena2_none_po_kernel(
 
         w3_rows = w3.rearrange("(p j) c -> p j c", j=PACK)
 
-        def load_w3(u):
-            raw = held([P, PACK, H // 2], F32, "w3_raw%d" % u)
-            nc.sync.dma_start(raw[:], w3_rows[:, :, u * (H // 2) : (u + 1) * (H // 2)])
+        def load_w3(first, last):
+            raw = held([P, PACK, last - first], F32, "w3_raw%d" % first)
+            nc.sync.dma_start(raw[:], w3_rows[:, :, first:last])
             return raw
 
         warm_in = held([P, 1], F32, "warm_in")
@@ -63,22 +64,22 @@ def tile_picked_hyena2_none_po_kernel(
 
         nc.sync.dma_start(offs_sb[:], offs)
         w4_raw = load_words(w4_words, "w4")
-        w3_raw = [load_w3(0)]
+        w2_raw = load_words(w2_words, "w2")
         x_scale_table = held([P, T], U8, "x_scale_table")
         nc.vector.memset(x_scale_table[:].bitcast(I32), 0)
         for j in range(2):
             nc.sync.dma_start(x_scale_table[j:P:16, :].bitcast(I32), x_scales[0, j:16:2, :].bitcast(I32))
+        x_word_table = held([P, T], U32, "x_word_table")
+        nc.sync.dma_start(x_word_table[:].bitcast(I32), x_words[0].rearrange("p c r -> p (c r)").bitcast(I32))
         w_scale_rows = held([P, 3 * H], U8, "w_scale_rows")
         nc.vector.memset(w_scale_rows[:].bitcast(I32), 0)
         for i, scales in enumerate((w2_scales, w1_scales, w4_scales)):
             nc.sync.dma_start(w_scale_rows[0:16, i * H : (i + 1) * H].bitcast(I32), scales[0].bitcast(I32))
-        w3_raw.append(load_w3(1))
-        x_word_table = held([P, T], U32, "x_word_table")
-        nc.sync.dma_start(x_word_table[:].bitcast(I32), x_words[0].rearrange("p c r -> p (c r)").bitcast(I32))
+        w3_raw = [load_w3(first, last) for first, last in W3_PIECES]
 
         def deal_words(engine, raw_words, name):
-            words = held([P, 2 * H], U8, name + "_words")
-            order = "p t b m" if name == "w2" else "p t m b"
+            words = held([P, 2 * H], U8, name)
+            order = "p t b m" if name == "w2_words" else "p t m b"
             engine.tensor_copy(
                 words[:].rearrange("p (t m b) -> " + order, t=PACK, b=2),
                 raw_words[:].rearrange("p (m t b) -> " + order, t=PACK, b=2),
@@ -86,7 +87,6 @@ def tile_picked_hyena2_none_po_kernel(
             return words
 
         nc.sync.dma_start(t1_sb[:], t1)
-        w2_raw = load_words(w2_words, "w2")
         w1_raw = load_words(w1_words, "w1")
         nc.sync.dma_start(t2_sb[:], t2)
 
@@ -97,6 +97,7 @@ def tile_picked_hyena2_none_po_kernel(
         for j in range(2):
             nc.scalar.dma_start(xq_scales[2 + j : P : 32, :].bitcast(I32), x_scale_picked[16 + j : P : 32, :].bitcast(I32))
 
+        w2_words_dealt = deal_words(nc.gpsimd, w2_raw, "w2_words")
         w_scales = held([P, 3 * H], U8, "w_scales")
         nc.gpsimd.tensor_copy(
             w_scales[:].rearrange("p (i t m) -> p i t m", i=3, t=PACK),
@@ -104,23 +105,23 @@ def tile_picked_hyena2_none_po_kernel(
         )
         for q in range(1, 4):
             nc.sync.dma_start(w_scales[32 * q : 32 * q + 4, :].bitcast(I32), w_scales[4 * q : 4 * q + 4, :].bitcast(I32))
+        w2_q = w2_words_dealt, w_scales[:, 0:H]
+
+        xq_words = held([P, S], U32, "xq_words")
+        nc.vector.tensor_copy(xq_words[:], x_word_table[:].indirect(offs_sb[:]))
+        w4_q = deal_words(nc.vector, w4_raw, "w4_words"), w_scales[:, 2 * H : 3 * H]
 
         w3_bf = held([P, PACK * P * PACK], BF16, "w3_bf")
         w3_dealt = w3_bf[:].rearrange("p (t m j) -> p m t j", t=PACK, j=PACK)
-        for u, copy in enumerate((nc.scalar.copy, nc.vector.tensor_copy)):
-            copy(w3_dealt[:, u * (P // 2) : (u + 1) * (P // 2), :, :], w3_raw[u][:].rearrange("p j (m t) -> p m t j", t=PACK))
+        for raw, (first, last), copy in zip(w3_raw, W3_PIECES, (nc.scalar.copy, nc.vector.tensor_copy, nc.vector.tensor_copy)):
+            copy(w3_dealt[:, first // PACK : last // PACK, :, :], raw[:].rearrange("p j (m t) -> p m t j", t=PACK))
         w3_codes = held([P, H], U32, "w3_codes")
         w3_scales = held([P, H], U8, "w3_scales")
-        nc.vector.quantize_mx(w3_codes[:].bitcast(FP8X4), w3_scales[:], w3_bf[:])
-
-        xq_words = held([P, S], U32, "xq_words")
-        for u in range(2):
-            nc.vector.tensor_copy(
-                xq_words[:, u * HALF : (u + 1) * HALF], x_word_table[:].indirect(entries(offs_sb, u * HALF, HALF))
+        for t in range(PACK):
+            nc.vector.quantize_mx(
+                w3_codes[:, P * t : P * (t + 1)].bitcast(FP8X4), w3_scales[:, P * t : P * (t + 1)],
+                w3_bf[:, P * PACK * t : P * PACK * (t + 1)],
             )
-
-        w4_q = deal_words(nc.vector, w4_raw, "w4"), w_scales[:, 2 * H : 3 * H]
-        w2_q = deal_words(nc.gpsimd, w2_raw, "w2"), w_scales[:, 0:H]
 
         def fp4_product(bank, weights, t, codes, scales):
             words, word_scales = weights
@@ -140,14 +141,14 @@ def tile_picked_hyena2_none_po_kernel(
         def project(t):
             for u in range(2):
                 cols = slice(u * HALF, (u + 1) * HALF)
-                val_bank = psum.tile([P, HALF], F32, name="val_bank")
+                val_bank = psum.tile([P, HALF], F32, name="bank%d" % (2 * t + u))
                 nc.tensor.matmul_mx(
                     val_bank[:], lhsT=w3_codes[:, P * t : P * (t + 1)].bitcast(FP8X4), lhsT_scale=w3_scales[:, P * t : P * (t + 1)],
                     rhs=xq_words[:, cols].bitcast(FP8X4), rhs_scale=xq_scales[:, cols], start=True, stop=True,
                 )
                 nc.scalar.copy(val_window[t][:, cols], val_bank[:])
                 nc.scalar.copy(val_plain[t][:, cols], val_bank[:])
-            e_banks[t] = psum.tile([P, S], F32, name="e_bank")
+            e_banks[t] = psum.tile([P, S], F32, name="bank%d" % (2 * t))
             fp4_product(e_banks[t][:], w2_q, t, xq_words[:], xq_scales[:])
 
         def first_tap(t, u):
@@ -163,7 +164,7 @@ def tile_picked_hyena2_none_po_kernel(
 
         steps = [(t, u) for t in range(PACK) for u in range(2)]
         project(0)
-        w1_q = deal_words(nc.vector, w1_raw, "w1"), w_scales[:, H : 2 * H]
+        w1_q = deal_words(nc.vector, w1_raw, "w3_bf"), w_scales[:, H : 2 * H]
         for i, (t, u) in enumerate(steps):
             if u == 0 and t + 1 < PACK:
                 project(t + 1)
@@ -188,10 +189,10 @@ def tile_picked_hyena2_none_po_kernel(
 
         def second_gate(c):
             cols = slice(c * CHUNK, (c + 1) * CHUNK)
-            y_bank = psum.tile([P, PACK, CHUNK], F32, name="y_bank")
+            y_bank = psum.tile([P, PACK, CHUNK], F32, name="bank%d" % (2 * c + 1))
             for t in range(PACK):
                 fp4_product(y_bank[:, t, :], w1_q, t, xq_words[:, cols], xq_scales[:, cols])
-            z_bf[c] = ring.tile([P, CHUNK * PACK], BF16, name="z_bf", align_bytes=64)
+            z_bf[c] = held([P, CHUNK * PACK], BF16, "z_bf%d" % c)
             nc.vector.tensor_tensor(
                 z_bf[c][:].rearrange("p (n i t) -> p n t i", i=2, t=PACK),
                 y_bank[:].rearrange("p t (n i) -> p n t i", i=2),
@@ -201,17 +202,25 @@ def tile_picked_hyena2_none_po_kernel(
 
         def last_layer(c):
             cols = slice(c * CHUNK, (c + 1) * CHUNK)
-            z_codes = ring.tile([P, CHUNK], U32, name="z_codes", align_bytes=64)
-            z_scales = ring.tile([P, CHUNK], U8, name="z_scales", align_bytes=64)
+            z_codes = held([P, CHUNK], U32, "z_codes%d" % c)
+            z_scales = held([P, CHUNK], U8, "z_scales%d" % c)
             nc.vector.quantize_mx(z_codes[:].bitcast(FP8X4), z_scales[:], z_bf[c][:])
-            out_bank = psum.tile([P, PACK, CHUNK], F32, name="out_bank")
-            for t in range(PACK):
-                fp4_product(out_bank[:, t, :], w4_q, t, z_codes[:], z_scales[:])
-            out_f32 = ring.tile([P, PACK, CHUNK], F32, name="out_f32", align_bytes=64)
-            nc.scalar.copy(out_f32[:], out_bank[:])
-            nc.sync.dma_start(out_rows[:, :, cols], out_f32[:])
-            out_bf[c] = ring.tile([P, CHUNK * PACK], BF16, name="out_bf", align_bytes=64)
+            out_f32 = held([P, PACK, CHUNK], F32, "out_f32%d" % c)
+            out_bf[c] = held([P, CHUNK * PACK], BF16, "out_bf%d" % c)
             if c + 1 < CHUNKS:
+                out_bank = psum.tile([P, PACK, CHUNK], F32, name="bank%d" % (2 * c))
+                for t in range(PACK):
+                    fp4_product(out_bank[:, t, :], w4_q, t, z_codes[:], z_scales[:])
+                nc.scalar.copy(out_f32[:], out_bank[:])
+                nc.sync.dma_start(out_rows[:, :, cols], out_f32[:])
+            else:
+                for pair in range(2):
+                    pair_bank = psum.tile([P, 2, CHUNK], F32, name="bank%d" % (2 * c if pair == 0 else 1))
+                    for t in range(2):
+                        fp4_product(pair_bank[:, t, :], w4_q, 2 * pair + t, z_codes[:], z_scales[:])
+                    nc.scalar.copy(out_f32[:, 2 * pair : 2 * pair + 2, :], pair_bank[:])
+                nc.sync.dma_start(out_rows[:, :, cols], out_f32[:])
+            if c + 2 < CHUNKS:
                 nc.scalar.copy(out_bf[c][:].rearrange("p (n t) -> p n t", t=PACK), out_bank[:].rearrange("p t n -> p n t"))
             else:
                 nc.vector.tensor_copy(

@@ -21,7 +21,7 @@ PACK = 4
 HALF = S // 2
 CHUNK = 128
 CHUNKS = S // CHUNK
-W3_PIECES = ((0, 256), (256, 384), (384, 512))
+SCALAR_W3_COLUMNS = 44
 
 
 def entries(lst, first, count):
@@ -35,7 +35,6 @@ def tile_picked_hyena2_none_po_kernel(
     nc = tc.nc
     with ExitStack() as ctx:
         keep = ctx.enter_context(tc.tile_pool(name="keep", bufs=1))
-        ring = ctx.enter_context(tc.tile_pool(name="ring", bufs=2))
         psum = ctx.enter_context(tc.psum_pool(name="psum", bufs=1))
 
         def held(shape, dtype, name):
@@ -50,199 +49,209 @@ def tile_picked_hyena2_none_po_kernel(
             nc.sync.dma_start(raw_words[:].bitcast(I32), words[0].bitcast(I32))
             return raw_words
 
-        w3_rows = w3.rearrange("(p j) c -> p j c", j=PACK)
-
-        def load_w3(first, last):
-            raw = held([P, PACK, last - first], F32, "w3_raw%d" % first)
-            nc.sync.dma_start(raw[:], w3_rows[:, :, first:last])
-            return raw
-
-        warm_in = held([P, 1], F32, "warm_in")
-        warm_out = held([P, 1], F32, "warm_out")
-        nc.gpsimd.memset(warm_in[:], 0.0)
-        nc.scalar.copy(warm_out[:], warm_in[:])
-
-        nc.sync.dma_start(offs_sb[:], offs)
-        w4_raw = load_words(w4_words, "w4")
-        w2_raw = load_words(w2_words, "w2")
         x_scale_table = held([P, T], U8, "x_scale_table")
         nc.vector.memset(x_scale_table[:].bitcast(I32), 0)
+        w_scale_rows = held([P, 3 * H], U8, "w_scale_rows")
+        nc.gpsimd.memset(w_scale_rows[:].bitcast(I32), 0)
+
+        nc.sync.dma_start(offs_sb[:], offs)
+        w3_raw = [held([P, PACK, H // 2], F32, "w3_raw%d" % u) for u in range(2)]
+        w3_rows = w3.rearrange("(p j) c -> p j c", j=PACK)
+        nc.sync.dma_start(w3_raw[0][:], w3_rows[:, :, : H // 2])
         for j in range(2):
             nc.sync.dma_start(x_scale_table[j:P:16, :].bitcast(I32), x_scales[0, j:16:2, :].bitcast(I32))
+        for i, scales in enumerate((w1_scales, w4_scales)):
+            nc.sync.dma_start(w_scale_rows[0:16, i * H : (i + 1) * H].bitcast(I32), scales[0].bitcast(I32))
+        nc.sync.dma_start(w3_raw[1][:], w3_rows[:, :, H // 2 :])
+        nc.sync.dma_start(w_scale_rows[0:16, 2 * H : 3 * H].bitcast(I32), w2_scales[0].bitcast(I32))
         x_word_table = held([P, T], U32, "x_word_table")
         nc.sync.dma_start(x_word_table[:].bitcast(I32), x_words[0].rearrange("p c r -> p (c r)").bitcast(I32))
-        w_scale_rows = held([P, 3 * H], U8, "w_scale_rows")
-        nc.vector.memset(w_scale_rows[:].bitcast(I32), 0)
-        for i, scales in enumerate((w2_scales, w1_scales, w4_scales)):
-            nc.sync.dma_start(w_scale_rows[0:16, i * H : (i + 1) * H].bitcast(I32), scales[0].bitcast(I32))
-        w3_raw = [load_w3(first, last) for first, last in W3_PIECES]
+        w2_raw = load_words(w2_words, "w2")
+        w1_raw = load_words(w1_words, "w1")
+        w4_raw = load_words(w4_words, "w4")
 
-        def deal_words(engine, raw_words, name):
-            words = held([P, 2 * H], U8, name)
-            order = "p t b m" if name == "w2_words" else "p t m b"
-            engine.tensor_copy(
-                words[:].rearrange("p (t m b) -> " + order, t=PACK, b=2),
-                raw_words[:].rearrange("p (m t b) -> " + order, t=PACK, b=2),
+        def deal_words(raw_words, words):
+            nc.vector.tensor_copy(
+                words.bitcast(U16).rearrange("p (t m) -> p t m", t=PACK),
+                raw_words[:].bitcast(U16).rearrange("p (m t) -> p t m", t=PACK),
             )
             return words
-
-        nc.sync.dma_start(t1_sb[:], t1)
-        w1_raw = load_words(w1_words, "w1")
-        nc.sync.dma_start(t2_sb[:], t2)
 
         x_scale_picked = held([P, S], U8, "x_scale_picked")
         nc.vector.tensor_copy(x_scale_picked[:], x_scale_table[:].indirect(offs_sb[:]))
         xq_scales = held([P, S], U8, "xq_scales")
         nc.vector.tensor_copy(xq_scales[:].bitcast(I32), x_scale_picked[:].bitcast(I32))
         for j in range(2):
-            nc.scalar.dma_start(xq_scales[2 + j : P : 32, :].bitcast(I32), x_scale_picked[16 + j : P : 32, :].bitcast(I32))
+            nc.sync.dma_start(xq_scales[2 + j : P : 32, :].bitcast(I32), x_scale_picked[16 + j : P : 32, :].bitcast(I32))
+        nc.sync.dma_start(t1_sb[:], t1)
 
-        w2_words_dealt = deal_words(nc.gpsimd, w2_raw, "w2_words")
-        w_scales = held([P, 3 * H], U8, "w_scales")
-        nc.gpsimd.tensor_copy(
-            w_scales[:].rearrange("p (i t m) -> p i t m", i=3, t=PACK),
-            w_scale_rows[:].rearrange("p (i m t) -> p i t m", i=3, t=PACK),
-        )
-        for q in range(1, 4):
-            nc.sync.dma_start(w_scales[32 * q : 32 * q + 4, :].bitcast(I32), w_scales[4 * q : 4 * q + 4, :].bitcast(I32))
-        w2_q = w2_words_dealt, w_scales[:, 0:H]
 
-        xq_words = held([P, S], U32, "xq_words")
-        nc.vector.tensor_copy(xq_words[:], x_word_table[:].indirect(offs_sb[:]))
-        w4_q = deal_words(nc.vector, w4_raw, "w4_words"), w_scales[:, 2 * H : 3 * H]
+        def deal_scales(engine, rows, dealt):
+            engine.tensor_copy(
+                dealt.rearrange("p (i t m) -> p t i m", t=PACK, m=P), rows.rearrange("p (i m t) -> p t i m", t=PACK, m=P)
+            )
+            for q in range(1, 4):
+                nc.sync.dma_start(dealt[32 * q : 32 * q + 4, :].bitcast(I32), dealt[4 * q : 4 * q + 4, :].bitcast(I32))
+
 
         w3_bf = held([P, PACK * P * PACK], BF16, "w3_bf")
         w3_dealt = w3_bf[:].rearrange("p (t m j) -> p m t j", t=PACK, j=PACK)
-        for raw, (first, last), copy in zip(w3_raw, W3_PIECES, (nc.scalar.copy, nc.vector.tensor_copy, nc.vector.tensor_copy)):
-            copy(w3_dealt[:, first // PACK : last // PACK, :, :], raw[:].rearrange("p j (m t) -> p m t j", t=PACK))
+        w3_walk = [raw[:].rearrange("p j (m t) -> p m t j", t=PACK) for raw in w3_raw]
+        nc.scalar.copy(w3_dealt[:, : P // 2, :, :], w3_walk[0])
+        nc.scalar.copy(w3_dealt[:, P // 2 : P // 2 + SCALAR_W3_COLUMNS, :, :], w3_walk[1][:, :SCALAR_W3_COLUMNS, :, :])
+        nc.vector.tensor_copy(w3_dealt[:, P // 2 + SCALAR_W3_COLUMNS :, :, :], w3_walk[1][:, SCALAR_W3_COLUMNS:, :, :])
+        w2_scales_dealt = held([P, H], U8, "w2_scales_dealt")
+        deal_scales(nc.vector, w_scale_rows[:, 2 * H : 3 * H], w2_scales_dealt[:])
+        nc.sync.dma_start(t2_sb[:], t2)
+        late_scales = held([P, 2 * H], U8, "late_scales")
+        deal_scales(nc.gpsimd, w_scale_rows[:, 0 : 2 * H], late_scales[:])
         w3_codes = held([P, H], U32, "w3_codes")
         w3_scales = held([P, H], U8, "w3_scales")
-        for t in range(PACK):
-            nc.vector.quantize_mx(
-                w3_codes[:, P * t : P * (t + 1)].bitcast(FP8X4), w3_scales[:, P * t : P * (t + 1)],
-                w3_bf[:, P * PACK * t : P * PACK * (t + 1)],
-            )
+        nc.vector.quantize_mx(w3_codes[:].bitcast(FP8X4), w3_scales[:], w3_bf[:])
 
-        def fp4_product(bank, weights, t, codes, scales):
+
+        xq_words = held([P, S], U32, "w3_bf")
+        for u in range(2):
+            nc.vector.tensor_copy(xq_words[:, u * HALF : (u + 1) * HALF], x_word_table[:].indirect(entries(offs_sb, u * HALF, HALF)))
+        w_dealt = held([P, 6 * H], U8, "x_word_table")
+        w2_q = deal_words(w2_raw, w_dealt[:, 0 : 2 * H]), w2_scales_dealt[:]
+        w1_q = deal_words(w1_raw, w_dealt[:, 2 * H : 4 * H]), late_scales[:, 0:H]
+        w4_q = deal_words(w4_raw, w_dealt[:, 4 * H : 6 * H]), late_scales[:, H : 2 * H]
+
+        def bank(number, shape):
+            return psum.tile(shape, F32, name="bank%d" % number)
+
+        def fp4_product(result, weights, t, codes, scales):
             words, word_scales = weights
             nc.tensor.matmul_mx(
-                bank, lhsT=words[:, 2 * P * t : 2 * P * (t + 1)].bitcast(FP4X4), lhsT_scale=word_scales[:, P * t : P * (t + 1)],
+                result, lhsT=words[:, 2 * P * t : 2 * P * (t + 1)].bitcast(FP4X4), lhsT_scale=word_scales[:, P * t : P * (t + 1)],
                 rhs=codes.bitcast(FP8X4), rhs_scale=scales, start=True, stop=True,
             )
 
-
-        val_window = [held([P, S], F32, "val_window%d" % t) for t in range(PACK)]
-        val_plain = [held([P, S], F32, "val_plain%d" % t) for t in range(PACK)]
+        val_window = [held([P, 2 * S], F32, "val_window%d" % t) for t in range(PACK)]
+        val_plain = [val_window[(t + 1) % PACK][:, S:] for t in range(PACK)]
         val_sum = [held([P, S], F32, "val_sum%d" % t) for t in range(PACK)]
         h_window = [held([P, S], F32, "h_window%d" % t) for t in range(PACK)]
         h_plain = [held([P, S], F32, "h_plain%d" % t) for t in range(PACK)]
         e_banks = {}
 
-        def project(t):
-            for u in range(2):
-                cols = slice(u * HALF, (u + 1) * HALF)
-                val_bank = psum.tile([P, HALF], F32, name="bank%d" % (2 * t + u))
-                nc.tensor.matmul_mx(
-                    val_bank[:], lhsT=w3_codes[:, P * t : P * (t + 1)].bitcast(FP8X4), lhsT_scale=w3_scales[:, P * t : P * (t + 1)],
-                    rhs=xq_words[:, cols].bitcast(FP8X4), rhs_scale=xq_scales[:, cols], start=True, stop=True,
-                )
-                nc.scalar.copy(val_window[t][:, cols], val_bank[:])
-                nc.scalar.copy(val_plain[t][:, cols], val_bank[:])
-            e_banks[t] = psum.tile([P, S], F32, name="bank%d" % (2 * t))
+        def val_product(t, cols, number, copy):
+            val_bank = bank(number, [P, cols.stop - cols.start])
+            nc.tensor.matmul_mx(
+                val_bank[:], lhsT=w3_codes[:, P * t : P * (t + 1)].bitcast(FP8X4), lhsT_scale=w3_scales[:, P * t : P * (t + 1)],
+                rhs=xq_words[:, cols].bitcast(FP8X4), rhs_scale=xq_scales[:, cols], start=True, stop=True,
+            )
+            copy(val_window[t][:, cols], val_bank[:])
+            copy(val_plain[t][:, cols], val_bank[:])
+
+        def e_product(t, number):
+            e_banks[t] = bank(number, [P, S])
             fp4_product(e_banks[t][:], w2_q, t, xq_words[:], xq_scales[:])
 
-        def first_tap(t, u):
-            cols = slice(u * HALF, (u + 1) * HALF)
+        def first_tap(t, first, count):
+            cols = slice(first, first + count)
             nc.vector.tensor_tensor(
-                val_sum[t][:, cols], val_window[t][:].indirect(entries(t1_sb, u * HALF, HALF)), val_plain[t][:, cols], ADD
+                val_sum[t][:, cols], val_window[t][:].indirect(entries(t1_sb, first, count)), val_plain[t][:, cols], ADD
             )
 
-        def first_gate(t, u):
-            cols = slice(u * HALF, (u + 1) * HALF)
-            nc.vector.tensor_tensor(h_window[t][:, cols], e_banks[t][:, cols], val_sum[t][:, cols], MULT)
-            nc.scalar.copy(h_plain[t][:, cols], h_window[t][:, cols])
+        def first_gate(t):
+            nc.vector.tensor_tensor(h_window[t][:], e_banks[t][:], val_sum[t][:], MULT)
 
-        steps = [(t, u) for t in range(PACK) for u in range(2)]
-        project(0)
-        w1_q = deal_words(nc.vector, w1_raw, "w3_bf"), w_scales[:, H : 2 * H]
-        for i, (t, u) in enumerate(steps):
-            if u == 0 and t + 1 < PACK:
-                project(t + 1)
-            first_tap(t, u)
-            if i > 0:
-                first_gate(*steps[i - 1])
-        first_gate(*steps[-1])
+        warm_bank = bank(7, [P, S])
+        for t in range(2):
+            nc.tensor.matmul_mx(
+                warm_bank[:], lhsT=w3_codes[:, P * t : P * (t + 1)].bitcast(FP8X4), lhsT_scale=w3_scales[:, P * t : P * (t + 1)],
+                rhs=w3_codes[:].bitcast(FP8X4), rhs_scale=w3_scales[:], start=True, stop=True,
+            )
+
+        val_product(0, slice(0, HALF), 0, nc.scalar.copy)
+        val_product(0, slice(HALF, S), 1, nc.scalar.copy)
+        first_tap(0, 0, HALF)
+        first_tap(0, HALF, HALF)
+        for t in range(1, PACK):
+            val_product(t, slice(0, S), t + 1, nc.scalar.copy)
+            e_product(t - 1, t + 1)
+            first_tap(t, 0, S)
+            first_gate(t - 1)
+        e_product(PACK - 1, 0)
 
         out_codes = held([P, S], U32, "out_codes")
         out_scales = held([P, S], U8, "out_scales")
         out_rows = out_0.rearrange("(p t) n -> p t n", t=PACK)
         out_words = out_1[0].rearrange("p c r -> p (c r)").bitcast(I32)
-        h_sum, z_bf, out_bf = {}, {}, {}
+        h_sum = held([P, PACK, S], F32, "h_sum")
+        z_bf = held([P, S * PACK], BF16, "z_bf")
+        z_codes = held([P, S], U32, "z_codes")
+        z_scales = held([P, S], U8, "z_scales")
+        out_f32 = [held([P, PACK, CHUNK], F32, "out_f32%d" % c) for c in range(CHUNKS)]
+        out_bf = held([P, S * PACK], BF16, "out_bf")
 
-        def second_tap(c, t):
-            if t == 0:
-                h_sum[c] = ring.tile([P, PACK, CHUNK], F32, name="h_sum", align_bytes=64)
+        def second_tap(t, first, count):
+            cols = slice(first, first + count)
             nc.vector.tensor_tensor(
-                h_sum[c][:, t, :], h_window[t][:].indirect(entries(t2_sb, c * CHUNK, CHUNK)),
-                h_plain[t][:, c * CHUNK : (c + 1) * CHUNK], ADD,
+                h_sum[:, t, cols], h_window[t][:].indirect(entries(t2_sb, first, count)), h_plain[t][:, cols], ADD
             )
 
         def second_gate(c):
             cols = slice(c * CHUNK, (c + 1) * CHUNK)
-            y_bank = psum.tile([P, PACK, CHUNK], F32, name="bank%d" % (2 * c + 1))
+            y_bank = bank(min(c + 1, 3), [P, PACK, CHUNK])
             for t in range(PACK):
                 fp4_product(y_bank[:, t, :], w1_q, t, xq_words[:, cols], xq_scales[:, cols])
-            z_bf[c] = held([P, CHUNK * PACK], BF16, "z_bf%d" % c)
             nc.vector.tensor_tensor(
-                z_bf[c][:].rearrange("p (n i t) -> p n t i", i=2, t=PACK),
+                z_bf[:, PACK * cols.start : PACK * cols.stop].rearrange("p (n i t) -> p n t i", i=2, t=PACK),
                 y_bank[:].rearrange("p t (n i) -> p n t i", i=2),
-                h_sum[c][:].rearrange("p t (n i) -> p n t i", i=2),
+                h_sum[:, :, cols].rearrange("p t (n i) -> p n t i", i=2),
                 MULT,
             )
 
+        def quantise_z(first, count):
+            cols = slice(first, first + count)
+            nc.vector.quantize_mx(z_codes[:, cols].bitcast(FP8X4), z_scales[:, cols], z_bf[:, PACK * first : PACK * (first + count)])
+
         def last_layer(c):
             cols = slice(c * CHUNK, (c + 1) * CHUNK)
-            z_codes = held([P, CHUNK], U32, "z_codes%d" % c)
-            z_scales = held([P, CHUNK], U8, "z_scales%d" % c)
-            nc.vector.quantize_mx(z_codes[:].bitcast(FP8X4), z_scales[:], z_bf[c][:])
-            out_f32 = held([P, PACK, CHUNK], F32, "out_f32%d" % c)
-            out_bf[c] = held([P, CHUNK * PACK], BF16, "out_bf%d" % c)
+            rounded = out_bf[:, PACK * cols.start : PACK * cols.stop]
             if c + 1 < CHUNKS:
-                out_bank = psum.tile([P, PACK, CHUNK], F32, name="bank%d" % (2 * c))
+                out_bank = bank(c + 5, [P, PACK, CHUNK])
                 for t in range(PACK):
-                    fp4_product(out_bank[:, t, :], w4_q, t, z_codes[:], z_scales[:])
-                nc.scalar.copy(out_f32[:], out_bank[:])
-                nc.sync.dma_start(out_rows[:, :, cols], out_f32[:])
+                    fp4_product(out_bank[:, t, :], w4_q, t, z_codes[:, cols], z_scales[:, cols])
+                nc.scalar.copy(out_f32[c][:], out_bank[:])
+                nc.sync.dma_start(out_rows[:, :, cols], out_f32[c][:])
+                nc.scalar.copy(rounded.rearrange("p (n t) -> p n t", t=PACK), out_bank[:].rearrange("p t n -> p n t"))
             else:
-                for pair in range(2):
-                    pair_bank = psum.tile([P, 2, CHUNK], F32, name="bank%d" % (2 * c if pair == 0 else 1))
+                for pair, copy in enumerate((nc.scalar.copy, nc.vector.tensor_copy)):
+                    pair_bank = bank(pair, [P, 2, CHUNK])
                     for t in range(2):
-                        fp4_product(pair_bank[:, t, :], w4_q, 2 * pair + t, z_codes[:], z_scales[:])
-                    nc.scalar.copy(out_f32[:, 2 * pair : 2 * pair + 2, :], pair_bank[:])
-                nc.sync.dma_start(out_rows[:, :, cols], out_f32[:])
-            if c + 2 < CHUNKS:
-                nc.scalar.copy(out_bf[c][:].rearrange("p (n t) -> p n t", t=PACK), out_bank[:].rearrange("p t n -> p n t"))
-            else:
+                        fp4_product(pair_bank[:, t, :], w4_q, 2 * pair + t, z_codes[:, cols], z_scales[:, cols])
+                    copy(out_f32[c][:, 2 * pair : 2 * pair + 2, :], pair_bank[:])
+                nc.sync.dma_start(out_rows[:, :, cols], out_f32[c][:])
                 nc.vector.tensor_copy(
-                    out_bf[c][:].rearrange("p (n i t) -> p n t i", i=4, t=PACK),
-                    out_f32[:].rearrange("p t (n i) -> p n t i", i=4),
+                    rounded.rearrange("p (n i t) -> p n t i", i=4, t=PACK),
+                    out_f32[c][:].rearrange("p t (n i) -> p n t i", i=4),
                 )
 
-        def hand_on(c):
-            cols = slice(c * CHUNK, (c + 1) * CHUNK)
-            nc.vector.quantize_mx(out_codes[:, cols].bitcast(FP8X4), out_scales[:, cols], out_bf[c][:])
+        def hand_on(first, count):
+            cols = slice(first, first + count)
+            nc.vector.quantize_mx(out_codes[:, cols].bitcast(FP8X4), out_scales[:, cols], out_bf[:, PACK * first : PACK * (first + count)])
             nc.sync.dma_start(out_words[:, cols], out_codes[:, cols].bitcast(I32))
 
-        for c in range(CHUNKS + 2):
+        for c in range(CHUNKS):
             for t in range(PACK):
-                if c < CHUNKS:
-                    second_tap(c, t)
-                if t == 0 and 1 <= c <= CHUNKS:
+                if c == 0:
+                    if t == 1:
+                        first_gate(PACK - 1)
+                    nc.scalar.copy(h_plain[t][:], h_window[t][:])
+                second_tap(t, c * CHUNK, CHUNK)
+                if t == 0 and c > 0:
                     second_gate(c - 1)
-                if t == 1 and 1 <= c <= CHUNKS:
+                if t == 1 and c > 0:
+                    quantise_z((c - 1) * CHUNK, CHUNK)
                     last_layer(c - 1)
-                if t == 2 and c >= 2:
-                    hand_on(c - 2)
+        second_gate(CHUNKS - 1)
+        quantise_z((CHUNKS - 1) * CHUNK, CHUNK)
+        hand_on(0, HALF)
+        last_layer(CHUNKS - 1)
+        hand_on(HALF, HALF)
         for q in range(4):
-            queue = nc.sync if q % 2 == 0 else nc.scalar
+            queue = nc.sync if q < 2 else nc.scalar
             queue.dma_start(out_2[0, 4 * q : 4 * q + 4, :].bitcast(I32), out_scales[32 * q : 32 * q + 4, :].bitcast(I32))

@@ -135,43 +135,39 @@ def tile_picked_hyena2_none_po_kernel(
         h_plain = [held([P, S], F32, "h_plain%d" % t) for t in range(PACK)]
         e_banks = {}
 
-        def val_product(t, cols, number, copy):
+        def val_product(t, cols, number):
             val_bank = bank(number, [P, cols.stop - cols.start])
             nc.tensor.matmul_mx(
                 val_bank[:], lhsT=w3_codes[:, P * t : P * (t + 1)].bitcast(FP8X4), lhsT_scale=w3_scales[:, P * t : P * (t + 1)],
                 rhs=xq_words[:, cols].bitcast(FP8X4), rhs_scale=xq_scales[:, cols], start=True, stop=True,
             )
-            copy(val_window[t][:, cols], val_bank[:])
-            copy(val_plain[t][:, cols], val_bank[:])
+            nc.scalar.copy(val_window[t][:, cols], val_bank[:])
+            width = HALF if t < 2 else S
+            for first in range(cols.start, cols.stop, width):
+                nc.scalar.copy(val_plain[t][:, first : first + width], val_bank[:, first - cols.start : first - cols.start + width])
 
         def e_product(t, number):
             e_banks[t] = bank(number, [P, S])
             fp4_product(e_banks[t][:], w2_q, t, xq_words[:], xq_scales[:])
 
-        def first_tap(t, first, count):
-            cols = slice(first, first + count)
-            nc.vector.tensor_tensor(
-                val_sum[t][:, cols], val_window[t][:].indirect(entries(t1_sb, first, count)), val_plain[t][:, cols], ADD
-            )
+        def first_tap(t):
+            width = HALF if t < 2 else S
+            for first in range(0, S, width):
+                cols = slice(first, first + width)
+                nc.vector.tensor_tensor(
+                    val_sum[t][:, cols], val_window[t][:].indirect(entries(t1_sb, first, width)), val_plain[t][:, cols], ADD
+                )
 
         def first_gate(t):
             nc.vector.tensor_tensor(h_window[t][:], e_banks[t][:], val_sum[t][:], MULT)
 
-        warm_bank = bank(7, [P, S])
-        for t in range(2):
-            nc.tensor.matmul_mx(
-                warm_bank[:], lhsT=w3_codes[:, P * t : P * (t + 1)].bitcast(FP8X4), lhsT_scale=w3_scales[:, P * t : P * (t + 1)],
-                rhs=w3_codes[:].bitcast(FP8X4), rhs_scale=w3_scales[:], start=True, stop=True,
-            )
-
-        val_product(0, slice(0, HALF), 0, nc.scalar.copy)
-        val_product(0, slice(HALF, S), 1, nc.scalar.copy)
-        first_tap(0, 0, HALF)
-        first_tap(0, HALF, HALF)
+        val_product(0, slice(0, HALF), 0)
+        val_product(0, slice(HALF, S), 1)
+        first_tap(0)
         for t in range(1, PACK):
-            val_product(t, slice(0, S), t + 1, nc.scalar.copy)
+            val_product(t, slice(0, S), t + 1)
             e_product(t - 1, t + 1)
-            first_tap(t, 0, S)
+            first_tap(t)
             first_gate(t - 1)
         e_product(PACK - 1, 0)
 
@@ -197,12 +193,14 @@ def tile_picked_hyena2_none_po_kernel(
             y_bank = bank(min(c + 1, 3), [P, PACK, CHUNK])
             for t in range(PACK):
                 fp4_product(y_bank[:, t, :], w1_q, t, xq_words[:, cols], xq_scales[:, cols])
-            nc.vector.tensor_tensor(
-                z_bf[:, PACK * cols.start : PACK * cols.stop].rearrange("p (n i t) -> p n t i", i=2, t=PACK),
-                y_bank[:].rearrange("p t (n i) -> p n t i", i=2),
-                h_sum[:, :, cols].rearrange("p t (n i) -> p n t i", i=2),
-                MULT,
-            )
+            width = CHUNK // 2 if c + 1 == CHUNKS else CHUNK
+            for first in range(cols.start, cols.stop, width):
+                nc.vector.tensor_tensor(
+                    z_bf[:, PACK * first : PACK * (first + width)].rearrange("p (n i t) -> p n t i", i=2, t=PACK),
+                    y_bank[:, :, first - cols.start : first - cols.start + width].rearrange("p t (n i) -> p n t i", i=2),
+                    h_sum[:, :, first : first + width].rearrange("p t (n i) -> p n t i", i=2),
+                    MULT,
+                )
 
         def quantise_z(first, count):
             cols = slice(first, first + count)
@@ -223,16 +221,23 @@ def tile_picked_hyena2_none_po_kernel(
                     pair_bank = bank(pair, [P, 2, CHUNK])
                     for t in range(2):
                         fp4_product(pair_bank[:, t, :], w4_q, 2 * pair + t, z_codes[:, cols], z_scales[:, cols])
-                    copy(out_f32[c][:, 2 * pair : 2 * pair + 2, :], pair_bank[:])
+                    for first in range(0, CHUNK, CHUNK // 2):
+                        half = slice(first, first + CHUNK // 2)
+                        copy(out_f32[c][:, 2 * pair : 2 * pair + 2, half], pair_bank[:, :, half])
                 nc.sync.dma_start(out_rows[:, :, cols], out_f32[c][:])
-                nc.vector.tensor_copy(
-                    rounded.rearrange("p (n i t) -> p n t i", i=4, t=PACK),
-                    out_f32[c][:].rearrange("p t (n i) -> p n t i", i=4),
-                )
+                quantise_out((c - 1) * CHUNK, CHUNK)
+                for first in range(0, CHUNK, CHUNK // 2):
+                    nc.vector.tensor_copy(
+                        rounded[:, PACK * first : PACK * (first + CHUNK // 2)].rearrange("p (n i t) -> p n t i", i=4, t=PACK),
+                        out_f32[c][:, :, first : first + CHUNK // 2].rearrange("p t (n i) -> p n t i", i=4),
+                    )
 
-        def hand_on(first, count):
+        def quantise_out(first, count):
             cols = slice(first, first + count)
             nc.vector.quantize_mx(out_codes[:, cols].bitcast(FP8X4), out_scales[:, cols], out_bf[:, PACK * first : PACK * (first + count)])
+
+        def store_codes(first, count):
+            cols = slice(first, first + count)
             nc.sync.dma_start(out_words[:, cols], out_codes[:, cols].bitcast(I32))
 
         for c in range(CHUNKS):
@@ -248,10 +253,14 @@ def tile_picked_hyena2_none_po_kernel(
                     quantise_z((c - 1) * CHUNK, CHUNK)
                     last_layer(c - 1)
         second_gate(CHUNKS - 1)
-        quantise_z((CHUNKS - 1) * CHUNK, CHUNK)
-        hand_on(0, HALF)
+        quantise_z(S - CHUNK, CHUNK // 2)
+        quantise_z(S - CHUNK // 2, CHUNK // 2)
+        quantise_out(0, HALF)
+        store_codes(0, HALF)
         last_layer(CHUNKS - 1)
-        hand_on(HALF, HALF)
+        quantise_out(S - CHUNK, CHUNK // 2)
+        quantise_out(S - CHUNK // 2, CHUNK // 2)
+        store_codes(HALF, HALF)
         for q in range(4):
             queue = nc.sync if q < 2 else nc.scalar
             queue.dma_start(out_2[0, 4 * q : 4 * q + 4, :].bitcast(I32), out_scales[32 * q : 32 * q + 4, :].bitcast(I32))

@@ -15,6 +15,7 @@ FP8X4 = mybir.dt.float8_e4m3fn_x4
 FP4X4 = mybir.dt.float4_e2m1fn_x4
 ADD = mybir.AluOpType.add
 MULT = mybir.AluOpType.mult
+COPY = mybir.ActivationFunctionType.Copy
 
 P = 128
 PACK = 4
@@ -22,6 +23,9 @@ HALF = S // 2
 CHUNK = 128
 CHUNKS = S // CHUNK
 SCALAR_W3_COLUMNS = 44
+VECTOR_TILE = 3
+EARLY_TILES = (0, 3)
+LATE_TILES = (1, 2)
 
 
 def entries(lst, first, count):
@@ -128,11 +132,11 @@ def tile_picked_hyena2_none_po_kernel(
                 rhs=codes.bitcast(FP8X4), rhs_scale=scales, start=True, stop=True,
             )
 
-        val_window = [held([P, 2 * S], F32, "val_window%d" % t) for t in range(PACK)]
-        val_plain = [val_window[(t + 1) % PACK][:, S:] for t in range(PACK)]
-        val_sum = [held([P, S], F32, "val_sum%d" % t) for t in range(PACK)]
+        val_window = [held([P, S], F32, "val_window%d" % t) for t in range(PACK)]
+        val_tap = [held([P, S], F32, "taps%d" % t) for t in range(PACK)]
         h_window = [held([P, S], F32, "h_window%d" % t) for t in range(PACK)]
-        h_plain = [held([P, S], F32, "h_plain%d" % t) for t in range(PACK)]
+        halves = [slice(0, HALF), slice(HALF, S)]
+        val_banks = {}
         e_banks = {}
 
         def val_product(t, cols, number):
@@ -141,56 +145,69 @@ def tile_picked_hyena2_none_po_kernel(
                 val_bank[:], lhsT=w3_codes[:, P * t : P * (t + 1)].bitcast(FP8X4), lhsT_scale=w3_scales[:, P * t : P * (t + 1)],
                 rhs=xq_words[:, cols].bitcast(FP8X4), rhs_scale=xq_scales[:, cols], start=True, stop=True,
             )
-            nc.scalar.copy(val_window[t][:, cols], val_bank[:])
-            width = HALF if t < 2 else S
-            for first in range(cols.start, cols.stop, width):
-                nc.scalar.copy(val_plain[t][:, first : first + width], val_bank[:, first - cols.start : first - cols.start + width])
+            for half in halves:
+                if cols.start <= half.start and half.stop <= cols.stop:
+                    val_banks[t, half.start] = val_bank[:, half.start - cols.start : half.stop - cols.start]
+            copy = nc.scalar.copy if t == 0 else nc.vector.tensor_copy
+            copy(val_window[t][:, cols], val_bank[:])
 
         def e_product(t, number):
             e_banks[t] = bank(number, [P, S])
             fp4_product(e_banks[t][:], w2_q, t, xq_words[:], xq_scales[:])
 
-        def first_tap(t):
-            width = HALF if t < 2 else S
-            for first in range(0, S, width):
-                cols = slice(first, first + width)
-                nc.vector.tensor_tensor(
-                    val_sum[t][:, cols], val_window[t][:].indirect(entries(t1_sb, first, width)), val_plain[t][:, cols], ADD
-                )
+        def look_up(result, window, lst, cols):
+            nc.scalar.activation(result, window[:].indirect(entries(lst, cols.start, cols.stop - cols.start)), COPY)
 
-        def first_gate(t):
-            nc.vector.tensor_tensor(h_window[t][:], e_banks[t][:], val_sum[t][:], MULT)
+        def first_add(t):
+            for half in halves:
+                if t == VECTOR_TILE:
+                    nc.vector.tensor_tensor(val_tap[t][:, half], val_banks[t, half.start], val_tap[t][:, half], ADD)
+                else:
+                    nc.gpsimd.tensor_tensor(val_tap[t][:, half], val_window[t][:, half], val_tap[t][:, half], ADD)
 
-        val_product(0, slice(0, HALF), 0)
-        val_product(0, slice(HALF, S), 1)
-        first_tap(0)
+        def first_gate(t, cols):
+            nc.vector.tensor_tensor(h_window[t][:, cols], e_banks[t][:, cols], val_tap[t][:, cols], MULT)
+
+        val_product(0, halves[0], 0)
+        val_product(0, halves[1], 1)
         for t in range(1, PACK):
             val_product(t, slice(0, S), t + 1)
-            e_product(t - 1, t + 1)
-            first_tap(t)
-            first_gate(t - 1)
-        e_product(PACK - 1, 0)
+        for t in range(PACK):
+            for half in halves:
+                if t == VECTOR_TILE:
+                    nc.vector.tensor_copy(val_tap[t][:, half], val_window[t][:].indirect(entries(t1_sb, half.start, HALF)))
+                else:
+                    look_up(val_tap[t][:, half], val_window[t], t1_sb, half)
+        first_add(VECTOR_TILE)
+        for t, number in zip(EARLY_TILES + LATE_TILES, (5, 6, 7, 0)):
+            e_product(t, number)
+            if t != VECTOR_TILE:
+                first_add(t)
+            for half in halves:
+                first_gate(t, half)
 
         out_codes = held([P, S], U32, "out_codes")
         out_scales = held([P, S], U8, "out_scales")
         out_rows = out_0.rearrange("(p t) n -> p t n", t=PACK)
         out_words = out_1[0].rearrange("p c r -> p (c r)").bitcast(I32)
-        h_sum = held([P, PACK, S], F32, "h_sum")
+        h_sums = [held([P, PACK, HALF], F32, name) for name in ("first_sums", "taps2")]
+
+        def h_sum(tiles, cols):
+            first = cols.start % HALF
+            return h_sums[cols.start // HALF][:, tiles, first : first + cols.stop - cols.start]
+
         z_bf = held([P, S * PACK], BF16, "z_bf")
         z_codes = held([P, S], U32, "z_codes")
         z_scales = held([P, S], U8, "z_scales")
         out_f32 = [held([P, PACK, CHUNK], F32, "out_f32%d" % c) for c in range(CHUNKS)]
         out_bf = held([P, S * PACK], BF16, "out_bf")
 
-        def second_tap(t, first, count):
-            cols = slice(first, first + count)
-            nc.vector.tensor_tensor(
-                h_sum[:, t, cols], h_window[t][:].indirect(entries(t2_sb, first, count)), h_plain[t][:, cols], ADD
-            )
+        def second_add(engine, t, cols):
+            engine.tensor_tensor(h_sum(t, cols), h_sum(t, cols), h_window[t][:, cols], ADD)
 
         def second_gate(c):
             cols = slice(c * CHUNK, (c + 1) * CHUNK)
-            y_bank = bank(min(c + 1, 3), [P, PACK, CHUNK])
+            y_bank = bank(c + 1, [P, PACK, CHUNK])
             for t in range(PACK):
                 fp4_product(y_bank[:, t, :], w1_q, t, xq_words[:, cols], xq_scales[:, cols])
             width = CHUNK // 2 if c + 1 == CHUNKS else CHUNK
@@ -198,7 +215,7 @@ def tile_picked_hyena2_none_po_kernel(
                 nc.vector.tensor_tensor(
                     z_bf[:, PACK * first : PACK * (first + width)].rearrange("p (n i t) -> p n t i", i=2, t=PACK),
                     y_bank[:, :, first - cols.start : first - cols.start + width].rearrange("p t (n i) -> p n t i", i=2),
-                    h_sum[:, :, first : first + width].rearrange("p t (n i) -> p n t i", i=2),
+                    h_sum(slice(0, PACK), slice(first, first + width)).rearrange("p t (n i) -> p n t i", i=2),
                     MULT,
                 )
 
@@ -215,7 +232,8 @@ def tile_picked_hyena2_none_po_kernel(
                     fp4_product(out_bank[:, t, :], w4_q, t, z_codes[:, cols], z_scales[:, cols])
                 nc.scalar.copy(out_f32[c][:], out_bank[:])
                 nc.sync.dma_start(out_rows[:, :, cols], out_f32[c][:])
-                nc.scalar.copy(rounded.rearrange("p (n t) -> p n t", t=PACK), out_bank[:].rearrange("p t n -> p n t"))
+                if c < 2:
+                    nc.scalar.copy(rounded.rearrange("p (n t) -> p n t", t=PACK), out_bank[:].rearrange("p t n -> p n t"))
             else:
                 for pair, copy in enumerate((nc.scalar.copy, nc.vector.tensor_copy)):
                     pair_bank = bank(pair, [P, 2, CHUNK])
@@ -225,12 +243,16 @@ def tile_picked_hyena2_none_po_kernel(
                         half = slice(first, first + CHUNK // 2)
                         copy(out_f32[c][:, 2 * pair : 2 * pair + 2, half], pair_bank[:, :, half])
                 nc.sync.dma_start(out_rows[:, :, cols], out_f32[c][:])
-                quantise_out((c - 1) * CHUNK, CHUNK)
+                round_out(c - 1, 0, CHUNK)
                 for first in range(0, CHUNK, CHUNK // 2):
-                    nc.vector.tensor_copy(
-                        rounded[:, PACK * first : PACK * (first + CHUNK // 2)].rearrange("p (n i t) -> p n t i", i=4, t=PACK),
-                        out_f32[c][:, :, first : first + CHUNK // 2].rearrange("p t (n i) -> p n t i", i=4),
-                    )
+                    round_out(c, first, CHUNK // 2)
+                quantise_out((c - 1) * CHUNK, CHUNK)
+
+        def round_out(c, first, count):
+            nc.vector.tensor_copy(
+                out_bf[:, PACK * (c * CHUNK + first) : PACK * (c * CHUNK + first + count)].rearrange("p (n i t) -> p n t i", i=4, t=PACK),
+                out_f32[c][:, :, first : first + count].rearrange("p t (n i) -> p n t i", i=4),
+            )
 
         def quantise_out(first, count):
             cols = slice(first, first + count)
@@ -240,19 +262,21 @@ def tile_picked_hyena2_none_po_kernel(
             cols = slice(first, first + count)
             nc.sync.dma_start(out_words[:, cols], out_codes[:, cols].bitcast(I32))
 
-        for c in range(CHUNKS):
-            for t in range(PACK):
-                if c == 0:
-                    if t == 1:
-                        first_gate(PACK - 1)
-                    nc.scalar.copy(h_plain[t][:], h_window[t][:])
-                second_tap(t, c * CHUNK, CHUNK)
-                if t == 0 and c > 0:
-                    second_gate(c - 1)
-                if t == 1 and c > 0:
-                    quantise_z((c - 1) * CHUNK, CHUNK)
-                    last_layer(c - 1)
-        second_gate(CHUNKS - 1)
+        chunks = [slice(c * CHUNK, (c + 1) * CHUNK) for c in range(CHUNKS)]
+        for c, cols in enumerate(chunks):
+            if c % 2 == 0:
+                for t in EARLY_TILES:
+                    look_up(h_sum(t, halves[c // 2]), h_window[t], t2_sb, halves[c // 2])
+                    second_add(nc.gpsimd, t, halves[c // 2])
+            for t in LATE_TILES:
+                look_up(h_sum(t, cols), h_window[t], t2_sb, cols)
+        for c, cols in enumerate(chunks):
+            for t in LATE_TILES:
+                second_add(nc.vector, t, cols)
+            if c > 0:
+                quantise_z((c - 1) * CHUNK, CHUNK)
+                last_layer(c - 1)
+            second_gate(c)
         quantise_z(S - CHUNK, CHUNK // 2)
         quantise_z(S - CHUNK // 2, CHUNK // 2)
         quantise_out(0, HALF)

@@ -23,9 +23,8 @@ HALF = S // 2
 CHUNK = 128
 CHUNKS = S // CHUNK
 SCALAR_W3_COLUMNS = 44
-VECTOR_TILE = 3
-EARLY_TILES = (0, 3)
-LATE_TILES = (1, 2)
+EARLY_TILES = (0, 1)
+LATE_TILES = (2, 3)
 
 
 def entries(lst, first, count):
@@ -74,8 +73,8 @@ def tile_picked_hyena2_none_po_kernel(
         w1_raw = load_words(w1_words, "w1")
         w4_raw = load_words(w4_words, "w4")
 
-        def deal_words(raw_words, words):
-            nc.vector.tensor_copy(
+        def deal_words(copy, raw_words, words):
+            copy(
                 words.bitcast(U16).rearrange("p (t m) -> p t m", t=PACK),
                 raw_words[:].bitcast(U16).rearrange("p (m t) -> p t m", t=PACK),
             )
@@ -117,10 +116,10 @@ def tile_picked_hyena2_none_po_kernel(
         xq_words = held([P, S], U32, "w3_bf")
         for u in range(2):
             nc.vector.tensor_copy(xq_words[:, u * HALF : (u + 1) * HALF], x_word_table[:].indirect(entries(offs_sb, u * HALF, HALF)))
-        w_dealt = held([P, 6 * H], U8, "x_word_table")
-        w2_q = deal_words(w2_raw, w_dealt[:, 0 : 2 * H]), w2_scales_dealt[:]
-        w1_q = deal_words(w1_raw, w_dealt[:, 2 * H : 4 * H]), late_scales[:, 0:H]
-        w4_q = deal_words(w4_raw, w_dealt[:, 4 * H : 6 * H]), late_scales[:, H : 2 * H]
+        w_dealt = held([P, 6 * H], U8, "w_dealt")
+        w2_q = deal_words(nc.scalar.copy, w2_raw, w_dealt[:, 0 : 2 * H]), w2_scales_dealt[:]
+        w1_q = deal_words(nc.scalar.copy, w1_raw, w_dealt[:, 2 * H : 4 * H]), late_scales[:, 0:H]
+        w4_q = deal_words(nc.vector.tensor_copy, w4_raw, w_dealt[:, 4 * H : 6 * H]), late_scales[:, H : 2 * H]
 
         def bank(number, shape):
             return psum.tile(shape, F32, name="bank%d" % number)
@@ -148,7 +147,7 @@ def tile_picked_hyena2_none_po_kernel(
             for half in halves:
                 if cols.start <= half.start and half.stop <= cols.stop:
                     val_banks[t, half.start] = val_bank[:, half.start - cols.start : half.stop - cols.start]
-            copy = nc.scalar.copy if t == 0 else nc.vector.tensor_copy
+            copy = nc.scalar.copy if t == 1 else nc.vector.tensor_copy
             copy(val_window[t][:, cols], val_bank[:])
 
         def e_product(t, number):
@@ -158,39 +157,42 @@ def tile_picked_hyena2_none_po_kernel(
         def look_up(result, window, lst, cols):
             nc.scalar.activation(result, window[:].indirect(entries(lst, cols.start, cols.stop - cols.start)), COPY)
 
+        def first_tap(t):
+            for half in halves:
+                if t == 0:
+                    nc.vector.tensor_copy(val_tap[t][:, half], val_window[t][:].indirect(entries(t1_sb, half.start, HALF)))
+                else:
+                    look_up(val_tap[t][:, half], val_window[t], t1_sb, half)
+
         def first_add(t):
             for half in halves:
-                if t == VECTOR_TILE:
+                if t in (0, 3):
                     nc.vector.tensor_tensor(val_tap[t][:, half], val_banks[t, half.start], val_tap[t][:, half], ADD)
                 else:
                     nc.gpsimd.tensor_tensor(val_tap[t][:, half], val_window[t][:, half], val_tap[t][:, half], ADD)
 
-        def first_gate(t, cols):
-            nc.vector.tensor_tensor(h_window[t][:, cols], e_banks[t][:, cols], val_tap[t][:, cols], MULT)
-
-        val_product(0, halves[0], 0)
-        val_product(0, halves[1], 1)
-        for t in range(1, PACK):
-            val_product(t, slice(0, S), t + 1)
-        for t in range(PACK):
-            for half in halves:
-                if t == VECTOR_TILE:
-                    nc.vector.tensor_copy(val_tap[t][:, half], val_window[t][:].indirect(entries(t1_sb, half.start, HALF)))
-                else:
-                    look_up(val_tap[t][:, half], val_window[t], t1_sb, half)
-        first_add(VECTOR_TILE)
-        for t, number in zip(EARLY_TILES + LATE_TILES, (5, 6, 7, 0)):
+        def first_gate(t, number):
             e_product(t, number)
-            if t != VECTOR_TILE:
-                first_add(t)
             for half in halves:
-                first_gate(t, half)
+                nc.vector.tensor_tensor(h_window[t][:, half], e_banks[t][:, half], val_tap[t][:, half], MULT)
+
+        for u, half in enumerate(halves):
+            for t in range(2):
+                val_product(t, half, 2 * u + t)
+        first_tap(0)
+        first_tap(1)
+        for t in range(2, PACK):
+            val_product(t, slice(0, S), t + 2)
+            first_tap(t)
+        for t, number in enumerate((6, 7, 1, 3)):
+            first_add(t)
+            first_gate(t, number)
 
         out_codes = held([P, S], U32, "out_codes")
         out_scales = held([P, S], U8, "out_scales")
         out_rows = out_0.rearrange("(p t) n -> p t n", t=PACK)
         out_words = out_1[0].rearrange("p c r -> p (c r)").bitcast(I32)
-        h_sums = [held([P, PACK, HALF], F32, name) for name in ("first_sums", "taps2")]
+        h_sums = [held([P, PACK, HALF], F32, name) for name in ("first_sums", "taps3")]
 
         def h_sum(tiles, cols):
             first = cols.start % HALF
@@ -207,7 +209,7 @@ def tile_picked_hyena2_none_po_kernel(
 
         def second_gate(c):
             cols = slice(c * CHUNK, (c + 1) * CHUNK)
-            y_bank = bank(c + 1, [P, PACK, CHUNK])
+            y_bank = bank((0, 2, 6, 7)[c], [P, PACK, CHUNK])
             for t in range(PACK):
                 fp4_product(y_bank[:, t, :], w1_q, t, xq_words[:, cols], xq_scales[:, cols])
             width = CHUNK // 2 if c + 1 == CHUNKS else CHUNK
@@ -227,7 +229,7 @@ def tile_picked_hyena2_none_po_kernel(
             cols = slice(c * CHUNK, (c + 1) * CHUNK)
             rounded = out_bf[:, PACK * cols.start : PACK * cols.stop]
             if c + 1 < CHUNKS:
-                out_bank = bank(c + 5, [P, PACK, CHUNK])
+                out_bank = bank((4, 1, 5)[c], [P, PACK, CHUNK])
                 for t in range(PACK):
                     fp4_product(out_bank[:, t, :], w4_q, t, z_codes[:, cols], z_scales[:, cols])
                 nc.scalar.copy(out_f32[c][:], out_bank[:])
@@ -236,7 +238,7 @@ def tile_picked_hyena2_none_po_kernel(
                     nc.scalar.copy(rounded.rearrange("p (n t) -> p n t", t=PACK), out_bank[:].rearrange("p t n -> p n t"))
             else:
                 for pair, copy in enumerate((nc.scalar.copy, nc.vector.tensor_copy)):
-                    pair_bank = bank(pair, [P, 2, CHUNK])
+                    pair_bank = bank(3 * (1 - pair), [P, 2, CHUNK])
                     for t in range(2):
                         fp4_product(pair_bank[:, t, :], w4_q, 2 * pair + t, z_codes[:, cols], z_scales[:, cols])
                     for first in range(0, CHUNK, CHUNK // 2):

@@ -22,7 +22,6 @@ PACK = 4
 HALF = S // 2
 CHUNK = 128
 CHUNKS = S // CHUNK
-SCALAR_W3_COLUMNS = 44
 EARLY_TILES = (0, 1)
 LATE_TILES = (2, 3)
 
@@ -58,14 +57,14 @@ def tile_picked_hyena2_none_po_kernel(
         nc.gpsimd.memset(w_scale_rows[:].bitcast(I32), 0)
 
         nc.sync.dma_start(offs_sb[:], offs)
-        w3_raw = [held([P, PACK, H // 2], F32, "w3_raw%d" % u) for u in range(2)]
+        w3_raw = [held([P, 2, H], F32, "w3_raw%d" % u) for u in range(2)]
         w3_rows = w3.rearrange("(p j) c -> p j c", j=PACK)
-        nc.sync.dma_start(w3_raw[0][:], w3_rows[:, :, : H // 2])
+        nc.sync.dma_start(w3_raw[0][:], w3_rows[:, 0:2, :])
         for j in range(2):
             nc.sync.dma_start(x_scale_table[j:P:16, :].bitcast(I32), x_scales[0, j:16:2, :].bitcast(I32))
         for i, scales in enumerate((w1_scales, w4_scales)):
             nc.sync.dma_start(w_scale_rows[0:16, i * H : (i + 1) * H].bitcast(I32), scales[0].bitcast(I32))
-        nc.sync.dma_start(w3_raw[1][:], w3_rows[:, :, H // 2 :])
+        nc.sync.dma_start(w3_raw[1][:], w3_rows[:, 2:4, :])
         nc.sync.dma_start(w_scale_rows[0:16, 2 * H : 3 * H].bitcast(I32), w2_scales[0].bitcast(I32))
         x_word_table = held([P, T], U32, "x_word_table")
         nc.sync.dma_start(x_word_table[:].bitcast(I32), x_words[0].rearrange("p c r -> p (c r)").bitcast(I32))
@@ -100,22 +99,26 @@ def tile_picked_hyena2_none_po_kernel(
         w3_bf = held([P, PACK * P * PACK], BF16, "w3_bf")
         w3_dealt = w3_bf[:].rearrange("p (t m j) -> p m t j", t=PACK, j=PACK)
         w3_walk = [raw[:].rearrange("p j (m t) -> p m t j", t=PACK) for raw in w3_raw]
-        nc.scalar.copy(w3_dealt[:, : P // 2, :, :], w3_walk[0])
-        nc.scalar.copy(w3_dealt[:, P // 2 : P // 2 + SCALAR_W3_COLUMNS, :, :], w3_walk[1][:, :SCALAR_W3_COLUMNS, :, :])
-        nc.vector.tensor_copy(w3_dealt[:, P // 2 + SCALAR_W3_COLUMNS :, :, :], w3_walk[1][:, SCALAR_W3_COLUMNS:, :, :])
+        nc.scalar.copy(w3_dealt[:, :, :, 0:2], w3_walk[0])
         w2_scales_dealt = held([P, H], U8, "w2_scales_dealt")
         deal_scales(nc.vector, w_scale_rows[:, 2 * H : 3 * H], w2_scales_dealt[:])
         nc.sync.dma_start(t2_sb[:], t2)
         late_scales = held([P, 2 * H], U8, "late_scales")
         deal_scales(nc.gpsimd, w_scale_rows[:, 0 : 2 * H], late_scales[:])
-        w3_codes = held([P, H], U32, "w3_codes")
         w3_scales = held([P, H], U8, "w3_scales")
-        nc.vector.quantize_mx(w3_codes[:].bitcast(FP8X4), w3_scales[:], w3_bf[:])
+        w3_code_pairs = []
 
+        def quantise_w3(pair, name):
+            nc.scalar.copy(w3_dealt[:, :, 2 * pair : 2 * pair + 2, 2:4], w3_walk[1][:, :, 2 * pair : 2 * pair + 2, :])
+            codes = held([P, 2 * P], U32, name)
+            nc.vector.quantize_mx(codes[:].bitcast(FP8X4), w3_scales[:, 2 * P * pair : 2 * P * (pair + 1)], w3_bf[:, 2 * H * pair : 2 * H * (pair + 1)])
+            w3_code_pairs.append(codes)
 
-        xq_words = held([P, S], U32, "w3_bf")
+        quantise_w3(0, "w3_codes")
+        xq_words = held([P, S], U32, "xq_words")
         for u in range(2):
             nc.vector.tensor_copy(xq_words[:, u * HALF : (u + 1) * HALF], x_word_table[:].indirect(entries(offs_sb, u * HALF, HALF)))
+        quantise_w3(1, "x_word_table")
         w_dealt = held([P, 6 * H], U8, "w_dealt")
         w2_q = deal_words(nc.scalar.copy, w2_raw, w_dealt[:, 0 : 2 * H]), w2_scales_dealt[:]
         w1_q = deal_words(nc.scalar.copy, w1_raw, w_dealt[:, 2 * H : 4 * H]), late_scales[:, 0:H]
@@ -133,6 +136,8 @@ def tile_picked_hyena2_none_po_kernel(
 
         val_window = [held([P, S], F32, "val_window%d" % t) for t in range(PACK)]
         val_tap = [held([P, S], F32, "taps%d" % t) for t in range(PACK)]
+        first_sums = held([P, PACK, HALF], F32, "first_sums")
+        last_sum = first_sums[:, 2, :]
         h_window = [held([P, S], F32, "h_window%d" % t) for t in range(PACK)]
         halves = [slice(0, HALF), slice(HALF, S)]
         val_banks = {}
@@ -141,7 +146,7 @@ def tile_picked_hyena2_none_po_kernel(
         def val_product(t, cols, number):
             val_bank = bank(number, [P, cols.stop - cols.start])
             nc.tensor.matmul_mx(
-                val_bank[:], lhsT=w3_codes[:, P * t : P * (t + 1)].bitcast(FP8X4), lhsT_scale=w3_scales[:, P * t : P * (t + 1)],
+                val_bank[:], lhsT=w3_code_pairs[t // 2][:, P * (t % 2) : P * (t % 2 + 1)].bitcast(FP8X4), lhsT_scale=w3_scales[:, P * t : P * (t + 1)],
                 rhs=xq_words[:, cols].bitcast(FP8X4), rhs_scale=xq_scales[:, cols], start=True, stop=True,
             )
             for half in halves:
@@ -164,17 +169,20 @@ def tile_picked_hyena2_none_po_kernel(
                 else:
                     look_up(val_tap[t][:, half], val_window[t], t1_sb, half)
 
+        def val_sum(t, half):
+            return last_sum if (t, half) == (3, halves[1]) else val_tap[t][:, half]
+
         def first_add(t):
             for half in halves:
-                if t in (0, 3):
-                    nc.vector.tensor_tensor(val_tap[t][:, half], val_banks[t, half.start], val_tap[t][:, half], ADD)
+                if t == 0 or (t, half) == (3, halves[1]):
+                    nc.vector.tensor_tensor(val_sum(t, half), val_banks[t, half.start], val_tap[t][:, half], ADD)
                 else:
                     nc.gpsimd.tensor_tensor(val_tap[t][:, half], val_window[t][:, half], val_tap[t][:, half], ADD)
 
         def first_gate(t, number):
             e_product(t, number)
             for half in halves:
-                nc.vector.tensor_tensor(h_window[t][:, half], e_banks[t][:, half], val_tap[t][:, half], MULT)
+                nc.vector.tensor_tensor(h_window[t][:, half], e_banks[t][:, half], val_sum(t, half), MULT)
 
         for u, half in enumerate(halves):
             for t in range(2):
@@ -192,7 +200,7 @@ def tile_picked_hyena2_none_po_kernel(
         out_scales = held([P, S], U8, "out_scales")
         out_rows = out_0.rearrange("(p t) n -> p t n", t=PACK)
         out_words = out_1[0].rearrange("p c r -> p (c r)").bitcast(I32)
-        h_sums = [held([P, PACK, HALF], F32, name) for name in ("first_sums", "taps3")]
+        h_sums = [first_sums]
 
         def h_sum(tiles, cols):
             first = cols.start % HALF
@@ -209,7 +217,7 @@ def tile_picked_hyena2_none_po_kernel(
 
         def second_gate(c):
             cols = slice(c * CHUNK, (c + 1) * CHUNK)
-            y_bank = bank((0, 2, 6, 7)[c], [P, PACK, CHUNK])
+            y_bank = bank((0, 2, 0, 2)[c], [P, PACK, CHUNK])
             for t in range(PACK):
                 fp4_product(y_bank[:, t, :], w1_q, t, xq_words[:, cols], xq_scales[:, cols])
             width = CHUNK // 2 if c + 1 == CHUNKS else CHUNK
@@ -234,18 +242,19 @@ def tile_picked_hyena2_none_po_kernel(
                     fp4_product(out_bank[:, t, :], w4_q, t, z_codes[:, cols], z_scales[:, cols])
                 nc.scalar.copy(out_f32[c][:], out_bank[:])
                 nc.sync.dma_start(out_rows[:, :, cols], out_f32[c][:])
-                if c < 2:
+                if c == 2:
                     nc.scalar.copy(rounded.rearrange("p (n t) -> p n t", t=PACK), out_bank[:].rearrange("p t n -> p n t"))
             else:
                 for pair, copy in enumerate((nc.scalar.copy, nc.vector.tensor_copy)):
-                    pair_bank = bank(3 * (1 - pair), [P, 2, CHUNK])
+                    pair_bank = bank(6 + pair, [P, 2, CHUNK])
                     for t in range(2):
                         fp4_product(pair_bank[:, t, :], w4_q, 2 * pair + t, z_codes[:, cols], z_scales[:, cols])
                     for first in range(0, CHUNK, CHUNK // 2):
                         half = slice(first, first + CHUNK // 2)
                         copy(out_f32[c][:, 2 * pair : 2 * pair + 2, half], pair_bank[:, :, half])
                 nc.sync.dma_start(out_rows[:, :, cols], out_f32[c][:])
-                round_out(c - 1, 0, CHUNK)
+                quantise_out(0, HALF)
+                store_codes(0, HALF)
                 for first in range(0, CHUNK, CHUNK // 2):
                     round_out(c, first, CHUNK // 2)
                 quantise_out((c - 1) * CHUNK, CHUNK)
@@ -265,24 +274,35 @@ def tile_picked_hyena2_none_po_kernel(
             nc.sync.dma_start(out_words[:, cols], out_codes[:, cols].bitcast(I32))
 
         chunks = [slice(c * CHUNK, (c + 1) * CHUNK) for c in range(CHUNKS)]
+        def early_tap(t, cols):
+            look_up(h_sum(t, cols), h_window[t], t2_sb, cols)
+            second_add(nc.gpsimd, t, cols)
+
+        for t in EARLY_TILES:
+            early_tap(t, halves[0])
+        for t, name in zip(LATE_TILES, ("staged", "later_sums")):
+            staged = held([P, CHUNK], F32, name)
+            look_up(staged[:], h_window[t], t2_sb, chunks[0])
+            nc.vector.tensor_tensor(h_sum(t, chunks[0]), staged[:], h_window[t][:, chunks[0]], ADD)
+        h_sums.append(held([P, PACK, HALF], F32, "later_sums"))
         for c, cols in enumerate(chunks):
-            if c % 2 == 0:
+            if c >= 2:
                 for t in EARLY_TILES:
-                    look_up(h_sum(t, halves[c // 2]), h_window[t], t2_sb, halves[c // 2])
-                    second_add(nc.gpsimd, t, halves[c // 2])
-            for t in LATE_TILES:
-                look_up(h_sum(t, cols), h_window[t], t2_sb, cols)
+                    early_tap(t, cols)
+            if c >= 1:
+                for t in LATE_TILES:
+                    look_up(h_sum(t, cols), h_window[t], t2_sb, cols)
         for c, cols in enumerate(chunks):
-            for t in LATE_TILES:
-                second_add(nc.vector, t, cols)
             if c > 0:
+                for t in LATE_TILES:
+                    second_add(nc.vector, t, cols)
                 quantise_z((c - 1) * CHUNK, CHUNK)
                 last_layer(c - 1)
             second_gate(c)
         quantise_z(S - CHUNK, CHUNK // 2)
         quantise_z(S - CHUNK // 2, CHUNK // 2)
-        quantise_out(0, HALF)
-        store_codes(0, HALF)
+        for c in range(2):
+            round_out(c, 0, CHUNK)
         last_layer(CHUNKS - 1)
         quantise_out(S - CHUNK, CHUNK // 2)
         quantise_out(S - CHUNK // 2, CHUNK // 2)

@@ -242,7 +242,7 @@ def tile_picked_hyena2_none_po_kernel(
                     fp4_product(out_bank[:, t, :], w4_q, t, z_codes[:, cols], z_scales[:, cols])
                 nc.scalar.copy(out_f32[c][:], out_bank[:])
                 nc.sync.dma_start(out_rows[:, :, cols], out_f32[c][:])
-                if c == 2:
+                if c < 2:
                     nc.scalar.copy(rounded.rearrange("p (n t) -> p n t", t=PACK), out_bank[:].rearrange("p t n -> p n t"))
             else:
                 for pair, copy in enumerate((nc.scalar.copy, nc.vector.tensor_copy)):
@@ -288,21 +288,20 @@ def tile_picked_hyena2_none_po_kernel(
         for c, cols in enumerate(chunks):
             if c >= 2:
                 for t in EARLY_TILES:
-                    early_tap(t, cols)
+                    look_up(h_sum(t, cols), h_window[t], t2_sb, cols)
             if c >= 1:
                 for t in LATE_TILES:
                     look_up(h_sum(t, cols), h_window[t], t2_sb, cols)
         for c, cols in enumerate(chunks):
             if c > 0:
-                for t in LATE_TILES:
+                for t in LATE_TILES if c < 2 else range(PACK):
                     second_add(nc.vector, t, cols)
                 quantise_z((c - 1) * CHUNK, CHUNK)
                 last_layer(c - 1)
             second_gate(c)
         quantise_z(S - CHUNK, CHUNK // 2)
         quantise_z(S - CHUNK // 2, CHUNK // 2)
-        for c in range(2):
-            round_out(c, 0, CHUNK)
+        round_out(2, 0, CHUNK)
         last_layer(CHUNKS - 1)
         quantise_out(S - CHUNK, CHUNK // 2)
         quantise_out(S - CHUNK // 2, CHUNK // 2)

@@ -196,8 +196,6 @@ def tile_picked_hyena2_none_po_kernel(
             first_add(t)
             first_gate(t, number)
 
-        out_codes = held([P, S], U32, "out_codes")
-        out_scales = held([P, S], U8, "out_scales")
         out_rows = out_0.rearrange("(p t) n -> p t n", t=PACK)
         out_words = out_1[0].rearrange("p c r -> p (c r)").bitcast(I32)
         h_sums = [first_sums]
@@ -206,11 +204,12 @@ def tile_picked_hyena2_none_po_kernel(
             first = cols.start % HALF
             return h_sums[cols.start // HALF][:, tiles, first : first + cols.stop - cols.start]
 
-        z_bf = held([P, S * PACK], BF16, "z_bf")
+        z_bf = {}
         z_codes = held([P, S], U32, "z_codes")
         z_scales = held([P, S], U8, "z_scales")
         out_f32 = [held([P, PACK, CHUNK], F32, "out_f32%d" % c) for c in range(CHUNKS)]
-        out_bf = held([P, S * PACK], BF16, "out_bf")
+        early_bf = {0: held([P, CHUNK * PACK], BF16, "out_bf0")}
+        late_bf = held([P, HALF * PACK], BF16, "late_bf")
 
         def second_add(engine, t, cols):
             engine.tensor_tensor(h_sum(t, cols), h_sum(t, cols), h_window[t][:, cols], ADD)
@@ -220,10 +219,11 @@ def tile_picked_hyena2_none_po_kernel(
             y_bank = bank((0, 2, 0, 2)[c], [P, PACK, CHUNK])
             for t in range(PACK):
                 fp4_product(y_bank[:, t, :], w1_q, t, xq_words[:, cols], xq_scales[:, cols])
-            width = CHUNK // 2 if c + 1 == CHUNKS else CHUNK
+            width = CHUNK
             for first in range(cols.start, cols.stop, width):
+                z_bf[first] = held([P, PACK * width], BF16, "z_bf%d" % first)
                 nc.vector.tensor_tensor(
-                    z_bf[:, PACK * first : PACK * (first + width)].rearrange("p (n i t) -> p n t i", i=2, t=PACK),
+                    z_bf[first][:].rearrange("p (n i t) -> p n t i", i=2, t=PACK),
                     y_bank[:, :, first - cols.start : first - cols.start + width].rearrange("p t (n i) -> p n t i", i=2),
                     h_sum(slice(0, PACK), slice(first, first + width)).rearrange("p t (n i) -> p n t i", i=2),
                     MULT,
@@ -231,18 +231,18 @@ def tile_picked_hyena2_none_po_kernel(
 
         def quantise_z(first, count):
             cols = slice(first, first + count)
-            nc.vector.quantize_mx(z_codes[:, cols].bitcast(FP8X4), z_scales[:, cols], z_bf[:, PACK * first : PACK * (first + count)])
+            nc.vector.quantize_mx(z_codes[:, cols].bitcast(FP8X4), z_scales[:, cols], z_bf[first][:])
 
         def last_layer(c):
             cols = slice(c * CHUNK, (c + 1) * CHUNK)
-            rounded = out_bf[:, PACK * cols.start : PACK * cols.stop]
             if c + 1 < CHUNKS:
                 out_bank = bank((4, 1, 5)[c], [P, PACK, CHUNK])
                 for t in range(PACK):
                     fp4_product(out_bank[:, t, :], w4_q, t, z_codes[:, cols], z_scales[:, cols])
                 nc.scalar.copy(out_f32[c][:], out_bank[:])
                 nc.sync.dma_start(out_rows[:, :, cols], out_f32[c][:])
-                if c < 2:
+                if c != 1:
+                    rounded = early_bf[0][:] if c == 0 else late_bf[:, : PACK * CHUNK]
                     nc.scalar.copy(rounded.rearrange("p (n t) -> p n t", t=PACK), out_bank[:].rearrange("p t n -> p n t"))
             else:
                 for pair, copy in enumerate((nc.scalar.copy, nc.vector.tensor_copy)):
@@ -253,25 +253,6 @@ def tile_picked_hyena2_none_po_kernel(
                         half = slice(first, first + CHUNK // 2)
                         copy(out_f32[c][:, 2 * pair : 2 * pair + 2, half], pair_bank[:, :, half])
                 nc.sync.dma_start(out_rows[:, :, cols], out_f32[c][:])
-                quantise_out(0, HALF)
-                store_codes(0, HALF)
-                for first in range(0, CHUNK, CHUNK // 2):
-                    round_out(c, first, CHUNK // 2)
-                quantise_out((c - 1) * CHUNK, CHUNK)
-
-        def round_out(c, first, count):
-            nc.vector.tensor_copy(
-                out_bf[:, PACK * (c * CHUNK + first) : PACK * (c * CHUNK + first + count)].rearrange("p (n i t) -> p n t i", i=4, t=PACK),
-                out_f32[c][:, :, first : first + count].rearrange("p t (n i) -> p n t i", i=4),
-            )
-
-        def quantise_out(first, count):
-            cols = slice(first, first + count)
-            nc.vector.quantize_mx(out_codes[:, cols].bitcast(FP8X4), out_scales[:, cols], out_bf[:, PACK * first : PACK * (first + count)])
-
-        def store_codes(first, count):
-            cols = slice(first, first + count)
-            nc.sync.dma_start(out_words[:, cols], out_codes[:, cols].bitcast(I32))
 
         chunks = [slice(c * CHUNK, (c + 1) * CHUNK) for c in range(CHUNKS)]
         def early_tap(t, cols):
@@ -299,13 +280,31 @@ def tile_picked_hyena2_none_po_kernel(
                 quantise_z((c - 1) * CHUNK, CHUNK)
                 last_layer(c - 1)
             second_gate(c)
-        quantise_z(S - CHUNK, CHUNK // 2)
-        quantise_z(S - CHUNK // 2, CHUNK // 2)
-        round_out(2, 0, CHUNK)
+        quantise_z(S - CHUNK, CHUNK)
+        out_scales = held([P, S], U8, "later_sums")
+        early_bf[1] = held([P, CHUNK * PACK], BF16, "z_bf%d" % (S - CHUNK))
+        nc.vector.tensor_copy(
+            early_bf[1][:].rearrange("p (n i t) -> p n t i", i=4, t=PACK), out_f32[1][:].rearrange("p t (n i) -> p n t i", i=4)
+        )
+        early_codes = held([P, HALF], U32, "early_codes")
+        for c in range(2):
+            nc.vector.quantize_mx(early_codes[:, chunks[c]].bitcast(FP8X4), out_scales[:, chunks[c]], early_bf[c][:])
+        nc.sync.dma_start(out_words[:, halves[0]], early_codes[:].bitcast(I32))
         last_layer(CHUNKS - 1)
-        quantise_out(S - CHUNK, CHUNK // 2)
-        quantise_out(S - CHUNK // 2, CHUNK // 2)
-        store_codes(HALF, HALF)
+        late_codes = held([P, HALF], U32, "late_codes")
+        nc.vector.quantize_mx(late_codes[:, :CHUNK].bitcast(FP8X4), out_scales[:, chunks[2]], late_bf[:, : PACK * CHUNK])
+        for first in range(0, CHUNK, CHUNK // 2):
+            nc.vector.tensor_copy(
+                late_bf[:, PACK * (CHUNK + first) : PACK * (CHUNK + first + CHUNK // 2)].rearrange("p (n i t) -> p n t i", i=4, t=PACK),
+                out_f32[CHUNKS - 1][:, :, first : first + CHUNK // 2].rearrange("p t (n i) -> p n t i", i=4),
+            )
+        for first in range(CHUNK, HALF, CHUNK // 2):
+            nc.vector.quantize_mx(
+                late_codes[:, first : first + CHUNK // 2].bitcast(FP8X4),
+                out_scales[:, HALF + first : HALF + first + CHUNK // 2],
+                late_bf[:, PACK * first : PACK * (first + CHUNK // 2)],
+            )
+        nc.sync.dma_start(out_words[:, halves[1]], late_codes[:].bitcast(I32))
         for q in range(4):
             queue = nc.sync if q < 2 else nc.scalar
             queue.dma_start(out_2[0, 4 * q : 4 * q + 4, :].bitcast(I32), out_scales[32 * q : 32 * q + 4, :].bitcast(I32))

@@ -57,14 +57,14 @@ def tile_picked_hyena2_none_po_kernel(
         nc.gpsimd.memset(w_scale_rows[:].bitcast(I32), 0)
 
         nc.sync.dma_start(offs_sb[:], offs)
-        w3_raw = [held([P, 2, H], F32, "w3_raw%d" % u) for u in range(2)]
+        w3_raw = held([P, PACK, H], F32, "w3_raw")
         w3_rows = w3.rearrange("(p j) c -> p j c", j=PACK)
-        nc.sync.dma_start(w3_raw[0][:], w3_rows[:, 0:2, :])
+        nc.sync.dma_start(w3_raw[:, 0:2, :], w3_rows[:, 0:2, :])
         for j in range(2):
             nc.sync.dma_start(x_scale_table[j:P:16, :].bitcast(I32), x_scales[0, j:16:2, :].bitcast(I32))
         for i, scales in enumerate((w1_scales, w4_scales)):
             nc.sync.dma_start(w_scale_rows[0:16, i * H : (i + 1) * H].bitcast(I32), scales[0].bitcast(I32))
-        nc.sync.dma_start(w3_raw[1][:], w3_rows[:, 2:4, :])
+        nc.sync.dma_start(w3_raw[:, 2:4, :], w3_rows[:, 2:4, :])
         nc.sync.dma_start(w_scale_rows[0:16, 2 * H : 3 * H].bitcast(I32), w2_scales[0].bitcast(I32))
         x_word_table = held([P, T], U32, "x_word_table")
         nc.sync.dma_start(x_word_table[:].bitcast(I32), x_words[0].rearrange("p c r -> p (c r)").bitcast(I32))
@@ -98,8 +98,10 @@ def tile_picked_hyena2_none_po_kernel(
 
         w3_bf = held([P, PACK * P * PACK], BF16, "w3_bf")
         w3_dealt = w3_bf[:].rearrange("p (t m j) -> p m t j", t=PACK, j=PACK)
-        w3_walk = [raw[:].rearrange("p j (m t) -> p m t j", t=PACK) for raw in w3_raw]
-        nc.scalar.copy(w3_dealt[:, :, :, 0:2], w3_walk[0])
+        w3_walk = w3_raw[:].rearrange("p j (m t) -> p m t j", t=PACK)
+        for rows in (slice(0, 2), slice(2, 4)):
+            nc.scalar.copy(w3_dealt[:, :, 0:2, rows], w3_walk[:, :, 0:2, rows])
+        nc.scalar.copy(w3_dealt[:, :, 2:4, :], w3_walk[:, :, 2:4, :])
         w2_scales_dealt = held([P, H], U8, "w2_scales_dealt")
         deal_scales(nc.vector, w_scale_rows[:, 2 * H : 3 * H], w2_scales_dealt[:])
         nc.sync.dma_start(t2_sb[:], t2)
@@ -109,12 +111,17 @@ def tile_picked_hyena2_none_po_kernel(
         w3_code_pairs = []
 
         def quantise_w3(pair, name):
-            nc.scalar.copy(w3_dealt[:, :, 2 * pair : 2 * pair + 2, 2:4], w3_walk[1][:, :, 2 * pair : 2 * pair + 2, :])
             codes = held([P, 2 * P], U32, name)
             nc.vector.quantize_mx(codes[:].bitcast(FP8X4), w3_scales[:, 2 * P * pair : 2 * P * (pair + 1)], w3_bf[:, 2 * H * pair : 2 * H * (pair + 1)])
             w3_code_pairs.append(codes)
 
         quantise_w3(0, "w3_codes")
+        warm = psum.tile([P, HALF], F32, name="bank7")
+        for repeat in range(4):
+            nc.tensor.matmul_mx(
+                warm[:], lhsT=w3_code_pairs[0][:, 0:P].bitcast(FP8X4), lhsT_scale=w3_scales[:, 0:P],
+                rhs=w3_code_pairs[0][:].bitcast(FP8X4), rhs_scale=w3_scales[:, 0 : 2 * P], start=True, stop=True,
+            )
         xq_words = held([P, S], U32, "xq_words")
         for u in range(2):
             nc.vector.tensor_copy(xq_words[:, u * HALF : (u + 1) * HALF], x_word_table[:].indirect(entries(offs_sb, u * HALF, HALF)))

@@ -56,12 +56,11 @@ def tile_picked_hyena2_none_po_kernel(
         w_scale_rows = held([P, 3 * H], U8, "w_scale_rows")
         nc.gpsimd.memset(w_scale_rows[:].bitcast(I32), 0)
 
-        nc.sync.dma_start(offs_sb[:], offs)
         w3_raw = held([P, PACK, H], F32, "w3_raw")
         w3_rows = w3.rearrange("(p j) c -> p j c", j=PACK)
         nc.sync.dma_start(w3_raw[:, 0:2, :], w3_rows[:, 0:2, :])
-        for j in range(2):
-            nc.sync.dma_start(x_scale_table[j:P:16, :].bitcast(I32), x_scales[0, j:16:2, :].bitcast(I32))
+        nc.sync.dma_start(offs_sb[:], offs)
+        nc.sync.dma_start(x_scale_table[0:P:8, :].bitcast(I32), x_scales[0].bitcast(I32))
         for i, scales in enumerate((w1_scales, w4_scales)):
             nc.sync.dma_start(w_scale_rows[0:16, i * H : (i + 1) * H].bitcast(I32), scales[0].bitcast(I32))
         nc.sync.dma_start(w3_raw[:, 2:4, :], w3_rows[:, 2:4, :])
@@ -83,8 +82,8 @@ def tile_picked_hyena2_none_po_kernel(
         nc.vector.tensor_copy(x_scale_picked[:], x_scale_table[:].indirect(offs_sb[:]))
         xq_scales = held([P, S], U8, "xq_scales")
         nc.vector.tensor_copy(xq_scales[:].bitcast(I32), x_scale_picked[:].bitcast(I32))
-        for j in range(2):
-            nc.sync.dma_start(xq_scales[2 + j : P : 32, :].bitcast(I32), x_scale_picked[16 + j : P : 32, :].bitcast(I32))
+        for j in range(1, 4):
+            nc.sync.dma_start(xq_scales[j:P:32, :].bitcast(I32), x_scale_picked[8 * j : P : 32, :].bitcast(I32))
         nc.sync.dma_start(t1_sb[:], t1)
 
 
@@ -192,7 +191,7 @@ def tile_picked_hyena2_none_po_kernel(
                 nc.vector.tensor_tensor(h_window[t][:, half], e_banks[t][:, half], val_sum(t, half), MULT)
 
         for u, half in enumerate(halves):
-            for t in range(2):
+            for t in (1, 0):
                 val_product(t, half, 2 * u + t)
         first_tap(0)
         first_tap(1)

@@ -69,7 +69,6 @@ def tile_picked_hyena2_none_po_kernel(
         nc.sync.dma_start(x_word_table[:].bitcast(I32), x_words[0].rearrange("p c r -> p (c r)").bitcast(I32))
         w2_raw = load_words(w2_words, "w2")
         w1_raw = load_words(w1_words, "w1")
-        w4_raw = load_words(w4_words, "w4")
 
         def deal_words(copy, raw_words, words):
             copy(
@@ -84,6 +83,7 @@ def tile_picked_hyena2_none_po_kernel(
         nc.vector.tensor_copy(xq_scales[:].bitcast(I32), x_scale_picked[:].bitcast(I32))
         for j in range(1, 4):
             nc.sync.dma_start(xq_scales[j:P:32, :].bitcast(I32), x_scale_picked[8 * j : P : 32, :].bitcast(I32))
+        w4_raw = load_words(w4_words, "w4")
         nc.sync.dma_start(t1_sb[:], t1)
 
 
@@ -100,7 +100,7 @@ def tile_picked_hyena2_none_po_kernel(
         w3_walk = w3_raw[:].rearrange("p j (m t) -> p m t j", t=PACK)
         for rows in (slice(0, 2), slice(2, 4)):
             nc.scalar.copy(w3_dealt[:, :, 0:2, rows], w3_walk[:, :, 0:2, rows])
-        nc.scalar.copy(w3_dealt[:, :, 2:4, :], w3_walk[:, :, 2:4, :])
+        nc.scalar.copy(w3_dealt[:, : P // 2, 2:4, :], w3_walk[:, : P // 2, 2:4, :])
         w2_scales_dealt = held([P, H], U8, "w2_scales_dealt")
         deal_scales(nc.vector, w_scale_rows[:, 2 * H : 3 * H], w2_scales_dealt[:])
         nc.sync.dma_start(t2_sb[:], t2)
@@ -121,14 +121,14 @@ def tile_picked_hyena2_none_po_kernel(
                 warm[:], lhsT=w3_code_pairs[0][:, 0:P].bitcast(FP8X4), lhsT_scale=w3_scales[:, 0:P],
                 rhs=w3_code_pairs[0][:].bitcast(FP8X4), rhs_scale=w3_scales[:, 0 : 2 * P], start=True, stop=True,
             )
+        nc.vector.tensor_copy(w3_dealt[:, P // 2 :, 2:4, :], w3_walk[:, P // 2 :, 2:4, :])
+        quantise_w3(1, "w3_codes_late")
         xq_words = held([P, S], U32, "xq_words")
         for u in range(2):
             nc.vector.tensor_copy(xq_words[:, u * HALF : (u + 1) * HALF], x_word_table[:].indirect(entries(offs_sb, u * HALF, HALF)))
-        quantise_w3(1, "x_word_table")
         w_dealt = held([P, 6 * H], U8, "w_dealt")
         w2_q = deal_words(nc.scalar.copy, w2_raw, w_dealt[:, 0 : 2 * H]), w2_scales_dealt[:]
         w1_q = deal_words(nc.scalar.copy, w1_raw, w_dealt[:, 2 * H : 4 * H]), late_scales[:, 0:H]
-        w4_q = deal_words(nc.vector.tensor_copy, w4_raw, w_dealt[:, 4 * H : 6 * H]), late_scales[:, H : 2 * H]
 
         def bank(number, shape):
             return psum.tile(shape, F32, name="bank%d" % number)
@@ -141,11 +141,15 @@ def tile_picked_hyena2_none_po_kernel(
             )
 
         val_window = [held([P, S], F32, "val_window%d" % t) for t in range(PACK)]
-        val_tap = [held([P, S], F32, "taps%d" % t) for t in range(PACK)]
+        halves = [slice(0, HALF), slice(HALF, S)]
         first_sums = held([P, PACK, HALF], F32, "first_sums")
         last_sum = first_sums[:, 2, :]
+        tap_tiles = [held([P, S], F32, "taps%d" % t) for t in range(PACK)]
+
+        def val_tap(t, half):
+            return last_sum if (t, half) == (2, halves[0]) else tap_tiles[t][:, half]
+
         h_window = [held([P, S], F32, "h_window%d" % t) for t in range(PACK)]
-        halves = [slice(0, HALF), slice(HALF, S)]
         val_banks = {}
         e_banks = {}
 
@@ -170,20 +174,24 @@ def tile_picked_hyena2_none_po_kernel(
 
         def first_tap(t):
             for half in halves:
-                if t == 0:
-                    nc.vector.tensor_copy(val_tap[t][:, half], val_window[t][:].indirect(entries(t1_sb, half.start, HALF)))
+                if (t, half) == (0, halves[0]):
+                    val_again = held([P, HALF], F32, "val_again")
+                    nc.gpsimd.tensor_copy(val_again[:], val_window[t][:, half])
+                    nc.vector.tensor_tensor(val_tap(t, half), val_window[t][:].indirect(entries(t1_sb, half.start, HALF)), val_again[:], ADD)
+                elif t == 0:
+                    nc.vector.tensor_copy(val_tap(t, half), val_window[t][:].indirect(entries(t1_sb, half.start, HALF)))
                 else:
-                    look_up(val_tap[t][:, half], val_window[t], t1_sb, half)
+                    look_up(val_tap(t, half), val_window[t], t1_sb, half)
 
         def val_sum(t, half):
-            return last_sum if (t, half) == (3, halves[1]) else val_tap[t][:, half]
+            return last_sum if (t, half) == (3, halves[1]) else val_tap(t, half)
 
         def first_add(t):
-            for half in halves:
+            for half in halves[1:] if t == 0 else halves:
                 if t == 0 or (t, half) == (3, halves[1]):
-                    nc.vector.tensor_tensor(val_sum(t, half), val_banks[t, half.start], val_tap[t][:, half], ADD)
+                    nc.vector.tensor_tensor(val_sum(t, half), val_banks[t, half.start], val_tap(t, half), ADD)
                 else:
-                    nc.gpsimd.tensor_tensor(val_tap[t][:, half], val_window[t][:, half], val_tap[t][:, half], ADD)
+                    nc.gpsimd.tensor_tensor(val_tap(t, half), val_window[t][:, half], val_tap(t, half), ADD)
 
         def first_gate(t, number):
             e_product(t, number)
@@ -191,10 +199,11 @@ def tile_picked_hyena2_none_po_kernel(
                 nc.vector.tensor_tensor(h_window[t][:, half], e_banks[t][:, half], val_sum(t, half), MULT)
 
         for u, half in enumerate(halves):
-            for t in (1, 0):
+            for t in ((0, 1), (1, 0))[u]:
                 val_product(t, half, 2 * u + t)
         first_tap(0)
         first_tap(1)
+        w4_q = deal_words(nc.vector.tensor_copy, w4_raw, w_dealt[:, 4 * H : 6 * H]), late_scales[:, H : 2 * H]
         for t in range(2, PACK):
             val_product(t, slice(0, S), t + 2)
             first_tap(t)
@@ -222,7 +231,7 @@ def tile_picked_hyena2_none_po_kernel(
 
         def second_gate(c):
             cols = slice(c * CHUNK, (c + 1) * CHUNK)
-            y_bank = bank((0, 2, 0, 2)[c], [P, PACK, CHUNK])
+            y_bank = bank((2, 6, 2, 6)[c], [P, PACK, CHUNK])
             for t in range(PACK):
                 fp4_product(y_bank[:, t, :], w1_q, t, xq_words[:, cols], xq_scales[:, cols])
             width = CHUNK
@@ -252,7 +261,7 @@ def tile_picked_hyena2_none_po_kernel(
                     nc.scalar.copy(rounded.rearrange("p (n t) -> p n t", t=PACK), out_bank[:].rearrange("p t n -> p n t"))
             else:
                 for pair, copy in enumerate((nc.scalar.copy, nc.vector.tensor_copy)):
-                    pair_bank = bank(6 + pair, [P, 2, CHUNK])
+                    pair_bank = bank(7 * pair, [P, 2, CHUNK])
                     for t in range(2):
                         fp4_product(pair_bank[:, t, :], w4_q, 2 * pair + t, z_codes[:, cols], z_scales[:, cols])
                     for first in range(0, CHUNK, CHUNK // 2):

@@ -172,23 +172,24 @@ def tile_picked_hyena2_none_po_kernel(
         def look_up(result, window, lst, cols):
             nc.scalar.activation(result, window[:].indirect(entries(lst, cols.start, cols.stop - cols.start)), COPY)
 
+        val_again = held([P, S], F32, "val_again")
+
         def first_tap(t):
             for half in halves:
-                if (t, half) == (0, halves[0]):
-                    val_again = held([P, HALF], F32, "val_again")
-                    nc.gpsimd.tensor_copy(val_again[:], val_window[t][:, half])
-                    nc.vector.tensor_tensor(val_tap(t, half), val_window[t][:].indirect(entries(t1_sb, half.start, HALF)), val_again[:], ADD)
-                elif t == 0:
-                    nc.vector.tensor_copy(val_tap(t, half), val_window[t][:].indirect(entries(t1_sb, half.start, HALF)))
+                if t == 0:
+                    nc.gpsimd.tensor_copy(val_again[:, half], val_window[t][:, half])
+                    nc.vector.tensor_tensor(val_tap(t, half), val_window[t][:].indirect(entries(t1_sb, half.start, HALF)), val_again[:, half], ADD)
                 else:
                     look_up(val_tap(t, half), val_window[t], t1_sb, half)
 
         def val_sum(t, half):
-            return last_sum if (t, half) == (3, halves[1]) else val_tap(t, half)
+            if t == 3:
+                return last_sum if half == halves[1] else val_tap(1, halves[1])
+            return val_tap(t, half)
 
         def first_add(t):
-            for half in halves[1:] if t == 0 else halves:
-                if t == 0 or (t, half) == (3, halves[1]):
+            for half in halves:
+                if t == 3:
                     nc.vector.tensor_tensor(val_sum(t, half), val_banks[t, half.start], val_tap(t, half), ADD)
                 else:
                     nc.gpsimd.tensor_tensor(val_tap(t, half), val_window[t][:, half], val_tap(t, half), ADD)
@@ -208,7 +209,8 @@ def tile_picked_hyena2_none_po_kernel(
             val_product(t, slice(0, S), t + 2)
             first_tap(t)
         for t, number in enumerate((6, 7, 1, 3)):
-            first_add(t)
+            if t > 0:
+                first_add(t)
             first_gate(t, number)
 
         out_rows = out_0.rearrange("(p t) n -> p t n", t=PACK)
@@ -231,7 +233,7 @@ def tile_picked_hyena2_none_po_kernel(
 
         def second_gate(c):
             cols = slice(c * CHUNK, (c + 1) * CHUNK)
-            y_bank = bank((2, 6, 2, 6)[c], [P, PACK, CHUNK])
+            y_bank = bank((6, 7, 6, 7)[c], [P, PACK, CHUNK])
             for t in range(PACK):
                 fp4_product(y_bank[:, t, :], w1_q, t, xq_words[:, cols], xq_scales[:, cols])
             width = CHUNK
@@ -261,7 +263,7 @@ def tile_picked_hyena2_none_po_kernel(
                     nc.scalar.copy(rounded.rearrange("p (n t) -> p n t", t=PACK), out_bank[:].rearrange("p t n -> p n t"))
             else:
                 for pair, copy in enumerate((nc.scalar.copy, nc.vector.tensor_copy)):
-                    pair_bank = bank(7 * pair, [P, 2, CHUNK])
+                    pair_bank = bank(2 * pair, [P, 2, CHUNK])
                     for t in range(2):
                         fp4_product(pair_bank[:, t, :], w4_q, 2 * pair + t, z_codes[:, cols], z_scales[:, cols])
                     for first in range(0, CHUNK, CHUNK // 2):

@@ -147,6 +147,8 @@ def tile_picked_hyena2_none_po_kernel(
         tap_tiles = [held([P, S], F32, "taps%d" % t) for t in range(PACK)]
 
         def val_tap(t, half):
+            if (t, half) == (1, halves[1]):
+                return first_sums[:, 1, :]
             return last_sum if (t, half) == (2, halves[0]) else tap_tiles[t][:, half]
 
         h_window = [held([P, S], F32, "h_window%d" % t) for t in range(PACK)]
@@ -194,10 +196,8 @@ def tile_picked_hyena2_none_po_kernel(
                 else:
                     nc.gpsimd.tensor_tensor(val_tap(t, half), val_window[t][:, half], val_tap(t, half), ADD)
 
-        def first_gate(t, number):
-            e_product(t, number)
-            for half in halves:
-                nc.vector.tensor_tensor(h_window[t][:, half], e_banks[t][:, half], val_sum(t, half), MULT)
+        def first_gate(t, half):
+            nc.vector.tensor_tensor(h_window[t][:, half], e_banks[t][:, half], val_sum(t, half), MULT)
 
         for u, half in enumerate(halves):
             for t in ((0, 1), (1, 0))[u]:
@@ -211,7 +211,10 @@ def tile_picked_hyena2_none_po_kernel(
         for t, number in enumerate((6, 7, 1, 3)):
             if t > 0:
                 first_add(t)
-            first_gate(t, number)
+            e_product(t, number)
+            for half in halves[:1] if t == 2 else halves:
+                first_gate(t, half)
+        first_gate(2, halves[1])
 
         out_rows = out_0.rearrange("(p t) n -> p t n", t=PACK)
         out_words = out_1[0].rearrange("p c r -> p (c r)").bitcast(I32)
@@ -276,12 +279,15 @@ def tile_picked_hyena2_none_po_kernel(
             look_up(h_sum(t, cols), h_window[t], t2_sb, cols)
             second_add(nc.gpsimd, t, cols)
 
-        for t in EARLY_TILES:
-            early_tap(t, halves[0])
-        for t, name in zip(LATE_TILES, ("staged", "later_sums")):
-            staged = held([P, CHUNK], F32, name)
-            look_up(staged[:], h_window[t], t2_sb, chunks[0])
-            nc.vector.tensor_tensor(h_sum(t, chunks[0]), staged[:], h_window[t][:, chunks[0]], ADD)
+        early_tap(0, halves[0])
+        half_staged = held([P, HALF], F32, "half_staged")
+        look_up(half_staged[:], h_window[1], t2_sb, halves[0])
+        staged = [held([P, CHUNK], F32, name) for name in ("staged", "later_sums")]
+        look_up(staged[0][:], h_window[2], t2_sb, chunks[0])
+        nc.vector.tensor_copy(staged[1][:], h_window[3][:].indirect(entries(t2_sb, 0, CHUNK)))
+        nc.vector.tensor_tensor(h_sum(1, halves[0]), half_staged[:], h_window[1][:, halves[0]], ADD)
+        for t in LATE_TILES:
+            nc.vector.tensor_tensor(h_sum(t, chunks[0]), staged[t - 2][:], h_window[t][:, chunks[0]], ADD)
         h_sums.append(held([P, PACK, HALF], F32, "later_sums"))
         for c, cols in enumerate(chunks):
             if c >= 2:

@@ -174,13 +174,15 @@ def tile_picked_hyena2_none_po_kernel(
         def look_up(result, window, lst, cols):
             nc.scalar.activation(result, window[:].indirect(entries(lst, cols.start, cols.stop - cols.start)), COPY)
 
-        val_again = held([P, S], F32, "val_again")
+        val_again = held([P, HALF], F32, "val_again")
 
         def first_tap(t):
             for half in halves:
-                if t == 0:
-                    nc.gpsimd.tensor_copy(val_again[:, half], val_window[t][:, half])
-                    nc.vector.tensor_tensor(val_tap(t, half), val_window[t][:].indirect(entries(t1_sb, half.start, HALF)), val_again[:, half], ADD)
+                if (t, half) == (0, halves[0]):
+                    nc.gpsimd.tensor_copy(val_again[:], val_window[t][:, half])
+                    nc.vector.tensor_tensor(val_tap(t, half), val_window[t][:].indirect(entries(t1_sb, half.start, HALF)), val_again[:], ADD)
+                elif t == 0:
+                    nc.vector.tensor_copy(val_tap(t, half), val_window[t][:].indirect(entries(t1_sb, half.start, HALF)))
                 else:
                     look_up(val_tap(t, half), val_window[t], t1_sb, half)
 
@@ -190,8 +192,8 @@ def tile_picked_hyena2_none_po_kernel(
             return val_tap(t, half)
 
         def first_add(t):
-            for half in halves:
-                if t == 3:
+            for half in halves[1:] if t == 0 else halves:
+                if t in (0, 3):
                     nc.vector.tensor_tensor(val_sum(t, half), val_banks[t, half.start], val_tap(t, half), ADD)
                 else:
                     nc.gpsimd.tensor_tensor(val_tap(t, half), val_window[t][:, half], val_tap(t, half), ADD)
@@ -209,8 +211,7 @@ def tile_picked_hyena2_none_po_kernel(
             val_product(t, slice(0, S), t + 2)
             first_tap(t)
         for t, number in enumerate((6, 7, 1, 3)):
-            if t > 0:
-                first_add(t)
+            first_add(t)
             e_product(t, number)
             for half in halves[:1] if t == 2 else halves:
                 first_gate(t, half)

@@ -22,12 +22,12 @@ PACK = 4
 HALF = S // 2
 CHUNK = 128
 CHUNKS = S // CHUNK
-EARLY_TILES = (0, 1)
-LATE_TILES = (2, 3)
+PIECE = 64
+WARM_UP_PASSES = 4
 
 
-def entries(lst, first, count):
-    return lst[:, first // 16 : (first + count) // 16]
+def entries(lst, cols):
+    return lst[:, cols.start // 16 : cols.stop // 16]
 
 
 def tile_picked_hyena2_none_po_kernel(
@@ -42,12 +42,19 @@ def tile_picked_hyena2_none_po_kernel(
         def held(shape, dtype, name):
             return keep.tile(shape, dtype, name=name, align_bytes=64)
 
+        def bank(number, shape):
+            return psum.tile(shape, F32, name="bank%d" % number)
+
+        whole = slice(0, S)
+        halves = [slice(0, HALF), slice(HALF, S)]
+        chunks = [slice(c * CHUNK, (c + 1) * CHUNK) for c in range(CHUNKS)]
+
         offs_sb = held([P, S // 16], U16, "offs_sb")
         t1_sb = held([P, S // 16], U16, "t1_sb")
         t2_sb = held([P, S // 16], U16, "t2_sb")
 
         def load_words(words, name):
-            raw_words = held([P, 2 * H], U8, name + "_raw_words")
+            raw_words = held([P, 2 * H], U8, name)
             nc.sync.dma_start(raw_words[:].bitcast(I32), words[0].bitcast(I32))
             return raw_words
 
@@ -67,8 +74,9 @@ def tile_picked_hyena2_none_po_kernel(
         nc.sync.dma_start(w_scale_rows[0:16, 2 * H : 3 * H].bitcast(I32), w2_scales[0].bitcast(I32))
         x_word_table = held([P, T], U32, "x_word_table")
         nc.sync.dma_start(x_word_table[:].bitcast(I32), x_words[0].rearrange("p c r -> p (c r)").bitcast(I32))
-        w2_raw = load_words(w2_words, "w2")
-        w1_raw = load_words(w1_words, "w1")
+        w2_raw = load_words(w2_words, "w2_raw")
+        w1_raw = load_words(w1_words, "w1_raw")
+        w4_raw = load_words(w4_words, "w4_raw")
 
         def deal_words(copy, raw_words, words):
             copy(
@@ -83,9 +91,7 @@ def tile_picked_hyena2_none_po_kernel(
         nc.vector.tensor_copy(xq_scales[:].bitcast(I32), x_scale_picked[:].bitcast(I32))
         for j in range(1, 4):
             nc.sync.dma_start(xq_scales[j:P:32, :].bitcast(I32), x_scale_picked[8 * j : P : 32, :].bitcast(I32))
-        w4_raw = load_words(w4_words, "w4")
         nc.sync.dma_start(t1_sb[:], t1)
-
 
         def deal_scales(engine, rows, dealt):
             engine.tensor_copy(
@@ -93,7 +99,6 @@ def tile_picked_hyena2_none_po_kernel(
             )
             for q in range(1, 4):
                 nc.sync.dma_start(dealt[32 * q : 32 * q + 4, :].bitcast(I32), dealt[4 * q : 4 * q + 4, :].bitcast(I32))
-
 
         w3_bf = held([P, PACK * P * PACK], BF16, "w3_bf")
         w3_dealt = w3_bf[:].rearrange("p (t m j) -> p m t j", t=PACK, j=PACK)
@@ -115,8 +120,8 @@ def tile_picked_hyena2_none_po_kernel(
             w3_code_pairs.append(codes)
 
         quantise_w3(0, "w3_codes")
-        warm = psum.tile([P, HALF], F32, name="bank7")
-        for repeat in range(4):
+        warm = bank(7, [P, HALF])
+        for repeat in range(WARM_UP_PASSES):
             nc.tensor.matmul_mx(
                 warm[:], lhsT=w3_code_pairs[0][:, 0:P].bitcast(FP8X4), lhsT_scale=w3_scales[:, 0:P],
                 rhs=w3_code_pairs[0][:].bitcast(FP8X4), rhs_scale=w3_scales[:, 0 : 2 * P], start=True, stop=True,
@@ -124,14 +129,13 @@ def tile_picked_hyena2_none_po_kernel(
         nc.vector.tensor_copy(w3_dealt[:, P // 2 :, 2:4, :], w3_walk[:, P // 2 :, 2:4, :])
         quantise_w3(1, "w3_codes_late")
         xq_words = held([P, S], U32, "xq_words")
-        for u in range(2):
-            nc.vector.tensor_copy(xq_words[:, u * HALF : (u + 1) * HALF], x_word_table[:].indirect(entries(offs_sb, u * HALF, HALF)))
-        w_dealt = held([P, 6 * H], U8, "w_dealt")
+        for half in halves:
+            nc.vector.tensor_copy(xq_words[:, half], x_word_table[:].indirect(entries(offs_sb, half)))
+        w_dealt = held([P, 4 * H], U8, "w_dealt")
+        w4_dealt = held([P, 2 * H], U8, "x_word_table")
         w2_q = deal_words(nc.scalar.copy, w2_raw, w_dealt[:, 0 : 2 * H]), w2_scales_dealt[:]
         w1_q = deal_words(nc.scalar.copy, w1_raw, w_dealt[:, 2 * H : 4 * H]), late_scales[:, 0:H]
-
-        def bank(number, shape):
-            return psum.tile(shape, F32, name="bank%d" % number)
+        w4_q = deal_words(nc.vector.tensor_copy, w4_raw, w4_dealt[:]), late_scales[:, H : 2 * H]
 
         def fp4_product(result, weights, t, codes, scales):
             words, word_scales = weights
@@ -140,193 +144,171 @@ def tile_picked_hyena2_none_po_kernel(
                 rhs=codes.bitcast(FP8X4), rhs_scale=scales, start=True, stop=True,
             )
 
+        def scalar_look_up(result, window, lst, cols):
+            nc.scalar.activation(result, window[:].indirect(entries(lst, cols)), COPY)
+
         val_window = [held([P, S], F32, "val_window%d" % t) for t in range(PACK)]
-        halves = [slice(0, HALF), slice(HALF, S)]
-        first_sums = held([P, PACK, HALF], F32, "first_sums")
-        last_sum = first_sums[:, 2, :]
-        tap_tiles = [held([P, S], F32, "taps%d" % t) for t in range(PACK)]
-
-        def val_tap(t, half):
-            if (t, half) == (1, halves[1]):
-                return first_sums[:, 1, :]
-            return last_sum if (t, half) == (2, halves[0]) else tap_tiles[t][:, half]
-
         h_window = [held([P, S], F32, "h_window%d" % t) for t in range(PACK)]
-        val_banks = {}
-        e_banks = {}
 
-        def val_product(t, cols, number):
+        def val_product(t, cols, number, copy):
             val_bank = bank(number, [P, cols.stop - cols.start])
             nc.tensor.matmul_mx(
                 val_bank[:], lhsT=w3_code_pairs[t // 2][:, P * (t % 2) : P * (t % 2 + 1)].bitcast(FP8X4), lhsT_scale=w3_scales[:, P * t : P * (t + 1)],
                 rhs=xq_words[:, cols].bitcast(FP8X4), rhs_scale=xq_scales[:, cols], start=True, stop=True,
             )
-            for half in halves:
-                if cols.start <= half.start and half.stop <= cols.stop:
-                    val_banks[t, half.start] = val_bank[:, half.start - cols.start : half.stop - cols.start]
-            copy = nc.scalar.copy if t == 1 else nc.vector.tensor_copy
             copy(val_window[t][:, cols], val_bank[:])
+            return val_bank
 
-        def e_product(t, number):
-            e_banks[t] = bank(number, [P, S])
+        val_product(1, halves[0], 1, nc.scalar.copy)
+        val0_banks = [val_product(0, halves[0], 0, nc.vector.tensor_copy)]
+        val_product(1, halves[1], 4, nc.scalar.copy)
+        val0_banks.append(val_product(0, halves[1], 3, nc.vector.tensor_copy))
+        val_product(2, halves[0], 2, nc.scalar.copy)
+        val_product(2, halves[1], 5, nc.vector.tensor_copy)
+
+        taps0 = held([P, S], F32, "taps0")
+        taps1 = held([P, S], F32, "taps1")
+        late_taps = held([P, 2, S], F32, "late_taps")
+        for half in halves:
+            nc.vector.tensor_copy(taps0[:, half], val_window[0][:].indirect(entries(t1_sb, half)))
+        for half in halves:
+            scalar_look_up(taps1[:, half], val_window[1], t1_sb, half)
+        val3_bank = val_product(3, whole, 6, nc.vector.tensor_copy)
+        for t in (2, 3):
+            for half in halves:
+                scalar_look_up(late_taps[:, t - 2, half], val_window[t], t1_sb, half)
+
+        e_banks = []
+        for t, number in enumerate((7, 1, 2, 4)):
+            e_banks.append(bank(number, [P, S]))
             fp4_product(e_banks[t][:], w2_q, t, xq_words[:], xq_scales[:])
 
-        def look_up(result, window, lst, cols):
-            nc.scalar.activation(result, window[:].indirect(entries(lst, cols.start, cols.stop - cols.start)), COPY)
+        def first_gate(t, sums, cols):
+            nc.vector.tensor_tensor(h_window[t][:, cols], e_banks[t][:, cols], sums, MULT)
 
-        val_again = held([P, HALF], F32, "val_again")
-
-        def first_tap(t):
-            for half in halves:
-                if (t, half) == (0, halves[0]):
-                    nc.gpsimd.tensor_copy(val_again[:], val_window[t][:, half])
-                    nc.vector.tensor_tensor(val_tap(t, half), val_window[t][:].indirect(entries(t1_sb, half.start, HALF)), val_again[:], ADD)
-                elif t == 0:
-                    nc.vector.tensor_copy(val_tap(t, half), val_window[t][:].indirect(entries(t1_sb, half.start, HALF)))
-                else:
-                    look_up(val_tap(t, half), val_window[t], t1_sb, half)
-
-        def val_sum(t, half):
-            if t == 3:
-                return last_sum if half == halves[1] else val_tap(1, halves[1])
-            return val_tap(t, half)
-
-        def first_add(t):
-            for half in halves[1:] if t == 0 else halves:
-                if t in (0, 3):
-                    nc.vector.tensor_tensor(val_sum(t, half), val_banks[t, half.start], val_tap(t, half), ADD)
-                else:
-                    nc.gpsimd.tensor_tensor(val_tap(t, half), val_window[t][:, half], val_tap(t, half), ADD)
-
-        def first_gate(t, half):
-            nc.vector.tensor_tensor(h_window[t][:, half], e_banks[t][:, half], val_sum(t, half), MULT)
-
+        sums1 = held([P, S], F32, "val_window0")
+        nc.gpsimd.tensor_tensor(sums1[:], val_window[1][:], taps1[:], ADD)
+        nc.gpsimd.tensor_tensor(late_taps[:, 0, :], val_window[2][:], late_taps[:, 0, :], ADD)
         for u, half in enumerate(halves):
-            for t in ((0, 1), (1, 0))[u]:
-                val_product(t, half, 2 * u + t)
-        first_tap(0)
-        first_tap(1)
-        w4_q = deal_words(nc.vector.tensor_copy, w4_raw, w_dealt[:, 4 * H : 6 * H]), late_scales[:, H : 2 * H]
-        for t in range(2, PACK):
-            val_product(t, slice(0, S), t + 2)
-            first_tap(t)
-        for t, number in enumerate((6, 7, 1, 3)):
-            first_add(t)
-            e_product(t, number)
-            for half in halves[:1] if t == 2 else halves:
-                first_gate(t, half)
-        first_gate(2, halves[1])
+            nc.vector.tensor_tensor(taps0[:, half], val0_banks[u][:], taps0[:, half], ADD)
+        for half in halves:
+            first_gate(0, taps0[:, half], half)
+        first_gate(1, sums1[:], whole)
+        sums3 = held([P, S], F32, "taps0")
+        for half in halves:
+            nc.vector.tensor_tensor(sums3[:, half], val3_bank[:, half], late_taps[:, 1, half], ADD)
+        first_gate(2, late_taps[:, 0, :], whole)
+        first_gate(3, sums3[:], whole)
 
         out_rows = out_0.rearrange("(p t) n -> p t n", t=PACK)
         out_words = out_1[0].rearrange("p c r -> p (c r)").bitcast(I32)
-        h_sums = [first_sums]
+        sum_area = held([P, 18 * CHUNK], F32, "sum_slots")
 
-        def h_sum(tiles, cols):
-            first = cols.start % HALF
-            return h_sums[cols.start // HALF][:, tiles, first : first + cols.stop - cols.start]
+        def slots(first):
+            return sum_area[:, first * CHUNK : (first + 3 * PACK) * CHUNK].rearrange("p (t n) -> p t n", t=PACK)[:, :, :HALF]
 
-        z_bf = {}
+        first_sums = slots(6)
+        later_sums = slots(0)
+        staged = sum_area[:, :HALF]
+        for t in range(3):
+            scalar_look_up(first_sums[:, t, :], h_window[t], t2_sb, halves[0])
+        scalar_look_up(staged[:, chunks[1]], h_window[3], t2_sb, chunks[1])
+        nc.gpsimd.tensor_tensor(first_sums[:, 0, :], first_sums[:, 0, :], h_window[0][:, halves[0]], ADD)
+        nc.vector.tensor_tensor(first_sums[:, 1, :], first_sums[:, 1, :], h_window[1][:, halves[0]], ADD)
+        nc.vector.tensor_copy(staged[:, chunks[0]], h_window[3][:].indirect(entries(t2_sb, chunks[0])))
+        nc.vector.tensor_tensor(first_sums[:, 2, :], first_sums[:, 2, :], h_window[2][:, halves[0]], ADD)
+        for c in range(2):
+            nc.vector.tensor_tensor(first_sums[:, 3, chunks[c]], staged[:, chunks[c]], h_window[3][:, chunks[c]], ADD)
+
+        later_taps = held([P, PACK, HALF], F32, "taps0")
+        for t in range(2):
+            scalar_look_up(later_taps[:, t, :], h_window[t], t2_sb, halves[1])
+        for c in (2, 3):
+            for t in (2, 3):
+                scalar_look_up(later_taps[:, t, chunks[c - 2]], h_window[t], t2_sb, chunks[c])
+
+        z_tiles = [sum_area[:, first * CHUNK : (first + 2) * CHUNK].bitcast(BF16) for first in (2, 4)]
+        z_tiles = z_tiles + [held([P, PACK * CHUNK], BF16, "z_bf%d" % c)[:] for c in (2, 3)]
         z_codes = held([P, S], U32, "z_codes")
         z_scales = held([P, S], U8, "z_scales")
         out_f32 = [held([P, PACK, CHUNK], F32, "out_f32%d" % c) for c in range(CHUNKS)]
-        early_bf = {0: held([P, CHUNK * PACK], BF16, "out_bf0")}
-        late_bf = held([P, HALF * PACK], BF16, "late_bf")
-
-        def second_add(engine, t, cols):
-            engine.tensor_tensor(h_sum(t, cols), h_sum(t, cols), h_window[t][:, cols], ADD)
 
         def second_gate(c):
-            cols = slice(c * CHUNK, (c + 1) * CHUNK)
-            y_bank = bank((6, 7, 6, 7)[c], [P, PACK, CHUNK])
+            y_bank = bank((5, 0)[c % 2], [P, PACK, CHUNK])
             for t in range(PACK):
-                fp4_product(y_bank[:, t, :], w1_q, t, xq_words[:, cols], xq_scales[:, cols])
-            width = CHUNK
-            for first in range(cols.start, cols.stop, width):
-                z_bf[first] = held([P, PACK * width], BF16, "z_bf%d" % first)
-                nc.vector.tensor_tensor(
-                    z_bf[first][:].rearrange("p (n i t) -> p n t i", i=2, t=PACK),
-                    y_bank[:, :, first - cols.start : first - cols.start + width].rearrange("p t (n i) -> p n t i", i=2),
-                    h_sum(slice(0, PACK), slice(first, first + width)).rearrange("p t (n i) -> p n t i", i=2),
-                    MULT,
-                )
+                fp4_product(y_bank[:, t, :], w1_q, t, xq_words[:, chunks[c]], xq_scales[:, chunks[c]])
+            sums = (first_sums, later_sums)[c // 2][:, :, chunks[c % 2]]
+            nc.vector.tensor_tensor(
+                z_tiles[c].rearrange("p (n i t) -> p n t i", i=2, t=PACK),
+                y_bank[:].rearrange("p t (n i) -> p n t i", i=2),
+                sums.rearrange("p t (n i) -> p n t i", i=2),
+                MULT,
+            )
 
-        def quantise_z(first, count):
-            cols = slice(first, first + count)
-            nc.vector.quantize_mx(z_codes[:, cols].bitcast(FP8X4), z_scales[:, cols], z_bf[first][:])
+        def quantise_z(c):
+            nc.vector.quantize_mx(z_codes[:, chunks[c]].bitcast(FP8X4), z_scales[:, chunks[c]], z_tiles[c])
 
-        def last_layer(c):
-            cols = slice(c * CHUNK, (c + 1) * CHUNK)
-            if c + 1 < CHUNKS:
-                out_bank = bank((4, 1, 5)[c], [P, PACK, CHUNK])
-                for t in range(PACK):
-                    fp4_product(out_bank[:, t, :], w4_q, t, z_codes[:, cols], z_scales[:, cols])
-                nc.scalar.copy(out_f32[c][:], out_bank[:])
-                nc.sync.dma_start(out_rows[:, :, cols], out_f32[c][:])
-                if c != 1:
-                    rounded = early_bf[0][:] if c == 0 else late_bf[:, : PACK * CHUNK]
-                    nc.scalar.copy(rounded.rearrange("p (n t) -> p n t", t=PACK), out_bank[:].rearrange("p t n -> p n t"))
-            else:
-                for pair, copy in enumerate((nc.scalar.copy, nc.vector.tensor_copy)):
-                    pair_bank = bank(2 * pair, [P, 2, CHUNK])
-                    for t in range(2):
-                        fp4_product(pair_bank[:, t, :], w4_q, 2 * pair + t, z_codes[:, cols], z_scales[:, cols])
-                    for first in range(0, CHUNK, CHUNK // 2):
-                        half = slice(first, first + CHUNK // 2)
-                        copy(out_f32[c][:, 2 * pair : 2 * pair + 2, half], pair_bank[:, :, half])
-                nc.sync.dma_start(out_rows[:, :, cols], out_f32[c][:])
+        def last_layer(c, number):
+            out_bank = bank(number, [P, PACK, CHUNK])
+            for t in range(PACK):
+                fp4_product(out_bank[:, t, :], w4_q, t, z_codes[:, chunks[c]], z_scales[:, chunks[c]])
+            nc.scalar.copy(out_f32[c][:], out_bank[:])
+            nc.sync.dma_start(out_rows[:, :, chunks[c]], out_f32[c][:])
+            return out_bank
 
-        chunks = [slice(c * CHUNK, (c + 1) * CHUNK) for c in range(CHUNKS)]
-        def early_tap(t, cols):
-            look_up(h_sum(t, cols), h_window[t], t2_sb, cols)
-            second_add(nc.gpsimd, t, cols)
+        def round_bank(rounded, out_bank):
+            nc.scalar.copy(rounded.rearrange("p (n t) -> p n t", t=PACK), out_bank[:].rearrange("p t n -> p n t"))
 
-        early_tap(0, halves[0])
-        half_staged = held([P, HALF], F32, "half_staged")
-        look_up(half_staged[:], h_window[1], t2_sb, halves[0])
-        staged = [held([P, CHUNK], F32, name) for name in ("staged", "later_sums")]
-        look_up(staged[0][:], h_window[2], t2_sb, chunks[0])
-        nc.vector.tensor_copy(staged[1][:], h_window[3][:].indirect(entries(t2_sb, 0, CHUNK)))
-        nc.vector.tensor_tensor(h_sum(1, halves[0]), half_staged[:], h_window[1][:, halves[0]], ADD)
-        for t in LATE_TILES:
-            nc.vector.tensor_tensor(h_sum(t, chunks[0]), staged[t - 2][:], h_window[t][:, chunks[0]], ADD)
-        h_sums.append(held([P, PACK, HALF], F32, "later_sums"))
-        for c, cols in enumerate(chunks):
-            if c >= 2:
-                for t in EARLY_TILES:
-                    look_up(h_sum(t, cols), h_window[t], t2_sb, cols)
-            if c >= 1:
-                for t in LATE_TILES:
-                    look_up(h_sum(t, cols), h_window[t], t2_sb, cols)
-        for c, cols in enumerate(chunks):
-            if c > 0:
-                for t in LATE_TILES if c < 2 else range(PACK):
-                    second_add(nc.vector, t, cols)
-                quantise_z((c - 1) * CHUNK, CHUNK)
-                last_layer(c - 1)
-            second_gate(c)
-        quantise_z(S - CHUNK, CHUNK)
-        out_scales = held([P, S], U8, "later_sums")
-        early_bf[1] = held([P, CHUNK * PACK], BF16, "z_bf%d" % (S - CHUNK))
-        nc.vector.tensor_copy(
-            early_bf[1][:].rearrange("p (n i t) -> p n t i", i=4, t=PACK), out_f32[1][:].rearrange("p t (n i) -> p n t i", i=4)
-        )
+        def round_stored(rounded, stored):
+            nc.vector.tensor_copy(rounded.rearrange("p (n i t) -> p n t i", i=4, t=PACK), stored.rearrange("p t (n i) -> p n t i", i=4))
+
+        def later_add(engine, t, cols, taps):
+            engine.tensor_tensor(later_sums[:, t, cols.start - HALF : cols.stop - HALF], taps, h_window[t][:, cols], ADD)
+
+        second_gate(0)
+        second_gate(1)
+        later_add(nc.gpsimd, 0, halves[1], later_taps[:, 0, :])
+        quantise_z(0)
+        first_bf = held([P, PACK * CHUNK], BF16, "first_bf")
+        round_bank(first_bf[:], last_layer(0, 7))
+        for t in (2, 1, 3):
+            later_add(nc.vector, t, chunks[2], later_taps[:, t, chunks[0]])
+        quantise_z(1)
+        last_layer(1, 1)
+        second_gate(2)
+        later_add(nc.gpsimd, 1, chunks[3], later_taps[:, 1, chunks[1]])
+        for t in (2, 3):
+            later_add(nc.vector, t, chunks[3], later_taps[:, t, chunks[1]])
+        quantise_z(2)
+        late_bf = held([P, PACK * HALF], BF16, "late_bf")
+        round_bank(late_bf[:, : PACK * CHUNK], last_layer(2, 2))
+        second_gate(3)
+        out_scales = held([P, S], U8, "sum_slots")
         early_codes = held([P, HALF], U32, "early_codes")
-        for c in range(2):
-            nc.vector.quantize_mx(early_codes[:, chunks[c]].bitcast(FP8X4), out_scales[:, chunks[c]], early_bf[c][:])
+        nc.vector.quantize_mx(early_codes[:, chunks[0]].bitcast(FP8X4), out_scales[:, chunks[0]], first_bf[:])
+        quantise_z(3)
+        second_bf = held([P, PACK * CHUNK], BF16, "z_bf3")
+        round_stored(second_bf[:], out_f32[1][:])
+        nc.vector.quantize_mx(early_codes[:, chunks[1]].bitcast(FP8X4), out_scales[:, chunks[1]], second_bf[:])
         nc.sync.dma_start(out_words[:, halves[0]], early_codes[:].bitcast(I32))
-        last_layer(CHUNKS - 1)
+
+        last = chunks[3]
+        for pair, copy in enumerate((nc.scalar.copy, nc.vector.tensor_copy)):
+            pair_bank = bank((4, 6)[pair], [P, 2, CHUNK])
+            for t in range(2):
+                fp4_product(pair_bank[:, t, :], w4_q, 2 * pair + t, z_codes[:, last], z_scales[:, last])
+            for first in range(0, CHUNK, PIECE):
+                copy(out_f32[3][:, 2 * pair : 2 * pair + 2, first : first + PIECE], pair_bank[:, :, first : first + PIECE])
+        nc.sync.dma_start(out_rows[:, :, last], out_f32[3][:])
         late_codes = held([P, HALF], U32, "late_codes")
         nc.vector.quantize_mx(late_codes[:, :CHUNK].bitcast(FP8X4), out_scales[:, chunks[2]], late_bf[:, : PACK * CHUNK])
-        for first in range(0, CHUNK, CHUNK // 2):
-            nc.vector.tensor_copy(
-                late_bf[:, PACK * (CHUNK + first) : PACK * (CHUNK + first + CHUNK // 2)].rearrange("p (n i t) -> p n t i", i=4, t=PACK),
-                out_f32[CHUNKS - 1][:, :, first : first + CHUNK // 2].rearrange("p t (n i) -> p n t i", i=4),
-            )
-        for first in range(CHUNK, HALF, CHUNK // 2):
+        for first in range(0, CHUNK, PIECE):
+            round_stored(late_bf[:, PACK * (CHUNK + first) : PACK * (CHUNK + first + PIECE)], out_f32[3][:, :, first : first + PIECE])
+        for first in range(CHUNK, HALF, PIECE):
             nc.vector.quantize_mx(
-                late_codes[:, first : first + CHUNK // 2].bitcast(FP8X4),
-                out_scales[:, HALF + first : HALF + first + CHUNK // 2],
-                late_bf[:, PACK * first : PACK * (first + CHUNK // 2)],
+                late_codes[:, first : first + PIECE].bitcast(FP8X4),
+                out_scales[:, HALF + first : HALF + first + PIECE],
+                late_bf[:, PACK * first : PACK * (first + PIECE)],
             )
         nc.sync.dma_start(out_words[:, halves[1]], late_codes[:].bitcast(I32))
         for q in range(4):

@@ -68,10 +68,10 @@ def tile_picked_hyena2_none_po_kernel(
         nc.sync.dma_start(w3_raw[:, 0:2, :], w3_rows[:, 0:2, :])
         nc.sync.dma_start(offs_sb[:], offs)
         nc.sync.dma_start(x_scale_table[0:P:8, :].bitcast(I32), x_scales[0].bitcast(I32))
-        for i, scales in enumerate((w1_scales, w4_scales)):
+        for i, scales in enumerate((w2_scales, w1_scales)):
             nc.sync.dma_start(w_scale_rows[0:16, i * H : (i + 1) * H].bitcast(I32), scales[0].bitcast(I32))
         nc.sync.dma_start(w3_raw[:, 2:4, :], w3_rows[:, 2:4, :])
-        nc.sync.dma_start(w_scale_rows[0:16, 2 * H : 3 * H].bitcast(I32), w2_scales[0].bitcast(I32))
+        nc.sync.dma_start(w_scale_rows[0:16, 2 * H : 3 * H].bitcast(I32), w4_scales[0].bitcast(I32))
         x_word_table = held([P, T], U32, "x_word_table")
         nc.sync.dma_start(x_word_table[:].bitcast(I32), x_words[0].rearrange("p c r -> p (c r)").bitcast(I32))
         w2_raw = load_words(w2_words, "w2_raw")
@@ -94,9 +94,9 @@ def tile_picked_hyena2_none_po_kernel(
         nc.sync.dma_start(t1_sb[:], t1)
 
         def deal_scales(engine, rows, dealt):
-            engine.tensor_copy(
-                dealt.rearrange("p (i t m) -> p t i m", t=PACK, m=P), rows.rearrange("p (i m t) -> p t i m", t=PACK, m=P)
-            )
+            engine.tensor_copy(dealt.rearrange("p (t m) -> p t m", t=PACK), rows.rearrange("p (m t) -> p t m", t=PACK))
+
+        def place_scales(dealt):
             for q in range(1, 4):
                 nc.sync.dma_start(dealt[32 * q : 32 * q + 4, :].bitcast(I32), dealt[4 * q : 4 * q + 4, :].bitcast(I32))
 
@@ -106,11 +106,6 @@ def tile_picked_hyena2_none_po_kernel(
         for rows in (slice(0, 2), slice(2, 4)):
             nc.scalar.copy(w3_dealt[:, :, 0:2, rows], w3_walk[:, :, 0:2, rows])
         nc.scalar.copy(w3_dealt[:, : P // 2, 2:4, :], w3_walk[:, : P // 2, 2:4, :])
-        w2_scales_dealt = held([P, H], U8, "w2_scales_dealt")
-        deal_scales(nc.vector, w_scale_rows[:, 2 * H : 3 * H], w2_scales_dealt[:])
-        nc.sync.dma_start(t2_sb[:], t2)
-        late_scales = held([P, 2 * H], U8, "late_scales")
-        deal_scales(nc.gpsimd, w_scale_rows[:, 0 : 2 * H], late_scales[:])
         w3_scales = held([P, H], U8, "w3_scales")
         w3_code_pairs = []
 
@@ -128,14 +123,23 @@ def tile_picked_hyena2_none_po_kernel(
             )
         nc.vector.tensor_copy(w3_dealt[:, P // 2 :, 2:4, :], w3_walk[:, P // 2 :, 2:4, :])
         quantise_w3(1, "w3_codes_late")
+        gate_scales = held([P, 2 * H], U8, "gate_scales")
+        for i in range(2):
+            deal_scales(nc.vector, w_scale_rows[:, i * H : (i + 1) * H], gate_scales[:, i * H : (i + 1) * H])
+        place_scales(gate_scales[:])
+        nc.sync.dma_start(t2_sb[:], t2)
         xq_words = held([P, S], U32, "xq_words")
         for half in halves:
             nc.vector.tensor_copy(xq_words[:, half], x_word_table[:].indirect(entries(offs_sb, half)))
         w_dealt = held([P, 4 * H], U8, "w_dealt")
         w4_dealt = held([P, 2 * H], U8, "x_word_table")
-        w2_q = deal_words(nc.scalar.copy, w2_raw, w_dealt[:, 0 : 2 * H]), w2_scales_dealt[:]
-        w1_q = deal_words(nc.scalar.copy, w1_raw, w_dealt[:, 2 * H : 4 * H]), late_scales[:, 0:H]
-        w4_q = deal_words(nc.vector.tensor_copy, w4_raw, w4_dealt[:]), late_scales[:, H : 2 * H]
+        w2_q = deal_words(nc.scalar.copy, w2_raw, w_dealt[:, 0 : 2 * H]), gate_scales[:, 0:H]
+        w1_q = deal_words(nc.scalar.copy, w1_raw, w_dealt[:, 2 * H : 4 * H]), gate_scales[:, H : 2 * H]
+        deal_words(nc.vector.tensor_copy, w4_raw, w4_dealt[:])
+        w4_scales_dealt = held([P, H], U8, "w4_raw")
+        deal_scales(nc.gpsimd, w_scale_rows[:, 2 * H : 3 * H], w4_scales_dealt[:])
+        place_scales(w4_scales_dealt[:])
+        w4_q = w4_dealt[:], w4_scales_dealt[:]
 
         def fp4_product(result, weights, t, codes, scales):
             words, word_scales = weights
@@ -168,15 +172,21 @@ def tile_picked_hyena2_none_po_kernel(
 
         taps0 = held([P, S], F32, "taps0")
         taps1 = held([P, S], F32, "taps1")
-        late_taps = held([P, 2, S], F32, "late_taps")
+        sum_area = held([P, 18 * CHUNK], F32, "sum_slots")
+
+        def slots(first):
+            return sum_area[:, first * CHUNK : (first + 3 * PACK) * CHUNK].rearrange("p (t n) -> p t n", t=PACK)[:, :, :HALF]
+
+        taps2 = sum_area[:, 9 * CHUNK : 13 * CHUNK]
+        taps3 = held([P, S], F32, "taps3")
         for half in halves:
             nc.vector.tensor_copy(taps0[:, half], val_window[0][:].indirect(entries(t1_sb, half)))
         for half in halves:
             scalar_look_up(taps1[:, half], val_window[1], t1_sb, half)
         val3_bank = val_product(3, whole, 6, nc.vector.tensor_copy)
-        for t in (2, 3):
+        for t, taps in ((2, taps2), (3, taps3)):
             for half in halves:
-                scalar_look_up(late_taps[:, t - 2, half], val_window[t], t1_sb, half)
+                scalar_look_up(taps[:, half], val_window[t], t1_sb, half)
 
         e_banks = []
         for t, number in enumerate((7, 1, 2, 4)):
@@ -188,39 +198,35 @@ def tile_picked_hyena2_none_po_kernel(
 
         sums1 = held([P, S], F32, "val_window0")
         nc.gpsimd.tensor_tensor(sums1[:], val_window[1][:], taps1[:], ADD)
-        nc.gpsimd.tensor_tensor(late_taps[:, 0, :], val_window[2][:], late_taps[:, 0, :], ADD)
+        nc.gpsimd.tensor_tensor(taps2, val_window[2][:], taps2, ADD)
         for u, half in enumerate(halves):
             nc.vector.tensor_tensor(taps0[:, half], val0_banks[u][:], taps0[:, half], ADD)
         for half in halves:
             first_gate(0, taps0[:, half], half)
-        first_gate(1, sums1[:], whole)
-        sums3 = held([P, S], F32, "taps0")
         for half in halves:
-            nc.vector.tensor_tensor(sums3[:, half], val3_bank[:, half], late_taps[:, 1, half], ADD)
-        first_gate(2, late_taps[:, 0, :], whole)
-        first_gate(3, sums3[:], whole)
+            first_gate(1, sums1[:, half], half)
+        for half in halves:
+            nc.vector.tensor_tensor(sums1[:, half], val3_bank[:, half], taps3[:, half], ADD)
+        first_gate(2, taps2, whole)
+        first_gate(3, sums1[:], whole)
 
         out_rows = out_0.rearrange("(p t) n -> p t n", t=PACK)
         out_words = out_1[0].rearrange("p c r -> p (c r)").bitcast(I32)
-        sum_area = held([P, 18 * CHUNK], F32, "sum_slots")
-
-        def slots(first):
-            return sum_area[:, first * CHUNK : (first + 3 * PACK) * CHUNK].rearrange("p (t n) -> p t n", t=PACK)[:, :, :HALF]
-
         first_sums = slots(6)
         later_sums = slots(0)
         staged = sum_area[:, :HALF]
-        for t in range(3):
-            scalar_look_up(first_sums[:, t, :], h_window[t], t2_sb, halves[0])
+        staged1 = held([P, HALF], F32, "staged1")
+        for t, taps in enumerate((first_sums[:, 0, :], staged1[:], first_sums[:, 2, :])):
+            scalar_look_up(taps, h_window[t], t2_sb, halves[0])
         scalar_look_up(staged[:, chunks[1]], h_window[3], t2_sb, chunks[1])
         nc.gpsimd.tensor_tensor(first_sums[:, 0, :], first_sums[:, 0, :], h_window[0][:, halves[0]], ADD)
-        nc.vector.tensor_tensor(first_sums[:, 1, :], first_sums[:, 1, :], h_window[1][:, halves[0]], ADD)
+        nc.vector.tensor_tensor(first_sums[:, 1, :], staged1[:], h_window[1][:, halves[0]], ADD)
         nc.vector.tensor_copy(staged[:, chunks[0]], h_window[3][:].indirect(entries(t2_sb, chunks[0])))
         nc.vector.tensor_tensor(first_sums[:, 2, :], first_sums[:, 2, :], h_window[2][:, halves[0]], ADD)
         for c in range(2):
             nc.vector.tensor_tensor(first_sums[:, 3, chunks[c]], staged[:, chunks[c]], h_window[3][:, chunks[c]], ADD)
 
-        later_taps = held([P, PACK, HALF], F32, "taps0")
+        later_taps = held([P, PACK, HALF], F32, "val_window0")
         for t in range(2):
             scalar_look_up(later_taps[:, t, :], h_window[t], t2_sb, halves[1])
         for c in (2, 3):

@@ -234,13 +234,14 @@ def tile_picked_hyena2_none_po_kernel(
                 scalar_look_up(later_taps[:, t, chunks[c - 2]], h_window[t], t2_sb, chunks[c])
 
         z_tiles = [sum_area[:, first * CHUNK : (first + 2) * CHUNK].bitcast(BF16) for first in (2, 4)]
-        z_tiles = z_tiles + [held([P, PACK * CHUNK], BF16, "z_bf%d" % c)[:] for c in (2, 3)]
+        late_z = held([P, PACK * HALF], BF16, "late_z")
+        z_tiles = z_tiles + [late_z[:, : PACK * CHUNK], late_z[:, PACK * CHUNK :]]
         z_codes = held([P, S], U32, "z_codes")
         z_scales = held([P, S], U8, "z_scales")
         out_f32 = [held([P, PACK, CHUNK], F32, "out_f32%d" % c) for c in range(CHUNKS)]
 
         def second_gate(c):
-            y_bank = bank((5, 0)[c % 2], [P, PACK, CHUNK])
+            y_bank = bank((2, 4)[c % 2], [P, PACK, CHUNK])
             for t in range(PACK):
                 fp4_product(y_bank[:, t, :], w1_q, t, xq_words[:, chunks[c]], xq_scales[:, chunks[c]])
             sums = (first_sums, later_sums)[c // 2][:, :, chunks[c % 2]]
@@ -263,7 +264,7 @@ def tile_picked_hyena2_none_po_kernel(
             return out_bank
 
         def round_bank(rounded, out_bank):
-            nc.scalar.copy(rounded.rearrange("p (n t) -> p n t", t=PACK), out_bank[:].rearrange("p t n -> p n t"))
+            nc.scalar.copy(rounded.rearrange("p (n t) -> p n t", t=PACK), out_bank.rearrange("p t n -> p n t"))
 
         def round_stored(rounded, stored):
             nc.vector.tensor_copy(rounded.rearrange("p (n i t) -> p n t i", i=4, t=PACK), stored.rearrange("p t (n i) -> p n t i", i=4))
@@ -275,8 +276,8 @@ def tile_picked_hyena2_none_po_kernel(
         second_gate(1)
         later_add(nc.gpsimd, 0, halves[1], later_taps[:, 0, :])
         quantise_z(0)
-        first_bf = held([P, PACK * CHUNK], BF16, "first_bf")
-        round_bank(first_bf[:], last_layer(0, 7))
+        pieces = [slice(first, first + PIECE) for first in range(0, CHUNK, PIECE)]
+        first_bank = last_layer(0, 7)
         for t in (2, 1, 3):
             later_add(nc.vector, t, chunks[2], later_taps[:, t, chunks[0]])
         quantise_z(1)
@@ -286,37 +287,45 @@ def tile_picked_hyena2_none_po_kernel(
         for t in (2, 3):
             later_add(nc.vector, t, chunks[3], later_taps[:, t, chunks[1]])
         quantise_z(2)
-        late_bf = held([P, PACK * HALF], BF16, "late_bf")
-        round_bank(late_bf[:, : PACK * CHUNK], last_layer(2, 2))
+        nc.gpsimd.tensor_copy(
+            late_z[:, : PACK * PIECE].rearrange("p (n t) -> p n t", t=PACK), out_f32[0][:, :, pieces[0]].rearrange("p t n -> p n t")
+        )
+        round_bank(late_z[:, PACK * PIECE : PACK * CHUNK], first_bank[:, :, pieces[1]])
+        third_bank = last_layer(2, 5)
         second_gate(3)
         out_scales = held([P, S], U8, "sum_slots")
-        early_codes = held([P, HALF], U32, "early_codes")
-        nc.vector.quantize_mx(early_codes[:, chunks[0]].bitcast(FP8X4), out_scales[:, chunks[0]], first_bf[:])
+        border = HALF + PIECE
+        out_codes = [held([P, HALF], U32, "early_codes")]
+
+        def quantise_out(first, rounded):
+            count = rounded.shape[1] // PACK
+            codes = out_codes[first // HALF][:, first % HALF : first % HALF + count]
+            nc.vector.quantize_mx(codes.bitcast(FP8X4), out_scales[:, first : first + count], rounded)
+
         quantise_z(3)
-        second_bf = held([P, PACK * CHUNK], BF16, "z_bf3")
-        round_stored(second_bf[:], out_f32[1][:])
-        nc.vector.quantize_mx(early_codes[:, chunks[1]].bitcast(FP8X4), out_scales[:, chunks[1]], second_bf[:])
-        nc.sync.dma_start(out_words[:, halves[0]], early_codes[:].bitcast(I32))
+        round_stored(z_tiles[3], out_f32[1][:])
+        middle_bf = held([P, PACK * PIECE], BF16, "middle_bf")
+        round_bank(middle_bf[:], third_bank[:, :, pieces[0]])
+        quantise_out(0, late_z[:])
+        nc.sync.dma_start(out_words[:, halves[0]], out_codes[0][:].bitcast(I32))
 
         last = chunks[3]
         for pair, copy in enumerate((nc.scalar.copy, nc.vector.tensor_copy)):
-            pair_bank = bank((4, 6)[pair], [P, 2, CHUNK])
+            pair_bank = bank((0, 6)[pair], [P, 2, CHUNK])
             for t in range(2):
                 fp4_product(pair_bank[:, t, :], w4_q, 2 * pair + t, z_codes[:, last], z_scales[:, last])
-            for first in range(0, CHUNK, PIECE):
-                copy(out_f32[3][:, 2 * pair : 2 * pair + 2, first : first + PIECE], pair_bank[:, :, first : first + PIECE])
+            for piece in pieces:
+                copy(out_f32[3][:, 2 * pair : 2 * pair + 2, piece], pair_bank[:, :, piece])
         nc.sync.dma_start(out_rows[:, :, last], out_f32[3][:])
-        late_codes = held([P, HALF], U32, "late_codes")
-        nc.vector.quantize_mx(late_codes[:, :CHUNK].bitcast(FP8X4), out_scales[:, chunks[2]], late_bf[:, : PACK * CHUNK])
-        for first in range(0, CHUNK, PIECE):
-            round_stored(late_bf[:, PACK * (CHUNK + first) : PACK * (CHUNK + first + PIECE)], out_f32[3][:, :, first : first + PIECE])
-        for first in range(CHUNK, HALF, PIECE):
-            nc.vector.quantize_mx(
-                late_codes[:, first : first + PIECE].bitcast(FP8X4),
-                out_scales[:, HALF + first : HALF + first + PIECE],
-                late_bf[:, PACK * first : PACK * (first + PIECE)],
-            )
-        nc.sync.dma_start(out_words[:, halves[1]], late_codes[:].bitcast(I32))
+        out_codes.append(held([P, HALF], U32, "z_codes"))
+        quantise_out(HALF, middle_bf[:])
+        late_bf = held([P, PACK * (S - border)], BF16, "z_scales")
+        round_bank(late_bf[:, : PACK * PIECE], third_bank[:, :, pieces[1]])
+        for piece in pieces:
+            round_stored(late_bf[:, PACK * (PIECE + piece.start) : PACK * (PIECE + piece.stop)], out_f32[3][:, :, piece])
+        quantise_out(border, late_bf[:, : PACK * CHUNK])
+        quantise_out(border + CHUNK, late_bf[:, PACK * CHUNK :])
+        nc.sync.dma_start(out_words[:, halves[1]], out_codes[1][:].bitcast(I32))
         for q in range(4):
             queue = nc.sync if q < 2 else nc.scalar
             queue.dma_start(out_2[0, 4 * q : 4 * q + 4, :].bitcast(I32), out_scales[32 * q : 32 * q + 4, :].bitcast(I32))

@@ -68,15 +68,14 @@ def tile_picked_hyena2_none_po_kernel(
         nc.sync.dma_start(w3_raw[:, 0:2, :], w3_rows[:, 0:2, :])
         nc.sync.dma_start(offs_sb[:], offs)
         nc.sync.dma_start(x_scale_table[0:P:8, :].bitcast(I32), x_scales[0].bitcast(I32))
-        for i, scales in enumerate((w2_scales, w1_scales)):
+        for i, scales in enumerate((w1_scales, w4_scales)):
             nc.sync.dma_start(w_scale_rows[0:16, i * H : (i + 1) * H].bitcast(I32), scales[0].bitcast(I32))
         nc.sync.dma_start(w3_raw[:, 2:4, :], w3_rows[:, 2:4, :])
-        nc.sync.dma_start(w_scale_rows[0:16, 2 * H : 3 * H].bitcast(I32), w4_scales[0].bitcast(I32))
+        nc.sync.dma_start(w_scale_rows[0:16, 2 * H : 3 * H].bitcast(I32), w2_scales[0].bitcast(I32))
         x_word_table = held([P, T], U32, "x_word_table")
         nc.sync.dma_start(x_word_table[:].bitcast(I32), x_words[0].rearrange("p c r -> p (c r)").bitcast(I32))
         w2_raw = load_words(w2_words, "w2_raw")
         w1_raw = load_words(w1_words, "w1_raw")
-        w4_raw = load_words(w4_words, "w4_raw")
 
         def deal_words(copy, raw_words, words):
             copy(
@@ -91,12 +90,13 @@ def tile_picked_hyena2_none_po_kernel(
         nc.vector.tensor_copy(xq_scales[:].bitcast(I32), x_scale_picked[:].bitcast(I32))
         for j in range(1, 4):
             nc.sync.dma_start(xq_scales[j:P:32, :].bitcast(I32), x_scale_picked[8 * j : P : 32, :].bitcast(I32))
+        w4_raw = load_words(w4_words, "w4_raw")
         nc.sync.dma_start(t1_sb[:], t1)
 
         def deal_scales(engine, rows, dealt):
-            engine.tensor_copy(dealt.rearrange("p (t m) -> p t m", t=PACK), rows.rearrange("p (m t) -> p t m", t=PACK))
-
-        def place_scales(dealt):
+            engine.tensor_copy(
+                dealt.rearrange("p (i t m) -> p t i m", t=PACK, m=P), rows.rearrange("p (i m t) -> p t i m", t=PACK, m=P)
+            )
             for q in range(1, 4):
                 nc.sync.dma_start(dealt[32 * q : 32 * q + 4, :].bitcast(I32), dealt[4 * q : 4 * q + 4, :].bitcast(I32))
 
@@ -106,6 +106,11 @@ def tile_picked_hyena2_none_po_kernel(
         for rows in (slice(0, 2), slice(2, 4)):
             nc.scalar.copy(w3_dealt[:, :, 0:2, rows], w3_walk[:, :, 0:2, rows])
         nc.scalar.copy(w3_dealt[:, : P // 2, 2:4, :], w3_walk[:, : P // 2, 2:4, :])
+        w2_scales_dealt = held([P, H], U8, "w2_scales_dealt")
+        deal_scales(nc.vector, w_scale_rows[:, 2 * H : 3 * H], w2_scales_dealt[:])
+        nc.sync.dma_start(t2_sb[:], t2)
+        late_scales = held([P, 2 * H], U8, "late_scales")
+        deal_scales(nc.gpsimd, w_scale_rows[:, 0 : 2 * H], late_scales[:])
         w3_scales = held([P, H], U8, "w3_scales")
         w3_code_pairs = []
 
@@ -123,28 +128,32 @@ def tile_picked_hyena2_none_po_kernel(
             )
         nc.vector.tensor_copy(w3_dealt[:, P // 2 :, 2:4, :], w3_walk[:, P // 2 :, 2:4, :])
         quantise_w3(1, "w3_codes_late")
-        gate_scales = held([P, 2 * H], U8, "gate_scales")
-        for i in range(2):
-            deal_scales(nc.vector, w_scale_rows[:, i * H : (i + 1) * H], gate_scales[:, i * H : (i + 1) * H])
-        place_scales(gate_scales[:])
-        nc.sync.dma_start(t2_sb[:], t2)
         xq_words = held([P, S], U32, "xq_words")
         for half in halves:
             nc.vector.tensor_copy(xq_words[:, half], x_word_table[:].indirect(entries(offs_sb, half)))
-        w_dealt = held([P, 4 * H], U8, "w_dealt")
-        w4_dealt = held([P, 2 * H], U8, "x_word_table")
-        w2_q = deal_words(nc.scalar.copy, w2_raw, w_dealt[:, 0 : 2 * H]), gate_scales[:, 0:H]
-        w1_q = deal_words(nc.scalar.copy, w1_raw, w_dealt[:, 2 * H : 4 * H]), gate_scales[:, H : 2 * H]
-        deal_words(nc.vector.tensor_copy, w4_raw, w4_dealt[:])
-        w4_scales_dealt = held([P, H], U8, "w4_raw")
-        deal_scales(nc.gpsimd, w_scale_rows[:, 2 * H : 3 * H], w4_scales_dealt[:])
-        place_scales(w4_scales_dealt[:])
-        w4_q = w4_dealt[:], w4_scales_dealt[:]
+        w2_dealt = held([P, 2 * H], U8, "w2_dealt")
+        w1_dealt = held([P, 2 * H], U8, "x_word_table")
+
+        def row_tiles(words):
+            return [words[:, 2 * P * t : 2 * P * (t + 1)] for t in range(words.shape[1] // (2 * P))]
+
+        w2_q = row_tiles(deal_words(nc.scalar.copy, w2_raw, w2_dealt[:])), w2_scales_dealt[:]
+        w1_q = row_tiles(deal_words(nc.vector.tensor_copy, w1_raw, w1_dealt[:])), late_scales[:, 0:H]
+
+        def deal_w4_pair(pair, name):
+            dealt = held([P, H], U8, name)
+            nc.gpsimd.tensor_copy(
+                dealt[:].rearrange("p (t m b) -> p b t m", t=2, b=2),
+                w4_raw[:].rearrange("p (m t b) -> p b t m", t=PACK, b=2)[:, :, 2 * pair : 2 * pair + 2, :],
+            )
+            return row_tiles(dealt[:])
+
+        w4_tiles = deal_w4_pair(0, "w1_raw")
 
         def fp4_product(result, weights, t, codes, scales):
             words, word_scales = weights
             nc.tensor.matmul_mx(
-                result, lhsT=words[:, 2 * P * t : 2 * P * (t + 1)].bitcast(FP4X4), lhsT_scale=word_scales[:, P * t : P * (t + 1)],
+                result, lhsT=words[t].bitcast(FP4X4), lhsT_scale=word_scales[:, P * t : P * (t + 1)],
                 rhs=codes.bitcast(FP8X4), rhs_scale=scales, start=True, stop=True,
             )
 
@@ -199,6 +208,7 @@ def tile_picked_hyena2_none_po_kernel(
         sums1 = held([P, S], F32, "val_window0")
         nc.gpsimd.tensor_tensor(sums1[:], val_window[1][:], taps1[:], ADD)
         nc.gpsimd.tensor_tensor(taps2, val_window[2][:], taps2, ADD)
+        w4_q = w4_tiles + deal_w4_pair(1, "val_window1"), late_scales[:, H : 2 * H]
         for u, half in enumerate(halves):
             nc.vector.tensor_tensor(taps0[:, half], val0_banks[u][:], taps0[:, half], ADD)
         for half in halves:

@@ -304,20 +304,15 @@ def tile_picked_hyena2_none_po_kernel(
         third_bank = last_layer(2, 5)
         second_gate(3)
         out_scales = held([P, S], U8, "sum_slots")
-        border = HALF + PIECE
-        out_codes = [held([P, HALF], U32, "early_codes")]
+        out_codes = held([P, S], U32, "out_codes")
 
         def quantise_out(first, rounded):
-            count = rounded.shape[1] // PACK
-            codes = out_codes[first // HALF][:, first % HALF : first % HALF + count]
-            nc.vector.quantize_mx(codes.bitcast(FP8X4), out_scales[:, first : first + count], rounded)
+            cols = slice(first, first + rounded.shape[1] // PACK)
+            nc.vector.quantize_mx(out_codes[:, cols].bitcast(FP8X4), out_scales[:, cols], rounded)
 
         quantise_z(3)
         round_stored(z_tiles[3], out_f32[1][:])
-        middle_bf = held([P, PACK * PIECE], BF16, "middle_bf")
-        round_bank(middle_bf[:], third_bank[:, :, pieces[0]])
         quantise_out(0, late_z[:])
-        nc.sync.dma_start(out_words[:, halves[0]], out_codes[0][:].bitcast(I32))
 
         last = chunks[3]
         for pair, copy in enumerate((nc.scalar.copy, nc.vector.tensor_copy)):
@@ -327,15 +322,15 @@ def tile_picked_hyena2_none_po_kernel(
             for piece in pieces:
                 copy(out_f32[3][:, 2 * pair : 2 * pair + 2, piece], pair_bank[:, :, piece])
         nc.sync.dma_start(out_rows[:, :, last], out_f32[3][:])
-        out_codes.append(held([P, HALF], U32, "z_codes"))
-        quantise_out(HALF, middle_bf[:])
-        late_bf = held([P, PACK * (S - border)], BF16, "z_scales")
-        round_bank(late_bf[:, : PACK * PIECE], third_bank[:, :, pieces[1]])
-        for piece in pieces:
-            round_stored(late_bf[:, PACK * (PIECE + piece.start) : PACK * (PIECE + piece.stop)], out_f32[3][:, :, piece])
-        quantise_out(border, late_bf[:, : PACK * CHUNK])
-        quantise_out(border + CHUNK, late_bf[:, PACK * CHUNK :])
-        nc.sync.dma_start(out_words[:, halves[1]], out_codes[1][:].bitcast(I32))
+        late_bf = held([P, PACK * HALF], BF16, "z_scales")
+        round_bank(late_bf[:, : PACK * CHUNK], third_bank[:])
+        last_bf = [late_bf[:, PACK * (CHUNK + piece.start) : PACK * (CHUNK + piece.stop)] for piece in pieces]
+        for piece, rounded in zip(pieces, last_bf):
+            round_stored(rounded, out_f32[3][:, :, piece])
+        for piece, rounded in zip(pieces, last_bf):
+            quantise_out(last.start + piece.start, rounded)
+        quantise_out(HALF, late_bf[:, : PACK * CHUNK])
+        nc.sync.dma_start(out_words, out_codes[:].bitcast(I32))
         for q in range(4):
             queue = nc.sync if q < 2 else nc.scalar
             queue.dma_start(out_2[0, 4 * q : 4 * q + 4, :].bitcast(I32), out_scales[32 * q : 32 * q + 4, :].bitcast(I32))

@@ -297,12 +297,10 @@ def tile_picked_hyena2_none_po_kernel(
         for t in (2, 3):
             later_add(nc.vector, t, chunks[3], later_taps[:, t, chunks[1]])
         quantise_z(2)
-        nc.gpsimd.tensor_copy(
-            late_z[:, : PACK * PIECE].rearrange("p (n t) -> p n t", t=PACK), out_f32[0][:, :, pieces[0]].rearrange("p t n -> p n t")
-        )
         round_bank(late_z[:, PACK * PIECE : PACK * CHUNK], first_bank[:, :, pieces[1]])
         third_bank = last_layer(2, 5)
         second_gate(3)
+        round_stored(late_z[:, : PACK * PIECE], out_f32[0][:, :, pieces[0]])
         out_scales = held([P, S], U8, "sum_slots")
         out_codes = held([P, S], U32, "out_codes")
 
@@ -332,5 +330,4 @@ def tile_picked_hyena2_none_po_kernel(
         quantise_out(HALF, late_bf[:, : PACK * CHUNK])
         nc.sync.dma_start(out_words, out_codes[:].bitcast(I32))
         for q in range(4):
-            queue = nc.sync if q < 2 else nc.scalar
-            queue.dma_start(out_2[0, 4 * q : 4 * q + 4, :].bitcast(I32), out_scales[32 * q : 32 * q + 4, :].bitcast(I32))
+            nc.scalar.dma_start(out_2[0, 4 * q : 4 * q + 4, :].bitcast(I32), out_scales[32 * q : 32 * q + 4, :].bitcast(I32))

@@ -23,7 +23,7 @@ HALF = S // 2
 CHUNK = 128
 CHUNKS = S // CHUNK
 PIECE = 64
-WARM_UP_PASSES = 4
+WARM_UP_PASSES = 3
 
 
 def entries(lst, cols):
@@ -309,8 +309,8 @@ def tile_picked_hyena2_none_po_kernel(
             nc.vector.quantize_mx(out_codes[:, cols].bitcast(FP8X4), out_scales[:, cols], rounded)
 
         quantise_z(3)
+        quantise_out(0, z_tiles[2])
         round_stored(z_tiles[3], out_f32[1][:])
-        quantise_out(0, late_z[:])
 
         last = chunks[3]
         for pair, copy in enumerate((nc.scalar.copy, nc.vector.tensor_copy)):
@@ -320,6 +320,7 @@ def tile_picked_hyena2_none_po_kernel(
             for piece in pieces:
                 copy(out_f32[3][:, 2 * pair : 2 * pair + 2, piece], pair_bank[:, :, piece])
         nc.sync.dma_start(out_rows[:, :, last], out_f32[3][:])
+        quantise_out(CHUNK, z_tiles[3])
         late_bf = held([P, PACK * HALF], BF16, "z_scales")
         round_bank(late_bf[:, : PACK * CHUNK], third_bank[:])
         last_bf = [late_bf[:, PACK * (CHUNK + piece.start) : PACK * (CHUNK + piece.stop)] for piece in pieces]

@@ -23,7 +23,6 @@ HALF = S // 2
 CHUNK = 128
 CHUNKS = S // CHUNK
 PIECE = 64
-WARM_UP_PASSES = 3
 
 
 def entries(lst, cols):
@@ -112,22 +111,26 @@ def tile_picked_hyena2_none_po_kernel(
         late_scales = held([P, 2 * H], U8, "late_scales")
         deal_scales(nc.gpsimd, w_scale_rows[:, 0 : 2 * H], late_scales[:])
         w3_scales = held([P, H], U8, "w3_scales")
-        w3_code_pairs = []
+        w3_codes = held([P, H], U32, "w3_codes")
 
-        def quantise_w3(pair, name):
-            codes = held([P, 2 * P], U32, name)
-            nc.vector.quantize_mx(codes[:].bitcast(FP8X4), w3_scales[:, 2 * P * pair : 2 * P * (pair + 1)], w3_bf[:, 2 * H * pair : 2 * H * (pair + 1)])
-            w3_code_pairs.append(codes)
+        def quantise_w3(pair):
+            cols = slice(2 * P * pair, 2 * P * (pair + 1))
+            nc.vector.quantize_mx(w3_codes[:, cols].bitcast(FP8X4), w3_scales[:, cols], w3_bf[:, 2 * H * pair : 2 * H * (pair + 1)])
 
-        quantise_w3(0, "w3_codes")
-        warm = bank(7, [P, HALF])
-        for repeat in range(WARM_UP_PASSES):
+        warm = bank(7, [P, S])
+
+        def warm_up(rows, cols):
             nc.tensor.matmul_mx(
-                warm[:], lhsT=w3_code_pairs[0][:, 0:P].bitcast(FP8X4), lhsT_scale=w3_scales[:, 0:P],
-                rhs=w3_code_pairs[0][:].bitcast(FP8X4), rhs_scale=w3_scales[:, 0 : 2 * P], start=True, stop=True,
+                warm[:rows, :cols], lhsT=w3_codes[:, 0:rows].bitcast(FP8X4), lhsT_scale=w3_scales[:, 0:rows],
+                rhs=w3_codes[:, :cols].bitcast(FP8X4), rhs_scale=w3_scales[:, :cols], start=True, stop=True,
             )
+
+        quantise_w3(0)
+        warm_up(P, HALF)
+        warm_up(P, HALF)
         nc.vector.tensor_copy(w3_dealt[:, P // 2 :, 2:4, :], w3_walk[:, P // 2 :, 2:4, :])
-        quantise_w3(1, "w3_codes_late")
+        quantise_w3(1)
+        warm_up(32, S)
         xq_words = held([P, S], U32, "xq_words")
         for half in halves:
             nc.vector.tensor_copy(xq_words[:, half], x_word_table[:].indirect(entries(offs_sb, half)))
@@ -166,7 +169,7 @@ def tile_picked_hyena2_none_po_kernel(
         def val_product(t, cols, number, copy):
             val_bank = bank(number, [P, cols.stop - cols.start])
             nc.tensor.matmul_mx(
-                val_bank[:], lhsT=w3_code_pairs[t // 2][:, P * (t % 2) : P * (t % 2 + 1)].bitcast(FP8X4), lhsT_scale=w3_scales[:, P * t : P * (t + 1)],
+                val_bank[:], lhsT=w3_codes[:, P * t : P * (t + 1)].bitcast(FP8X4), lhsT_scale=w3_scales[:, P * t : P * (t + 1)],
                 rhs=xq_words[:, cols].bitcast(FP8X4), rhs_scale=xq_scales[:, cols], start=True, stop=True,
             )
             copy(val_window[t][:, cols], val_bank[:])

@@ -74,6 +74,7 @@ def tile_picked_hyena2_none_po_kernel(
         x_word_table = held([P, T], U32, "x_word_table")
         nc.sync.dma_start(x_word_table[:].bitcast(I32), x_words[0].rearrange("p c r -> p (c r)").bitcast(I32))
         w2_raw = load_words(w2_words, "w2_raw")
+        w4_raw = load_words(w4_words, "w4_raw")
         w1_raw = load_words(w1_words, "w1_raw")
 
         def deal_words(copy, raw_words, words):
@@ -89,7 +90,6 @@ def tile_picked_hyena2_none_po_kernel(
         nc.vector.tensor_copy(xq_scales[:].bitcast(I32), x_scale_picked[:].bitcast(I32))
         for j in range(1, 4):
             nc.sync.dma_start(xq_scales[j:P:32, :].bitcast(I32), x_scale_picked[8 * j : P : 32, :].bitcast(I32))
-        w4_raw = load_words(w4_words, "w4_raw")
         nc.sync.dma_start(t1_sb[:], t1)
 
         def deal_scales(engine, rows, dealt):
@@ -143,15 +143,8 @@ def tile_picked_hyena2_none_po_kernel(
         w2_q = row_tiles(deal_words(nc.scalar.copy, w2_raw, w2_dealt[:])), w2_scales_dealt[:]
         w1_q = row_tiles(deal_words(nc.vector.tensor_copy, w1_raw, w1_dealt[:])), late_scales[:, 0:H]
 
-        def deal_w4_pair(pair, name):
-            dealt = held([P, H], U8, name)
-            nc.gpsimd.tensor_copy(
-                dealt[:].rearrange("p (t m b) -> p b t m", t=2, b=2),
-                w4_raw[:].rearrange("p (m t b) -> p b t m", t=PACK, b=2)[:, :, 2 * pair : 2 * pair + 2, :],
-            )
-            return row_tiles(dealt[:])
-
-        w4_tiles = deal_w4_pair(0, "w1_raw")
+        w4_dealt = held([P, 2 * H], U8, "w4_dealt")
+        w4_q = row_tiles(deal_words(nc.scalar.copy, w4_raw, w4_dealt[:])), late_scales[:, H : 2 * H]
 
         def fp4_product(result, weights, t, codes, scales):
             words, word_scales = weights
@@ -211,7 +204,6 @@ def tile_picked_hyena2_none_po_kernel(
         sums1 = held([P, S], F32, "val_window0")
         nc.gpsimd.tensor_tensor(sums1[:], val_window[1][:], taps1[:], ADD)
         nc.gpsimd.tensor_tensor(taps2, val_window[2][:], taps2, ADD)
-        w4_q = w4_tiles + deal_w4_pair(1, "val_window1"), late_scales[:, H : 2 * H]
         for u, half in enumerate(halves):
             nc.vector.tensor_tensor(taps0[:, half], val0_banks[u][:], taps0[:, half], ADD)
         for half in halves:

@@ -67,8 +67,6 @@ def tile_picked_hyena2_none_po_kernel(
         nc.sync.dma_start(w3_raw[:, 0:2, :], w3_rows[:, 0:2, :])
         nc.sync.dma_start(offs_sb[:], offs)
         nc.sync.dma_start(x_scale_table[0:P:8, :].bitcast(I32), x_scales[0].bitcast(I32))
-        for i, scales in enumerate((w1_scales, w4_scales)):
-            nc.sync.dma_start(w_scale_rows[0:16, i * H : (i + 1) * H].bitcast(I32), scales[0].bitcast(I32))
         nc.sync.dma_start(w3_raw[:, 2:4, :], w3_rows[:, 2:4, :])
         nc.sync.dma_start(w_scale_rows[0:16, 2 * H : 3 * H].bitcast(I32), w2_scales[0].bitcast(I32))
         x_word_table = held([P, T], U32, "x_word_table")
@@ -91,6 +89,8 @@ def tile_picked_hyena2_none_po_kernel(
         for j in range(1, 4):
             nc.sync.dma_start(xq_scales[j:P:32, :].bitcast(I32), x_scale_picked[8 * j : P : 32, :].bitcast(I32))
         nc.sync.dma_start(t1_sb[:], t1)
+        for i, scales in enumerate((w1_scales, w4_scales)):
+            nc.sync.dma_start(w_scale_rows[0:16, i * H : (i + 1) * H].bitcast(I32), scales[0].bitcast(I32))
 
         def deal_scales(engine, rows, dealt):
             engine.tensor_copy(

@@ -72,7 +72,6 @@ def tile_picked_hyena2_none_po_kernel(
         x_word_table = held([P, T], U32, "x_word_table")
         nc.sync.dma_start(x_word_table[:].bitcast(I32), x_words[0].rearrange("p c r -> p (c r)").bitcast(I32))
         w2_raw = load_words(w2_words, "w2_raw")
-        w4_raw = load_words(w4_words, "w4_raw")
         w1_raw = load_words(w1_words, "w1_raw")
 
         def deal_words(copy, raw_words, words):
@@ -88,9 +87,10 @@ def tile_picked_hyena2_none_po_kernel(
         nc.vector.tensor_copy(xq_scales[:].bitcast(I32), x_scale_picked[:].bitcast(I32))
         for j in range(1, 4):
             nc.sync.dma_start(xq_scales[j:P:32, :].bitcast(I32), x_scale_picked[8 * j : P : 32, :].bitcast(I32))
-        nc.sync.dma_start(t1_sb[:], t1)
+        w4_raw = load_words(w4_words, "w4_raw")
         for i, scales in enumerate((w1_scales, w4_scales)):
             nc.sync.dma_start(w_scale_rows[0:16, i * H : (i + 1) * H].bitcast(I32), scales[0].bitcast(I32))
+        nc.sync.dma_start(t1_sb[:], t1)
 
         def deal_scales(engine, rows, dealt):
             engine.tensor_copy(
@@ -108,8 +108,6 @@ def tile_picked_hyena2_none_po_kernel(
         w2_scales_dealt = held([P, H], U8, "w2_scales_dealt")
         deal_scales(nc.vector, w_scale_rows[:, 2 * H : 3 * H], w2_scales_dealt[:])
         nc.sync.dma_start(t2_sb[:], t2)
-        late_scales = held([P, 2 * H], U8, "late_scales")
-        deal_scales(nc.gpsimd, w_scale_rows[:, 0 : 2 * H], late_scales[:])
         w3_scales = held([P, H], U8, "w3_scales")
         w3_codes = held([P, H], U32, "w3_codes")
 
@@ -135,16 +133,23 @@ def tile_picked_hyena2_none_po_kernel(
         for half in halves:
             nc.vector.tensor_copy(xq_words[:, half], x_word_table[:].indirect(entries(offs_sb, half)))
         w2_dealt = held([P, 2 * H], U8, "w2_dealt")
-        w1_dealt = held([P, 2 * H], U8, "x_word_table")
+        w1_dealt = held([P, 2 * H], U8, "w1_dealt")
 
         def row_tiles(words):
             return [words[:, 2 * P * t : 2 * P * (t + 1)] for t in range(words.shape[1] // (2 * P))]
 
         w2_q = row_tiles(deal_words(nc.scalar.copy, w2_raw, w2_dealt[:])), w2_scales_dealt[:]
-        w1_q = row_tiles(deal_words(nc.vector.tensor_copy, w1_raw, w1_dealt[:])), late_scales[:, 0:H]
+        w1_tiles = row_tiles(deal_words(nc.scalar.copy, w1_raw, w1_dealt[:]))
 
         w4_dealt = held([P, 2 * H], U8, "w4_dealt")
-        w4_q = row_tiles(deal_words(nc.scalar.copy, w4_raw, w4_dealt[:])), late_scales[:, H : 2 * H]
+        nc.gpsimd.tensor_copy(
+            w4_dealt[:].rearrange("p (t m b) -> p b t m", t=PACK, b=2), w4_raw[:].rearrange("p (m t b) -> p b t m", t=PACK, b=2)
+        )
+        late_scales = held([P, 2 * H], U8, "w4_raw")
+        deal_scales(nc.gpsimd, w_scale_rows[:, 0 : 2 * H], late_scales[:])
+        w4_q = row_tiles(w4_dealt[:]), late_scales[:, H : 2 * H]
+
+        w1_q = w1_tiles, late_scales[:, 0:H]
 
         def fp4_product(result, weights, t, codes, scales):
             words, word_scales = weights
@@ -201,7 +206,7 @@ def tile_picked_hyena2_none_po_kernel(
         def first_gate(t, sums, cols):
             nc.vector.tensor_tensor(h_window[t][:, cols], e_banks[t][:, cols], sums, MULT)
 
-        sums1 = held([P, S], F32, "val_window0")
+        sums1 = held([P, S], F32, "sums1")
         nc.gpsimd.tensor_tensor(sums1[:], val_window[1][:], taps1[:], ADD)
         nc.gpsimd.tensor_tensor(taps2, val_window[2][:], taps2, ADD)
         for u, half in enumerate(halves):
@@ -231,7 +236,7 @@ def tile_picked_hyena2_none_po_kernel(
         for c in range(2):
             nc.vector.tensor_tensor(first_sums[:, 3, chunks[c]], staged[:, chunks[c]], h_window[3][:, chunks[c]], ADD)
 
-        later_taps = held([P, PACK, HALF], F32, "val_window0")
+        later_taps = held([P, PACK, HALF], F32, "sums1")
         for t in range(2):
             scalar_look_up(later_taps[:, t, :], h_window[t], t2_sb, halves[1])
         for c in (2, 3):

@@ -68,9 +68,9 @@ def tile_picked_hyena2_none_po_kernel(
         nc.sync.dma_start(offs_sb[:], offs)
         nc.sync.dma_start(x_scale_table[0:P:8, :].bitcast(I32), x_scales[0].bitcast(I32))
         nc.sync.dma_start(w3_raw[:, 2:4, :], w3_rows[:, 2:4, :])
-        nc.sync.dma_start(w_scale_rows[0:16, 2 * H : 3 * H].bitcast(I32), w2_scales[0].bitcast(I32))
         x_word_table = held([P, T], U32, "x_word_table")
         nc.sync.dma_start(x_word_table[:].bitcast(I32), x_words[0].rearrange("p c r -> p (c r)").bitcast(I32))
+        nc.sync.dma_start(w_scale_rows[0:16, 2 * H : 3 * H].bitcast(I32), w2_scales[0].bitcast(I32))
         w2_raw = load_words(w2_words, "w2_raw")
         w1_raw = load_words(w1_words, "w1_raw")
 
@@ -106,7 +106,7 @@ def tile_picked_hyena2_none_po_kernel(
             nc.scalar.copy(w3_dealt[:, :, 0:2, rows], w3_walk[:, :, 0:2, rows])
         nc.scalar.copy(w3_dealt[:, : P // 2, 2:4, :], w3_walk[:, : P // 2, 2:4, :])
         w2_scales_dealt = held([P, H], U8, "w2_scales_dealt")
-        deal_scales(nc.vector, w_scale_rows[:, 2 * H : 3 * H], w2_scales_dealt[:])
+        deal_scales(nc.gpsimd, w_scale_rows[:, 2 * H : 3 * H], w2_scales_dealt[:])
         nc.sync.dma_start(t2_sb[:], t2)
         w3_scales = held([P, H], U8, "w3_scales")
         w3_codes = held([P, H], U32, "w3_codes")

from contextlib import ExitStack

import concourse.mybir as mybir

K, T, S, H, N = 512, 2048, 512, 512, 512
FLOPS = 4 * 2 * K * H * S

F32 = mybir.dt.float32
BF16 = mybir.dt.bfloat16
I32 = mybir.dt.int32
U32 = mybir.dt.uint32
U16 = mybir.dt.uint16
U8 = mybir.dt.uint8
FP8X4 = mybir.dt.float8_e4m3fn_x4
FP4X4 = mybir.dt.float4_e2m1fn_x4
ADD = mybir.AluOpType.add
MULT = mybir.AluOpType.mult
COPY = mybir.ActivationFunctionType.Copy

P = 128
PACK = 4
HALF = S // 2
CHUNK = 128
CHUNKS = S // CHUNK
PIECE = 64


def entries(lst, cols):
    return lst[:, cols.start // 16 : cols.stop // 16]


def tile_picked_hyena2_none_po_kernel(
    tc, x_words, x_scales, w1_words, w1_scales, w2_words, w2_scales, w3, w4_words, w4_scales,
    offs, t1, t2, out_0, out_1, out_2,
):
    nc = tc.nc
    with ExitStack() as ctx:
        keep = ctx.enter_context(tc.tile_pool(name="keep", bufs=1))
        psum = ctx.enter_context(tc.psum_pool(name="psum", bufs=1))

        def held(shape, dtype, name):
            return keep.tile(shape, dtype, name=name, align_bytes=64)

        def bank(number, shape):
            return psum.tile(shape, F32, name="bank%d" % number)

        whole = slice(0, S)
        halves = [slice(0, HALF), slice(HALF, S)]
        chunks = [slice(c * CHUNK, (c + 1) * CHUNK) for c in range(CHUNKS)]

        offs_sb = held([P, S // 16], U16, "offs_sb")
        t1_sb = held([P, S // 16], U16, "t1_sb")
        t2_sb = held([P, S // 16], U16, "t2_sb")

        def load_words(words, name):
            raw_words = held([P, 2 * H], U8, name)
            nc.sync.dma_start(raw_words[:].bitcast(I32), words[0].bitcast(I32))
            return raw_words

        x_scale_table = held([P, T], U8, "x_scale_table")
        nc.vector.memset(x_scale_table[:].bitcast(I32), 0)
        w_scale_rows = held([P, 3 * H], U8, "w_scale_rows")
        nc.gpsimd.memset(w_scale_rows[:].bitcast(I32), 0)

        w3_raw = held([P, PACK, H], F32, "w3_raw")
        w3_rows = w3.rearrange("(p j) c -> p j c", j=PACK)
        nc.sync.dma_start(w3_raw[:, 0:2, :], w3_rows[:, 0:2, :])
        nc.sync.dma_start(offs_sb[:], offs)
        nc.sync.dma_start(x_scale_table[0:P:8, :].bitcast(I32), x_scales[0].bitcast(I32))
        nc.sync.dma_start(w3_raw[:, 2:4, :], w3_rows[:, 2:4, :])
        x_word_table = held([P, T], U32, "x_word_table")
        nc.sync.dma_start(x_word_table[:].bitcast(I32), x_words[0].rearrange("p c r -> p (c r)").bitcast(I32))
        nc.sync.dma_start(w_scale_rows[0:16, 2 * H : 3 * H].bitcast(I32), w2_scales[0].bitcast(I32))
        w2_raw = load_words(w2_words, "w2_raw")
        w1_raw = load_words(w1_words, "w1_raw")

        def deal_words(copy, raw_words, words):
            copy(
                words.bitcast(U16).rearrange("p (t m) -> p t m", t=PACK),
                raw_words[:].bitcast(U16).rearrange("p (m t) -> p t m", t=PACK),
            )
            return words

        x_scale_picked = held([P, S], U8, "x_scale_picked")
        nc.vector.tensor_copy(x_scale_picked[:], x_scale_table[:].indirect(offs_sb[:]))
        xq_scales = held([P, S], U8, "xq_scales")
        nc.vector.tensor_copy(xq_scales[:].bitcast(I32), x_scale_picked[:].bitcast(I32))
        for j in range(1, 4):
            nc.sync.dma_start(xq_scales[j:P:32, :].bitcast(I32), x_scale_picked[8 * j : P : 32, :].bitcast(I32))
        w4_raw = load_words(w4_words, "w4_raw")
        for i, scales in enumerate((w1_scales, w4_scales)):
            nc.sync.dma_start(w_scale_rows[0:16, i * H : (i + 1) * H].bitcast(I32), scales[0].bitcast(I32))
        nc.sync.dma_start(t1_sb[:], t1)

        def deal_scales(engine, rows, dealt):
            engine.tensor_copy(
                dealt.rearrange("p (i t m) -> p t i m", t=PACK, m=P), rows.rearrange("p (i m t) -> p t i m", t=PACK, m=P)
            )
            for q in range(1, 4):
                nc.sync.dma_start(dealt[32 * q : 32 * q + 4, :].bitcast(I32), dealt[4 * q : 4 * q + 4, :].bitcast(I32))

        w3_bf = held([P, PACK * P * PACK], BF16, "w3_bf")
        w3_dealt = w3_bf[:].rearrange("p (t m j) -> p m t j", t=PACK, j=PACK)
        w3_walk = w3_raw[:].rearrange("p j (m t) -> p m t j", t=PACK)
        for rows in (slice(0, 2), slice(2, 4)):
            nc.scalar.copy(w3_dealt[:, :, 0:2, rows], w3_walk[:, :, 0:2, rows])
        nc.scalar.copy(w3_dealt[:, : P // 2, 2:4, :], w3_walk[:, : P // 2, 2:4, :])
        w2_scales_dealt = held([P, H], U8, "w2_scales_dealt")
        deal_scales(nc.gpsimd, w_scale_rows[:, 2 * H : 3 * H], w2_scales_dealt[:])
        nc.sync.dma_start(t2_sb[:], t2)
        w3_scales = held([P, H], U8, "w3_scales")
        w3_codes = held([P, H], U32, "w3_codes")

        def quantise_w3(pair):
            cols = slice(2 * P * pair, 2 * P * (pair + 1))
            nc.vector.quantize_mx(w3_codes[:, cols].bitcast(FP8X4), w3_scales[:, cols], w3_bf[:, 2 * H * pair : 2 * H * (pair + 1)])

        warm = bank(7, [P, S])

        def warm_up(rows, cols):
            nc.tensor.matmul_mx(
                warm[:rows, :cols], lhsT=w3_codes[:, 0:rows].bitcast(FP8X4), lhsT_scale=w3_scales[:, 0:rows],
                rhs=w3_codes[:, :cols].bitcast(FP8X4), rhs_scale=w3_scales[:, :cols], start=True, stop=True,
            )

        quantise_w3(0)
        warm_up(P, HALF)
        warm_up(P, HALF)
        nc.vector.tensor_copy(w3_dealt[:, P // 2 :, 2:4, :], w3_walk[:, P // 2 :, 2:4, :])
        quantise_w3(1)
        warm_up(32, S)
        xq_words = held([P, S], U32, "xq_words")
        for half in halves:
            nc.vector.tensor_copy(xq_words[:, half], x_word_table[:].indirect(entries(offs_sb, half)))
        w2_dealt = held([P, 2 * H], U8, "w2_dealt")
        w1_dealt = held([P, 2 * H], U8, "w1_dealt")

        def row_tiles(words):
            return [words[:, 2 * P * t : 2 * P * (t + 1)] for t in range(words.shape[1] // (2 * P))]

        w2_q = row_tiles(deal_words(nc.scalar.copy, w2_raw, w2_dealt[:])), w2_scales_dealt[:]
        w1_tiles = row_tiles(deal_words(nc.scalar.copy, w1_raw, w1_dealt[:]))

        w4_dealt = held([P, 2 * H], U8, "w4_dealt")
        nc.gpsimd.tensor_copy(
            w4_dealt[:].rearrange("p (t m b) -> p b t m", t=PACK, b=2), w4_raw[:].rearrange("p (m t b) -> p b t m", t=PACK, b=2)
        )
        late_scales = held([P, 2 * H], U8, "w4_raw")
        deal_scales(nc.gpsimd, w_scale_rows[:, 0 : 2 * H], late_scales[:])
        w4_q = row_tiles(w4_dealt[:]), late_scales[:, H : 2 * H]

        w1_q = w1_tiles, late_scales[:, 0:H]

        def fp4_product(result, weights, t, codes, scales):
            words, word_scales = weights
            nc.tensor.matmul_mx(
                result, lhsT=words[t].bitcast(FP4X4), lhsT_scale=word_scales[:, P * t : P * (t + 1)],
                rhs=codes.bitcast(FP8X4), rhs_scale=scales, start=True, stop=True,
            )

        def scalar_look_up(result, window, lst, cols):
            nc.scalar.activation(result, window[:].indirect(entries(lst, cols)), COPY)

        val_window = [held([P, S], F32, "val_window%d" % t) for t in range(PACK)]
        h_window = [held([P, S], F32, "h_window%d" % t) for t in range(PACK)]

        def val_product(t, cols, number, copy):
            val_bank = bank(number, [P, cols.stop - cols.start])
            nc.tensor.matmul_mx(
                val_bank[:], lhsT=w3_codes[:, P * t : P * (t + 1)].bitcast(FP8X4), lhsT_scale=w3_scales[:, P * t : P * (t + 1)],
                rhs=xq_words[:, cols].bitcast(FP8X4), rhs_scale=xq_scales[:, cols], start=True, stop=True,
            )
            copy(val_window[t][:, cols], val_bank[:])
            return val_bank

        val_product(1, halves[0], 1, nc.scalar.copy)
        val0_banks = [val_product(0, halves[0], 0, nc.vector.tensor_copy)]
        val_product(1, halves[1], 4, nc.scalar.copy)
        val0_banks.append(val_product(0, halves[1], 3, nc.vector.tensor_copy))
        val_product(2, halves[0], 2, nc.scalar.copy)
        val_product(2, halves[1], 5, nc.vector.tensor_copy)

        taps0 = held([P, S], F32, "taps0")
        taps1 = held([P, S], F32, "taps1")
        sum_area = held([P, 18 * CHUNK], F32, "sum_slots")

        def slots(first):
            return sum_area[:, first * CHUNK : (first + 3 * PACK) * CHUNK].rearrange("p (t n) -> p t n", t=PACK)[:, :, :HALF]

        taps2 = sum_area[:, 9 * CHUNK : 13 * CHUNK]
        taps3 = held([P, S], F32, "taps3")
        for half in halves:
            nc.vector.tensor_copy(taps0[:, half], val_window[0][:].indirect(entries(t1_sb, half)))
        for half in halves:
            scalar_look_up(taps1[:, half], val_window[1], t1_sb, half)
        val3_bank = val_product(3, whole, 6, nc.vector.tensor_copy)
        for t, taps in ((2, taps2), (3, taps3)):
            for half in halves:
                scalar_look_up(taps[:, half], val_window[t], t1_sb, half)

        e_banks = []
        for t, number in enumerate((7, 1, 2, 4)):
            e_banks.append(bank(number, [P, S]))
            fp4_product(e_banks[t][:], w2_q, t, xq_words[:], xq_scales[:])

        def first_gate(t, sums, cols):
            nc.vector.tensor_tensor(h_window[t][:, cols], e_banks[t][:, cols], sums, MULT)

        sums1 = held([P, S], F32, "sums1")
        nc.gpsimd.tensor_tensor(sums1[:], val_window[1][:], taps1[:], ADD)
        nc.gpsimd.tensor_tensor(taps2, val_window[2][:], taps2, ADD)
        for u, half in enumerate(halves):
            nc.vector.tensor_tensor(taps0[:, half], val0_banks[u][:], taps0[:, half], ADD)
        for half in halves:
            first_gate(0, taps0[:, half], half)
        for half in halves:
            first_gate(1, sums1[:, half], half)
        for half in halves:
            nc.vector.tensor_tensor(sums1[:, half], val3_bank[:, half], taps3[:, half], ADD)
        first_gate(2, taps2, whole)
        first_gate(3, sums1[:], whole)

        out_rows = out_0.rearrange("(p t) n -> p t n", t=PACK)
        out_words = out_1[0].rearrange("p c r -> p (c r)").bitcast(I32)
        first_sums = slots(6)
        later_sums = slots(0)
        staged = sum_area[:, :HALF]
        staged1 = held([P, HALF], F32, "staged1")
        for t, taps in enumerate((first_sums[:, 0, :], staged1[:], first_sums[:, 2, :])):
            scalar_look_up(taps, h_window[t], t2_sb, halves[0])
        scalar_look_up(staged[:, chunks[1]], h_window[3], t2_sb, chunks[1])
        nc.gpsimd.tensor_tensor(first_sums[:, 0, :], first_sums[:, 0, :], h_window[0][:, halves[0]], ADD)
        nc.vector.tensor_tensor(first_sums[:, 1, :], staged1[:], h_window[1][:, halves[0]], ADD)
        nc.vector.tensor_copy(staged[:, chunks[0]], h_window[3][:].indirect(entries(t2_sb, chunks[0])))
        nc.vector.tensor_tensor(first_sums[:, 2, :], first_sums[:, 2, :], h_window[2][:, halves[0]], ADD)
        for c in range(2):
            nc.vector.tensor_tensor(first_sums[:, 3, chunks[c]], staged[:, chunks[c]], h_window[3][:, chunks[c]], ADD)

        later_taps = held([P, PACK, HALF], F32, "sums1")
        for t in range(2):
            scalar_look_up(later_taps[:, t, :], h_window[t], t2_sb, halves[1])
        for c in (2, 3):
            for t in (2, 3):
                scalar_look_up(later_taps[:, t, chunks[c - 2]], h_window[t], t2_sb, chunks[c])

        z_tiles = [sum_area[:, first * CHUNK : (first + 2) * CHUNK].bitcast(BF16) for first in (2, 4)]
        late_z = held([P, PACK * HALF], BF16, "late_z")
        z_tiles = z_tiles + [late_z[:, : PACK * CHUNK], late_z[:, PACK * CHUNK :]]
        z_codes = held([P, S], U32, "z_codes")
        z_scales = held([P, S], U8, "z_scales")
        out_f32 = [held([P, PACK, CHUNK], F32, "out_f32%d" % c) for c in range(CHUNKS)]

        def second_gate(c):
            y_bank = bank((2, 4)[c % 2], [P, PACK, CHUNK])
            for t in range(PACK):
                fp4_product(y_bank[:, t, :], w1_q, t, xq_words[:, chunks[c]], xq_scales[:, chunks[c]])
            sums = (first_sums, later_sums)[c // 2][:, :, chunks[c % 2]]
            nc.vector.tensor_tensor(
                z_tiles[c].rearrange("p (n i t) -> p n t i", i=2, t=PACK),
                y_bank[:].rearrange("p t (n i) -> p n t i", i=2),
                sums.rearrange("p t (n i) -> p n t i", i=2),
                MULT,
            )

        def quantise_z(c):
            nc.vector.quantize_mx(z_codes[:, chunks[c]].bitcast(FP8X4), z_scales[:, chunks[c]], z_tiles[c])

        def last_layer(c, number):
            out_bank = bank(number, [P, PACK, CHUNK])
            for t in range(PACK):
                fp4_product(out_bank[:, t, :], w4_q, t, z_codes[:, chunks[c]], z_scales[:, chunks[c]])
            nc.scalar.copy(out_f32[c][:], out_bank[:])
            nc.sync.dma_start(out_rows[:, :, chunks[c]], out_f32[c][:])
            return out_bank

        def round_bank(rounded, out_bank):
            nc.scalar.copy(rounded.rearrange("p (n t) -> p n t", t=PACK), out_bank.rearrange("p t n -> p n t"))

        def round_stored(rounded, stored):
            nc.vector.tensor_copy(rounded.rearrange("p (n i t) -> p n t i", i=4, t=PACK), stored.rearrange("p t (n i) -> p n t i", i=4))

        def later_add(engine, t, cols, taps):
            engine.tensor_tensor(later_sums[:, t, cols.start - HALF : cols.stop - HALF], taps, h_window[t][:, cols], ADD)

        second_gate(0)
        second_gate(1)
        later_add(nc.gpsimd, 0, halves[1], later_taps[:, 0, :])
        quantise_z(0)
        pieces = [slice(first, first + PIECE) for first in range(0, CHUNK, PIECE)]
        first_bank = last_layer(0, 7)
        for t in (2, 1, 3):
            later_add(nc.vector, t, chunks[2], later_taps[:, t, chunks[0]])
        quantise_z(1)
        last_layer(1, 1)
        second_gate(2)
        later_add(nc.gpsimd, 1, chunks[3], later_taps[:, 1, chunks[1]])
        for t in (2, 3):
            later_add(nc.vector, t, chunks[3], later_taps[:, t, chunks[1]])
        quantise_z(2)
        round_bank(late_z[:, PACK * PIECE : PACK * CHUNK], first_bank[:, :, pieces[1]])
        third_bank = last_layer(2, 5)
        second_gate(3)
        round_stored(late_z[:, : PACK * PIECE], out_f32[0][:, :, pieces[0]])
        out_scales = held([P, S], U8, "sum_slots")
        out_codes = held([P, S], U32, "out_codes")

        def quantise_out(first, rounded):
            cols = slice(first, first + rounded.shape[1] // PACK)
            nc.vector.quantize_mx(out_codes[:, cols].bitcast(FP8X4), out_scales[:, cols], rounded)

        quantise_z(3)
        quantise_out(0, z_tiles[2])
        round_stored(z_tiles[3], out_f32[1][:])

        last = chunks[3]
        for pair, copy in enumerate((nc.scalar.copy, nc.vector.tensor_copy)):
            pair_bank = bank((0, 6)[pair], [P, 2, CHUNK])
            for t in range(2):
                fp4_product(pair_bank[:, t, :], w4_q, 2 * pair + t, z_codes[:, last], z_scales[:, last])
            for piece in pieces:
                copy(out_f32[3][:, 2 * pair : 2 * pair + 2, piece], pair_bank[:, :, piece])
        nc.sync.dma_start(out_rows[:, :, last], out_f32[3][:])
        quantise_out(CHUNK, z_tiles[3])
        late_bf = held([P, PACK * HALF], BF16, "z_scales")
        round_bank(late_bf[:, : PACK * CHUNK], third_bank[:])
        last_bf = [late_bf[:, PACK * (CHUNK + piece.start) : PACK * (CHUNK + piece.stop)] for piece in pieces]
        for piece, rounded in zip(pieces, last_bf):
            round_stored(rounded, out_f32[3][:, :, piece])
        for piece, rounded in zip(pieces, last_bf):
            quantise_out(last.start + piece.start, rounded)
        quantise_out(HALF, late_bf[:, : PACK * CHUNK])
        nc.sync.dma_start(out_words, out_codes[:].bitcast(I32))
        for q in range(4):
            nc.scalar.dma_start(out_2[0, 4 * q : 4 * q + 4, :].bitcast(I32), out_scales[32 * q : 32 * q + 4, :].bitcast(I32))
